import numpy as np, ml_dtypes
CORES = [48,51,52,55]
N = 4
BF = ml_dtypes.bfloat16
def gentries(a):
    return np.ascontiguousarray(a.reshape(8, 16, -1).transpose(0, 2, 1)).reshape(8, -1)
def gtable(e):
    e = np.asarray(e); return np.ascontiguousarray(e.reshape(8, -1, 16).transpose(0, 2, 1)).reshape(128, -1).astype(np.int32)
CN, Q0, S, H, RO, EPS, RHO = 2560, 768, 192, 64, 6, 40, 56
LN = S + H
def pick4(w, ix):
    return np.take_along_axis(w, ix[:, :, None, :], 3)
def noise(rng, m, shape):
    return np.rint((2 * rng.random(shape) - 1) * m).astype(np.int64)
def clip(v):
    return np.minimum(np.maximum(v, 0), 15)
def pos(rng, lo, hi, *shape):
    return (lo + (hi - lo) * rng.random(shape, dtype=np.float32)).astype(BF)
def split(rng, T, m, c):
    r = rng.random(T.shape + (m * c,)); lim = np.take_along_axis(np.sort(r, axis=-1), (T - 1)[..., None], -1)
    return np.moveaxis(np.add.reduce((r <= lim).astype(np.int64).reshape(T.shape + (m, c)), axis=-1), -1, -2)
def parts(rng):
    K = rng.integers(0, 16, (N, 8, 16, Q0)); nb = rng.integers(0, Q0, (N, 8, 16, Q0))
    me = (np.arange(16)[:, None] == rng.integers(0, 16, (N, 8, 1, Q0))) & (rng.random((N, 8, 1, Q0)) < 0.75)
    nb = np.where(me, np.arange(Q0), nb)
    pm = np.argsort(rng.random((N, 8, Q0)), axis=-1); inv = np.argsort(pm, axis=-1)
    home = np.ascontiguousarray(np.tile(pm, (1, 1, CN // Q0 + 1))[..., :CN])
    C = clip(pick4(K, home) + noise(rng, rng.integers(0, 4, (N, 8, 1, CN)), (N, 8, 16, CN)))
    near = inv[:, :, None, :] + Q0 * rng.integers(0, CN // Q0, (N, 8, 16, Q0))
    dl = np.where(rng.random((N, 8, 16, Q0)) < 0.45, near, rng.integers(0, CN, (N, 8, 16, Q0)))
    st = np.take_along_axis(np.argsort(rng.random((N, 8, Q0)), axis=-1), (Q0 * rng.random((N, 8, LN)) ** 2).astype(np.int64), 2)
    j = st[..., :S]; xs = np.zeros((N, 8, 16, RO, S), np.int64); x = None
    for t in range(RO):
        go = np.take_along_axis(pick4(nb, j), rng.integers(0, 16, (N, 8, 1, S)), 2)[:, :, 0]
        stay = (rng.random((N, 8, S)) < 0.5) & (t > 0); j = np.where(stay, j, go)
        z = clip(pick4(K, j) + noise(rng, rng.choice(np.array([1, 3, 5, 8, 12]), (N, 8, 1, S)), (N, 8, 16, S)))
        x = z if x is None else np.where(stay[:, :, None, :], clip(x + noise(rng, 1, x.shape)), z)
        xs[:, :, :, t] = x
    return {"kq": K, "nb": nb, "dl": dl, "cc": C, "aa": pos(rng, 16, 128, N, 8, 16, CN), "xs": xs, "ys": pos(rng, 64, 1024, N, 8, 16, RO, S), "st": st}
def pack(p):
    d = {}
    for k in ("kq", "nb", "dl", "cc", "aa", "xs", "ys"):
        d[k] = np.ascontiguousarray(p[k].reshape(N, 128, -1)).astype(np.int32 if k in ("nb", "dl") else BF)
    d["st"] = np.stack([gtable(a) for a in p["st"]]); return d
def setup_inputs(rng):
    return pack(parts(rng))
def relay(rng, p, pat, g):
    m = H // 3; n = H - 2 * m; X = p["xs"][:, g]
    for a in range(N):
        c = np.zeros((RO, S), np.int64); c[0, :m] = 1; c[1:, :m] = 2; c[:2, m:H] = 4 + a; c[2:, m:H] = 4 + (a - 1) % N
        X[a] = pat[:, c] + rng.integers(-1, 2, (16, RO, S)); X[a, :, 2, :m] = rng.integers(14, 16, (16, m))
    for a in range(N):
        st = rng.permutation(Q0)[:LN]; own, gst = st[:S], st[S:]; p["st"][a, g] = st
        nb = p["nb"][a, g]; nb[:] = np.arange(Q0); nb[1::2][:, own[:H]] = gst
        o = rng.permutation(CN); h = CN // 4; be, b2, b1, b0 = o[:n], o[n:h], o[h:2 * h], o[2 * h:]
        c = p["cc"][a, g]; c[:, b0] = 2 + rng.integers(-1, 2, (16, b0.size)); c[:, b1] = rng.integers(14, 16, (16, b1.size))
        c[:, b2] = pat[:, 2:3] + rng.integers(-1, 2, (16, b2.size))
        x = X[(a - 1) % N, :, 0, 2 * m:H]; z = split(rng, np.full(n, EPS), 16, 4); c[:, be] = np.where(x > 7, x - z, x + z)
        w = np.concatenate([rng.choice(b1, (8, H)), rng.choice(b2, (2, H)), rng.choice(b0, (6, H))]); w[15, 2 * m:] = be
        dl = p["dl"][a, g]; dl[:, own] = rng.choice(b0, (16, S)); dl[:, gst] = rng.permuted(w, axis=0)
        k = p["kq"][a, g]; k[:, own[:m]] = 2; k[:, gst[:m]] = 15
        k[:, own[m:H]] = pat[:, 4 + a][:, None]; k[:, gst[m:]] = pat[:, 4 + (a - 1) % N][:, None]
def far(rng, p, g):
    v = np.exp(-0.015625 * np.arange(EPS + 1, EPS + 9)); far_d = EPS + 1 + int(np.argmax(np.abs(v.astype(BF).astype(np.float64) - v)))
    u = rng.integers(0, 16, (N, 16, 4)); b = np.arange(H) % 4; n = CN // 8
    for a in range(N):
        me, up = u[a], u[(a - 1) % N]
        st = rng.permutation(Q0)[:LN]; own, gst = st[:H], st[S:]; p["st"][a, g] = st
        nb = p["nb"][a, g]; nb[:] = np.arange(Q0); nb[1::2][:, own] = gst
        k = p["kq"][a, g]; k[:, own] = me[:, b]; k[:, gst] = up[:, b]
        X = p["xs"][a, g]; X[:, :2, :H] = me[:, b][:, None, :]; X[:, 2:, :H] = up[:, b][:, None, :]
        Y = p["ys"][a, g]; Y[:, 0, :H] = pos(rng, 1800, 2048, 16, H).astype(np.float32); Y[:, 1:, :H] = pos(rng, 128, 1024, 16, RO - 1, H).astype(np.float32)
        o = rng.permutation(CN)
        for i in range(4):
            c1, c2 = o[2 * i * n:(2 * i + 1) * n], o[(2 * i + 1) * n:(2 * i + 2) * n]
            for x, ix, T, q, lo, hi in ((me[:, i:i + 1], c1, np.full(n, far_d), own[i::4], 124, 128), (up[:, i:i + 1], c2, rng.integers(EPS + 1, 61, n), gst[i::4], 16, 32)):
                z = split(rng, T, 16, 4); p["cc"][a, g][:, ix] = np.where(x > 7, x - z, x + z)
                p["aa"][a, g][:, ix] = pos(rng, lo, hi, 16, n).astype(np.float32)
                p["dl"][a, g][:, q] = rng.choice(ix, (16, q.size))
def setup_inputs_corners(rng):
    p = parts(rng); off = int(rng.integers(0, 8)); vals = (0, 1, 2, 3, H - 1, H, H + 1, S)
    pat = 2 + 10 * np.array([[bin(f & j).count("1") & 1 for j in range(16)] for f in range(16)])
    for a in range(N):
        for g in range(8):
            st = rng.permutation(Q0)[:LN]; own, gst = st[:S], st[S:]; p["st"][a, g] = st
            nb = p["nb"][a, g]; nb[:] = np.arange(Q0); nb[1::2][:, own[:H]] = gst
            o = rng.permutation(CN); h = CN // 2; b0, b1, b2 = o[:h], o[h:h + h // 2], o[h + h // 2:]
            c = p["cc"][a, g]; c[:, b0] = 2 + rng.integers(-1, 2, (16, b0.size)); c[:, b1] = rng.integers(14, 16, (16, b1.size))
            c[:, b2] = pat[:, 1 + np.arange(b2.size) % (RO - 1)] + rng.integers(-1, 2, (16, b2.size))
            dl = p["dl"][a, g]; dl[:, own] = rng.choice(b0, (16, S))
            w = [rng.choice(b1, (8, H))] + [rng.choice(b2[t::RO - 1], (1, H)) for t in range(RO - 1)] + [rng.choice(b0, (9 - RO, H))]
            dl[:, gst] = rng.permuted(np.concatenate(w), axis=0)
            k = p["kq"][a, g]; k[:, own[:H]] = 2; k[:, gst] = 15
            k[:, own[H:]] = pat[:, rng.integers(0, RO, S - H)] + rng.integers(-1, 2, (16, S - H))
            for t in range(RO):
                new = rng.permutation(S) < vals[(a + g + 3 * t + off) % 8]
                x = pat[:, np.where(new & (t < RO - 1), t + 1, 0)] + rng.integers(-1, 2, (16, S))
                if t == RO - 1: x[:, :H] = rng.integers(14, 16, (16, H))
                p["xs"][a, g, :, t] = x
    relay(rng, p, pat, int(rng.integers(0, 8)))
    return pack(p)
def setup_inputs_crowd(rng):
    p = parts(rng)
    for a in range(N):
        for g in range(8):
            o = rng.permutation(Q0); st, nb = p["st"][a, g], p["nb"][a, g]; kind = g // 2
            if (a + g) % 2 == 1:
                st[:] = o[:LN]; nb[:] = np.arange(Q0); p["xs"][a, g] = rng.integers(0, 16, (16, RO, S)); continue
            z = o[:4] if kind == 2 else o[:1]
            nb[:, z] = rng.choice(z, (16, z.size)); st[:] = rng.choice(z, LN)
            if kind == 1 or kind == 3:
                st[LN - 1 if kind == 1 else int(rng.integers(1, S))] = o[5]; nb[:, o[5]] = o[5]
            if kind != 2: p["xs"][a, g][:, :2, 0] = p["cc"][a, g][:, p["dl"][a, g, 0, z[0]]][:, None]
    return pack(p)
def setup_inputs_ends(rng):
    p = parts(rng); sw = (np.arange(N)[:, None] + np.arange(8)) % 2
    hs = 15 * (np.argsort(rng.random((N, 8, 16, 3)), axis=2) < 8)
    pr = np.zeros((N, 8, 16, 8), np.int64); pr[..., 1] = 15; pr[..., 2::2] = hs; pr[..., 3::2] = 15 - hs
    ki = rng.integers(0, 8, (N, 8, Q0)); ci = rng.integers(0, 8, (N, 8, CN)); xi = rng.integers(0, 8, (N, 8, RO, S))
    ci[..., 0] = sw; ci[..., CN - 1] = 1 - sw; ki[..., 0] = 1 - sw; ki[..., Q0 - 1] = sw
    ci[:, 7, 0] = 0; ci[:, 7, CN - 1] = 0; ki[:, 7, 0] = 0; ki[:, 7, Q0 - 1] = 0
    xi[..., 0] = rng.integers(0, 2, (N, 8, RO)); xi[..., S - 1] = rng.integers(0, 2, (N, 8, RO)); xi[:, 7, 0, 0] = 1; xi[:, 7, 0, S - 1] = 1
    p["kq"] = pick4(pr, ki); p["cc"] = pick4(pr, ci); p["xs"] = pick4(pr, xi.reshape(N, 8, RO * S))
    for k, top in (("nb", Q0 - 1), ("dl", CN - 1)):
        v = rng.integers(0, top + 1, (N, 8, 16, Q0)); v[:, :, :6] = 0; v[:, :, 6:11] = top
        v[:, :, :11] = np.where(rng.random((N, 8, 1, Q0)) < 0.5, top - v[:, :, :11], v[:, :, :11])
        v = rng.permuted(v, axis=2)
        for a in range(N):
            for c in (0, Q0 - 1): v[a, 7, :, c] = rng.permutation(np.repeat(np.array([0, top]), 8))
        p[k] = v
    st = np.where(rng.random((N, 8, LN)) < 0.72, (Q0 - 1) * rng.integers(0, 2, (N, 8, LN)), rng.integers(0, Q0, (N, 8, LN)))
    st[..., 0] = 0; st[..., S - 1] = Q0 - 1; st[..., LN - 1] = Q0 - 1; st[:, 7, 0] = Q0 - 1; p["st"] = st
    aa = pos(rng, 64, 128, N, 8, 16, CN).astype(np.float32)
    aa[:, 7, :, CN - 1] = 0.5 * aa[:, 7, :, 0]; p["aa"] = aa
    return pack(p)
def setup_inputs_spread(rng):
    p = parts(rng)
    for k, lo, hi in (("aa", 32, 64), ("ys", 128, 1024)):
        s = (N, 8, 1) + p[k].shape[3:]
        p[k] = pos(rng, lo, hi, *p[k].shape).astype(np.float32) * np.exp2(rng.integers(-1, 2, s))
    far(rng, p, int(rng.integers(0, 8)))
    return pack(p)
def setup_inputs_ties(rng):
    p = parts(rng)
    st = np.argsort(rng.random((N, 4, Q0)), axis=-1)[..., :LN]; p["st"][:, ::2] = st; p["nb"][:, ::2] = np.arange(Q0); p["cc"][:, ::2] = 7
    for t in range(RO):
        h = 8 * ((t // 2) % 2); x = np.full((N, 4, 16, S), 7)
        x[:, :, h:h + 8] += (1 - 2 * (t % 2)) * split(rng, EPS + rng.integers(0, 2, (N, 4, S)), 8, 7)
        p["xs"][:, ::2, :, t] = x
        if t == 0:
            z = split(rng, RHO + rng.integers(0, 2, (N, 4, S)), 16, 8); K = np.where(x > 7, x - z, x + z)
            for a in range(N):
                for g in range(4): p["kq"][a, 2 * g][:, st[a, g, :S]] = K[a, g]
    p["dl"][:, 2, 8:] = p["dl"][:, 2, :8]; p["dl"][:, 6, 8:] = p["dl"][:, 6, :8]
    pr = rng.integers(0, 16, (N, 4, 16, 6)); p["kq"][:, 1::2] = pick4(pr, rng.integers(0, 6, (N, 4, Q0)))
    p["cc"][:, 1::2] = np.where(rng.random((N, 4, 1, CN)) < 0.6, pick4(pr, rng.integers(0, 6, (N, 4, CN))), p["cc"][:, 1::2])
    for t in range(RO):
        m = rng.choice(np.array([0, 0, 1, 4, 9]), (N, 4, 1, S))
        p["xs"][:, 1::2, :, t] = clip(pick4(pr, rng.integers(0, 6, (N, 4, S))) + noise(rng, m, (N, 4, 16, S)))
    return pack(p)
def check_ranges(d):
    bad = []
    for k, hi in (("kq", 15), ("cc", 15), ("xs", 15), ("nb", Q0 - 1), ("dl", CN - 1), ("st", Q0 - 1)):
        v = np.asarray(d[k]).astype(np.float64)
        if not (np.min(v) >= 0 and np.max(v) <= hi): bad.append("range of " + k)
        elif np.any(v != np.floor(v)): bad.append("whole numbers of " + k)
    for k, lo, hi in (("aa", 16, 128), ("ys", 64, 2048)):
        v = np.asarray(d[k]).astype(np.float64)
        if not np.all((v >= lo) & (v <= hi)): bad.append("range of " + k)
    return bad
def pick(w, ix):
    return np.take_along_axis(w, ix[:, None, :], 2)
def entry(v, k):
    return np.take_along_axis(v, k[:, None, :], 1)[:, 0]
def dist(w, ix, x):
    v = pick(w, ix.reshape(8, -1)).reshape(8, 16, 16, -1)
    return np.add.reduce(np.abs(v - x[:, :, None, :]), axis=1)
def reference(kq, nb, dl, cc, aa, xs, ys, st):
    QT, CT = Q0 + LN * (RO - 1), CN + LN * (RO - 1)
    kk = np.zeros((N, 8, 16, QT), np.int32); nn = np.zeros((N, 8, 16, QT), np.int64); ll = np.zeros((N, 8, 16, QT), np.int64)
    ce = np.zeros((N, 8, 16, CT), np.int32); ac = np.zeros((N, 8, 16, CT), np.float64)
    kk[..., :Q0] = kq.astype(np.float32).astype(np.int32).reshape(N, 8, 16, Q0); nn[..., :Q0] = nb.reshape(N, 8, 16, Q0); ll[..., :Q0] = dl.reshape(N, 8, 16, Q0)
    ce[..., :CN] = cc.astype(np.float32).astype(np.int32).reshape(N, 8, 16, CN); ac[..., :CN] = aa.astype(np.float64).reshape(N, 8, 16, CN)
    x0 = xs.astype(np.float32).astype(np.int32).reshape(N, 8, 16, RO, S); y0 = ys.astype(np.float64).reshape(N, 8, 16, RO, S)
    cl = np.stack([gentries(a) for a in st]).astype(np.int64)
    gx = np.zeros((N, 8, 16, H), np.int32); ga = np.zeros((N, 8, 16, H), np.float64); gn = np.zeros((N, 8), np.int64)
    out = np.zeros((N, 8, 16, RO, S), np.float64); lane = np.arange(LN); rows = np.arange(16)[:, None]; before = np.tri(LN, LN, -1, dtype=bool)
    for t in range(RO):
        hx, ha, hn = np.zeros_like(gx), np.zeros_like(ga), np.zeros_like(gn)
        for a in range(N):
            x = np.concatenate([x0[a, :, :, t], gx[a]], axis=2); live = (lane < S) | (lane - S < gn[a][:, None])
            cand = pick(nn[a], cl[a]); d = dist(kk[a], cand, x)
            q = entry(cand, np.argmin(d, axis=1)); dq = np.min(d, axis=1)
            li = pick(ll[a], q); D = dist(ce[a], li, x)
            w = np.exp(-0.015625 * D[:, None, :, :S])
            P = np.add.reduce(w * pick(ac[a], li[:, :, :S].reshape(8, -1)).reshape(8, 16, 16, S), axis=2)
            out[a, :, :, t] = P
            if t == RO - 1: continue
            win = live & ~np.any((q[:, :, None] == q[:, None, :]) & live[:, None, :] & before, axis=2)
            ks, kl = np.argmin(D, axis=1), np.argmax(D, axis=1)
            upd = np.min(D, axis=1) <= EPS; fork = ~upd & (dq > RHO)
            cs = entry(li, ks); lo, ql = CN + LN * t, Q0 + LN * t
            cn = np.where(upd[:, None, :], pick(ce[a], cs), x)
            an = np.concatenate([np.where(upd[:, None, :S], pick(ac[a], cs[:, :S]), 0.0) + 0.25 * (y0[a, :, :, t] - P), ga[a]], axis=2)
            nl = np.where(rows == np.where(upd, ks, kl)[:, None, :], lo + lane, li)
            nq = np.where(rows == t, q[:, None, :], pick(nn[a], q))
            ce[a][:, :, lo:lo + LN] = cn; ac[a][:, :, lo:lo + LN] = an
            b = (a + 1 + t % (N - 1)) % N
            for g in range(8):
                i = np.nonzero(win[g] & ~fork[g])[0]; ll[a, g][:, q[g, i]] = nl[g][:, i]
                i = np.nonzero(win[g] & fork[g])[0]
                ll[a, g][:, ql + i] = nl[g][:, i]; nn[a, g][:, ql + i] = nq[g][:, i]; kk[a, g][:, ql + i] = x[g][:, i]; nn[a, g][8 + t, q[g, i]] = ql + i
                i = np.nonzero(win[g, :S] & ~upd[g, :S])[0][:H]
                hx[b, g][:, :i.size] = x[g][:, i]; ha[b, g][:, :i.size] = an[g][:, i]; hn[b, g] = i.size
            cl[a] = np.where(live, q, cl[a])
        gx, ga, gn = hx, ha, hn
    return {"yp": out.reshape(N, 128, RO * S).astype(np.float32)}

def check_inputs(d):
    bad = list(check_ranges(d))
    if not bad:
        for name, y in reference(**d).items():
            for q in range(N):
                v = np.abs(np.asarray(y[q], np.float64)); s = np.sqrt(np.mean(v * v))
                if v.max() > 5 * s or s < 2.0 ** 7: bad.append('%s of rank %d is uneven or too small' % (name, q))
    return bad

@@ -1,0 +1,668 @@
+from concourse.bass import DstId, RemoteDMATransfer
+from concourse.mybir import dt, AluOpType, AxisListType, ActivationFunctionType
+
+ALU = AluOpType
+ACT = ActivationFunctionType
+CN, Q0, S, H, RO, LN = 2560, 768, 192, 64, 6, 256
+XW = 272
+IDW = 4512
+BIG = 1.0e6
+MODE = {}
+for _t in range(RO):
+    MODE[(1, _t)] = ['VSSVVSSS', 'VVSSVSSS', 'VVSVVVSS', 'VVSSVSSS', 'VVSVVVSS', 'VVSSVSSS'][_t]
+    MODE[(2, _t)] = ['VVSSVVSS', 'VVSSVVSS', 'VVSSVVSS', 'VVSSVVSS', 'SVSSVVSS', 'VVSSVVSS'][_t]
+SUM = ['VPV', 'VPV', 'VPV', 'VPP', 'VPP', 'VPV']
+BIAS = {'Vdmax': 4400, 'PSB0': 600, 'GI1': 1000, 'SX': 1000, 'Vc1': -400, 'GB1': 1000, 'SliC': 1000, 'VZ': 400, 'Ssj': -1000, 'GQP': -1000,
+        'GPt': 4000, 'YY': -4000, 'Vij': 2400, 'VI16': -2000, 'Vb0': 4000, 'YKt': -2000, 'Vpr': -4000, 'Vf2': 6800, 'Vxr0': -1000,
+        'VliU0': -1000, 'VtnU': -400, 'Vcum': 4000, 'Shh': 5600, 'Vone': -1000, 'Vmn': -1000, 'Vpm': 2000, 'Vk1U': 400, 'Yqpm': 1000,
+        'Vrs': 4000, 'Swin': 400, 'Vn1': 1400, 'SKt': 1000, 'VtdU': 4000, 'VwR': -1000, 'Vsel2': 2000, 'VIf': -1000, 'GnR': -1000,
+        'Vjb': -400, 'Shi': 3000, 'VSX': -2000, 'Vqpm': -1000, 'Yyp': -2000, 'SqF': -400, 'Vd1': 1000, 'Sfar': 2000, 'VIp': -1000,
+        'VCt': -1000, 'YId': 4000, 'YCt': -400, 'Sf1': 400, 'VI1': 400, 'GAt': 12000, 'Vwf': -400, 'SliF': 400, 'Gxr1': -2000, 'Ysti': 2000}
+for _t in range(RO):
+    MODE[(1, _t)] = ['SVSVVSSS', 'VVSSVSSS', 'VVSVVVSS', 'VVSSVSSS', 'VVVSVVSS', 'VVSSVSSS'][_t]
+    MODE[(2, _t)] = ['VVSSVVSS', 'VVSSVVSS', 'VVSSVVSS', 'VVSSVVSS', 'SSVSVVSS', 'SVVSVVSS'][_t]
+SUM = ['VPV', 'VPV', 'VPV', 'VPP', 'VPP', 'PVV']
+BIAS = {'Vdmax': 4400, 'PSB0': -1000, 'GI1': 1000, 'SX': 1000, 'Vc1': -800, 'SliC': 1000, 'VZ': 2400, 'Ssj': 1800, 'GQP': -4000, 'GPt': 7000, 'YY': -10000, 'Vij': 2400, 'VI16': -2000, 'Vb0': 4000, 'YKt': -400, 'Vpr': -4000, 'Vf2': 800, 'Vxr0': -1000, 'VliU0': 1000, 'VtnU': 1600, 'Vcum': 4000, 'Shh': 5600, 'Vmn': -1000, 'Vpm': 2000, 'Vk1U': 2400, 'Yqpm': -1000, 'Vrs': 3600, 'Swin': 3400, 'Vn1': 1400, 'SKt': -11400, 'VtdU': 5600, 'VwR': -2000, 'Vsel2': 6000, 'VIf': -1400, 'GnR': 1000, 'Vjb': 1600, 'Shi': 9000, 'VSX': -2400, 'Vqpm': -600, 'Yyp': -2000, 'SqF': -800, 'Vd1': 1000, 'VIp': 1000, 'VCt': -1000, 'YId': 600, 'YCt': -400, 'Sf1': 400, 'VI1': -1000, 'GAt': 12000, 'Vwf': -1400, 'SliF': 400, 'Gxr1': -5000, 'Ysti': 6000, 'VB16': 1000, 'GNE': -4000, 'VQP': 400, 'VId': -400, 'VT01': -3600, 'Gii': 2000, 'YX': -9000, 'PM': 400, 'Gxr0': 600, 'VliU1': -1000, 'Swr': 1600, 'Vsel': -400, 'Vd2': 2000, 'Ynbi': -4000, 'Vclg': 400, 'Vwin': -3000, 'Vso': -400, 'Vsm': 4000, 'Vf3': 400, 'Grem': 1600, 'SPt': -3000, 'VfR': 3600, 'VsrU': 400, 'YNB': -1000, 'VNB': -4000, 'Gqn': 1000, 'Vseed': 4000, 'SqL': -1000, 'Vdmin': -800, 'VX': 1000, 'Ydli': 1400, 'SCt': -3600, 'Sqp': -400, 'PD0': 400, 'Vn2': -1000, 'Vthr': 2000, 'Sun': -2000, 'Vsx': 1400, 'VIy': -1000, 'Suu': -1000, 'Vtm': 2000}
+NENG = 8
+
+SCRATCH = {
+    "Kt": ("sbuf", [128, 2048], "bfloat16"), "Ct": ("sbuf", [128, 4096], "bfloat16"), "At": ("sbuf", [128, 4096], "float32"),
+    "NB": ("sbuf", [128, 2304], "float32"), "DL": ("sbuf", [128, 2048], "float32"),
+    "nbi": ("sbuf", [128, 768], "int32"), "dli": ("sbuf", [128, 768], "int32"), "sti": ("sbuf", [128, 16], "int32"),
+    "X": ("sbuf", [128, RO * XW], "bfloat16"), "Y": ("sbuf", [128, RO * S], "bfloat16"), "Pt": ("sbuf", [128, RO * S], "float32"),
+    "Id": ("sbuf", [128, IDW], "bfloat16"), "Z": ("sbuf", [128, 144], "bfloat16"), "B1": ("sbuf", [128, 128], "bfloat16"),
+    "B16": ("sbuf", [128, 128], "bfloat16"), "I1": ("sbuf", [128, 128], "bfloat16"), "Iy": ("sbuf", [128, 128], "bfloat16"),
+    "Ip": ("sbuf", [128, 128], "float32"), "If": ("sbuf", [128, 128], "float32"), "NE": ("sbuf", [128, 1024], "bfloat16"), "xT": ("sbuf", [128, 4 * 128], "bfloat16"),
+    "xr0": ("sbuf", [128, 3072], "bfloat16"), "xr1": ("sbuf", [128, 3072], "bfloat16"),
+    "ab1": ("sbuf", [128, 16, 256], "bfloat16"), "ab2": ("sbuf", [128, 16, 256], "bfloat16"), "ag": ("sbuf", [128, 4096], "bfloat16"),
+    "vv": ("sbuf", [128, 3072], "bfloat16"),
+    "wr": ("sbuf", [128, 3072], "float32"), "pr": ("sbuf", [128, 3072], "float32"), "so": ("sbuf", [128, 3072], "float32"),
+    "Eb": ("sbuf", [128, 16, 256], "bfloat16"),
+    "caU": ("sbuf", [128, 256], "uint16"), "caF": ("sbuf", [128, 256], "float32"), "sel": ("sbuf", [128, 256], "float16"),
+    "liU0": ("sbuf", [128, 256], "uint16"), "liU1": ("sbuf", [128, 256], "uint16"),
+    "liF": ("sbuf", [128, 256], "float32"), "liC": ("sbuf", [128, 256], "float32"), "sel2": ("sbuf", [128, 256], "float16"),
+    "mn": ("sbuf", [128, 256], "float32"), "qR": ("sbuf", [128, 256], "float16"), "qF": ("sbuf", [128, 256], "float32"),
+    "qpm": ("sbuf", [128, 256], "float32"), "nR": ("sbuf", [128, 1280], "float32"), "wR": ("sbuf", [128, 256], "bfloat16"),
+    "fR": ("sbuf", [128, 192], "bfloat16"), "cum": ("sbuf", [128, 192], "bfloat16"), "sj": ("sbuf", [128, 192], "bfloat16"),
+    "one": ("sbuf", [128, 192], "bfloat16"), "hh": ("sbuf", [128, 192], "float32"),
+    "s1": ("sbuf", [128, 256], "float32"), "sm": ("sbuf", [128, 256], "float32"), "sx": ("sbuf", [128, 256], "float32"),
+    "dmin": ("sbuf", [128, 256], "float32"), "dmax": ("sbuf", [128, 256], "float32"), "rs": ("sbuf", [128, 1024], "bfloat16"),
+    "qn": ("sbuf", [128, 256], "float32"),
+    "thr": ("sbuf", [128, 256], "float32"), "seed": ("sbuf", [128, 256], "float32"), "half": ("sbuf", [128, 256], "float32"),
+    "ii": ("sbuf", [128, 16], "int32"), "ij": ("sbuf", [128, 16], "int32"), "I16": ("sbuf", [128, 16], "float32"),
+    "tm": ("sbuf", [128, 16], "float32"), "pw": ("sbuf", [128, 4], "float32"),
+    "pm": ("sbuf", [128, 4], "float32"), "LL": ("sbuf", [128, 80], "float32"), "QP": ("sbuf", [128, 80], "float32"),
+    "jb": ("sbuf", [128, 4], "float32"), "T01": ("sbuf", [128, 16], "bfloat16"),
+    "SX": ("sbuf", [128, 4 * 72], "bfloat16"), "SA": ("sbuf", [128, 4 * 64], "float32"),
+    "K0": ("psum", [128, 512], "float32"), "K1": ("psum", [128, 512], "float32"), "M": ("psum", [128, 512], "float32"),
+    "SB0": ("psum", [128, 512], "float32"), "SB1": ("psum", [128, 512], "float32"), "D0": ("psum", [128, 512], "float32"),
+    "D1": ("psum", [128, 512], "float32"), "PS": ("psum", [128, 512], "float32"),
+}
+for _n in ("k1U", "qU", "tnU", "cxU", "nvU", "srU"):
+    SCRATCH[_n] = ("sbuf", [128, 16], "uint16")
+for _n in ("qL", "clg", "c1", "c2", "win", "far", "wf", "qp", "a2", "b0", "un", "n1", "n2", "f1", "f2", "f3", "acc"):
+    SCRATCH[_n] = ("sbuf", [128, 16], "float32")
+for _n in ("uu", "lo", "hi", "d1", "d2"):
+    SCRATCH[_n] = ("sbuf", [128, 32], "float32")
+SCRATCH["tdU"] = ("sbuf", [128, 32], "uint16")
+NDMA = 56
+SEMAPHORES = ["eV", "eS", "eP", "eG"] + ["d%d" % i for i in range(NDMA)] + ["ax%d" % i for i in range(4)] + ["aa%d" % i for i in range(4)] + ["lx"]
+
+BYTES = {"float32": 4, "int32": 4, "bfloat16": 2, "float16": 2, "uint16": 2}
+CG, CSC, CYC, PEC, LAT, DMAL, AHEAD = 1.55, 3.8, 0.83, 0.42, 100.0, 2200.0, 60.0
+
+
+def sl(a, b, s=None):
+    return slice(a, b, s)
+
+
+def A(name, *idx, p=None):
+    return ("ap", name, p, idx)
+
+
+def C(name, a, b, s=None):
+    return A(name, sl(a, b, s))
+
+
+def IND(win, off):
+    return ("ind", win, off)
+
+
+def span(x):
+    name, idx = x[1], x[3]
+    if name not in SCRATCH:
+        return name, 0, 1 << 30, 0
+    where, shape, _ = SCRATCH[name]
+    lo, hi, n, stride = 0, 0, 1, 1
+    dims = shape[1:]
+    for d in range(len(dims) - 1, -1, -1):
+        i = idx[d] if d < len(idx) else slice(None)
+        r = range(dims[d])[i] if isinstance(i, slice) else range(i, i + 1)
+        lo += r[0] * stride
+        hi += r[-1] * stride
+        n *= len(r)
+        stride *= dims[d]
+    return name, lo, hi + 1, n
+
+
+def ap(T, x):
+    if not isinstance(x, tuple):
+        return x
+    if x[0] == "ind":
+        return ap(T, x[1]).indirect(ap(T, x[2]))
+    ps = x[2] if x[2] is not None else slice(None)
+    if not x[3]:
+        return T[x[1]][ps]
+    return T[x[1]][(ps,) + tuple(x[3])]
+
+
+def parts(x):
+    if not isinstance(x, tuple):
+        return []
+    return [x[1], x[2]] if x[0] == "ind" else [x]
+
+
+def wide(x):
+    return BYTES[SCRATCH[x[1]][2]]
+
+
+def build_ops():
+    ops = []
+
+    def add(eng, cost, fn, reads, writes, kind="c", arr=None):
+        rd = [y for x in reads for y in parts(x)]
+        wr = []
+        for x in writes:
+            if x[0] == "ind":
+                wr.append(x[1])
+                rd.append(x[2])
+            else:
+                wr.append(x)
+        ops.append({"eng": eng, "cost": cost, "fn": fn, "r": [span(x) for x in rd], "w": [span(x) for x in wr], "kind": kind, "arr": arr})
+
+    def count(out, ins):
+        if out[0] == "ind":
+            return span(ins[0])[3]
+        return span(out)[3]
+
+    def vcost(out, ins, f=None):
+        n = count(out, ins)
+        if out[0] == "ind":
+            return 50 + n * CSC * CYC
+        if ins and ins[0][0] == "ind":
+            return 50 + n * CG * CYC
+        if f is None:
+            f = 0.5 if all(wide(x) == 2 for x in [out] + ins) else 1.0
+        return 30 + max(64, n * f) * CYC
+
+    def cp(out, a, arr=None):
+        add("V", vcost(out, [a]), lambda g, T: g.vector.tensor_copy(ap(T, out), ap(T, a)), [a], [out], arr=arr)
+
+    def ms(out, v):
+        add("V", vcost(out, []), lambda g, T: g.vector.memset(ap(T, out), v), [], [out])
+
+    def ts(out, a, s1, op0, s2=None, op1=None):
+        if op1 is None:
+            fn = lambda g, T: g.vector.tensor_scalar(ap(T, out), ap(T, a), ap(T, s1), None, op0)
+        else:
+            fn = lambda g, T: g.vector.tensor_scalar(ap(T, out), ap(T, a), ap(T, s1), ap(T, s2), op0, op1)
+        add("V", vcost(out, [a]), fn, [a, s1, s2], [out])
+
+    def tt(out, a, b, op, arr=None):
+        f = 2.0 if a[0] == "ind" or (SCRATCH[a[1]][0] == "sbuf" and SCRATCH[b[1]][0] == "sbuf") else 1.0
+        add("V", vcost(out, [a, b], f), lambda g, T: g.vector.tensor_tensor(ap(T, out), ap(T, a), ap(T, b), op), [a, b], [out], arr=arr)
+
+    def scan(out, d0, d1, init, op0, op1):
+        add("V", vcost(out, [d0, d1]), lambda g, T: g.vector.tensor_tensor_scan(ap(T, out), ap(T, d0), ap(T, d1), init, op0, op1), [d0, d1], [out])
+
+    def red(out, a):
+        add("V", 90, lambda g, T: g.vector.tensor_reduce(ap(T, out), ap(T, a), AxisListType.X, ALU.add), [a], [out])
+
+    def act(out, a, func, bias=None, scale=None, acc=None, arr=None):
+        n = span(out)[3]
+        cost = 65 + n * CG * CYC if a[0] == "ind" else 30 + max(64, n) * CYC + (20 if acc else 0)
+
+        def fn(g, T):
+            kw = {}
+            if bias is not None:
+                kw["bias"] = ap(T, bias)
+            if scale is not None:
+                kw["scale"] = ap(T, scale)
+            if acc is not None:
+                kw["accum_out"] = ap(T, acc)
+            return g.scalar.activation(ap(T, out), ap(T, a), func, **kw)
+        add("S", cost, fn, [a, bias, scale], [out] + ([acc] if acc else []), arr=arr)
+
+    def mm(items):
+        cost = sum(max(64, span(o)[3]) * (4 if wide(r) == 4 else 1) for o, l, r, s0, s1 in items) * PEC + 60
+
+        def fn(g, T):
+            ins = None
+            for o, l, r, s0, s1 in items:
+                ins = g.tensor.matmul(ap(T, o), ap(T, l), ap(T, r), s0, s1)
+            return ins
+        add("P", cost, fn, [x for it in items for x in it[1:3]], [it[0] for it in items])
+
+    def dma(eng, out, a, cost=60.0):
+        if eng == "G":
+            fn = lambda g, T: g.dma_start(ap(T, out), ap(T, a))
+        elif eng == "S":
+            fn = lambda g, T: g.scalar.dma_start(ap(T, out), ap(T, a))
+        else:
+            fn = lambda g, T: g.sync.dma_start(ap(T, out), ap(T, a))
+        add(eng, cost, fn, [a], [out], kind="dma")
+
+    def iota(out, pat, base, cm):
+        n = span(out)[3]
+        if SCRATCH[out[1]][2] == "int32":
+            fn = lambda g, T: g.iota(ap(T, out), pat, base, cm)
+        else:
+            fn = lambda g, T: g.iota(ap(T, out), pat, base, cm, allow_small_or_imprecise_dtypes=True)
+        add("G", 130 + 2 * n * CYC, fn, [], [out])
+
+    def asel(out, a, pat, op, fill, base, cm):
+        add("G", 170 + 2 * span(out)[3] * CYC, lambda g, T: g.affine_select(ap(T, out), ap(T, a), pat, op, fill, base, cm), [a], [out])
+
+    def selr(r):
+        return C("Z", 15 - r, 143 - r)
+
+    def tolist(out, src, c0, c1):
+        mm([(out, selr(r), C(src, 16 * c0 + r, 16 * c1, 16), r == 0, r == 15) for r in range(16)])
+
+    dma("Y", A("sti"), A("st"))
+    dma("Y", A("nbi"), A("nb"))
+    dma("S", C("X", 0, S), C("xs", 0, S))
+    dma("S", C("Kt", 0, Q0), A("kq"))
+    dma("Y", A("dli"), A("dl"))
+    dma("Y", C("Ct", 256, 256 + CN), A("cc"))
+    dma("G", C("At", 256, 256 + CN), A("aa"), 300.0)
+    for t in range(1, RO):
+        dma("Y", C("X", XW * t, XW * t + S), C("xs", S * t, S * t + S))
+    dma("Y", A("Y"), A("ys"))
+    iota(A("ii"), [[-1, 16]], 16, 1)
+    ts(A("ij"), A("ii"), 15, ALU.bitwise_and)
+    ts(A("I16"), A("ij"), 0.0, ALU.is_equal)
+    ts(C("pm", 0, 1), C("ij", 0, 1), 1.0, ALU.mult)
+    cp(C("Id", 0, 16), A("I16"))
+    w = 16
+    while w < 512:
+        cp(C("Id", w, 2 * w), C("Id", 0, w))
+        w *= 2
+    while w < IDW:
+        n = min(512, IDW - w)
+        dma("Y", C("Id", w, w + n), C("Id", 0, n))
+        w += n
+    ms(A("B1"), 1.0)
+    asel(A("B1"), A("B1"), [[-16, 8], [0, 16]], ALU.is_ge, 0.0, 0, 1)
+    asel(A("B1"), A("B1"), [[16, 8], [0, 16]], ALU.is_ge, 0.0, 15, -1)
+    ms(A("Z"), 0.0)
+    ts(C("Z", 15, 143, 16), C("B1", 0, 128, 16), 16.0, ALU.mult)
+    ms(A("I1"), 1.0)
+    asel(A("I1"), A("I1"), [[-1, 128]], ALU.is_equal, 0.0, 0, 1)
+    ms(A("NE", p=sl(0, 64)), -1.0)
+    asel(A("NE", p=sl(0, 64)), A("NE", p=sl(0, 64)), [[-1, 64], [0, 16]], ALU.is_equal, 0.0, 0, 1)
+    ts(A("B16"), A("B1"), 65536.0, ALU.mult)
+    ts(A("Iy"), A("I1"), 0.25, ALU.mult)
+    ts(A("Ip"), A("I1"), -0.25, ALU.mult)
+    cp(A("If"), A("I1"))
+    ms(A("dmin"), -1.0)
+    ms(C("dmin", 0, 256, 16), BIG)
+    ms(A("dmax"), 1.0)
+    ms(C("dmax", 0, 256, 16), -BIG)
+    ms(A("rs"), 1.0)
+    ms(C("rs", 0, 1024, 16), 0.0)
+    ms(A("seed"), 0.0)
+    ms(C("seed", 0, 256, 16), 2.5 * 32768.0)
+    ms(A("half"), 0.5)
+    scan(A("thr"), A("half"), A("seed"), 0.0, ALU.mult, ALU.max)
+    tt(A("tm"), C("thr", 0, 16), A("I16"), ALU.mult)
+    red(C("pw", 1, 2), A("tm"))
+    ts(C("pw", 0, 1), C("pw", 1, 2), 0.4, ALU.mult, 8388608.0, ALU.add)
+    ts(C("pw", 2, 3), C("pw", 0, 1), -8388608.0, ALU.add)
+    iota(A("QP"), [[16, 80]], 0, 0)
+    ts(A("LL"), A("QP"), C("pm", 0, 1), ALU.add)
+    ts(A("QP"), A("LL"), float(Q0), ALU.add)
+    ts(A("jb"), C("LL", 0, 4), 0.5, ALU.add)
+    ms(A("qpm"), 0.0)
+    ms(A("T01"), 1.0)
+    ms(C("T01", 0, 1), 0.0)
+    ms(A("one"), 1.0)
+    ms(A("SX"), 0.0)
+    ms(C("At", 0, 256), 0.0)
+    ms(C("At", 256 + CN + S, 256 + CN + LN), 0.0)
+    ms(C("Ct", 256 + CN + S, 256 + CN + LN), 0.0)
+    ms(C("X", S, XW), 0.0)
+    ms(C("NB", 256 + Q0 + S, 256 + Q0 + LN), 0.0)
+    ms(C("DL", Q0 + S, Q0 + LN), 0.0)
+    for name in ("uu", "lo", "hi"):
+        ms(A(name), 0.0)
+    cp(A("qU"), A("sti"))
+    cp(C("clg", 0, 4), C("sti", 12, 16))
+    cp(C("NB", 256, 256 + Q0), A("nbi"))
+    ts(C("DL", 0, Q0), A("dli"), 256.0, ALU.add)
+
+    def xrep(t):
+        nv = max(MODE[(1, t)].rfind("V"), MODE[(2, t)].rfind("V")) + 1
+        xr = "xr%d" % (t % 2)
+        for k in range(16):
+            o, a = C(xr, k, 512 * nv, 16), C("X", XW * t, XW * t + 32 * nv)
+            if t == 0:
+                cp(o, a)
+            else:
+                asel(o, a, [[0, 32 * nv]], ALU.is_equal, 0.0, 0, 0)
+
+    flip = [0]
+
+    def quarter(stage, t, q, win, lst, key):
+        abn = "ab%d" % stage
+        md = MODE[(stage, t)][2 * q:2 * q + 2]
+        for b0, b1 in ([(0, 2)] if md[0] == md[1] else [(0, 1), (1, 2)]):
+            off = C(lst, 64 * q + 32 * b0, 64 * q + 32 * b1)
+            j0, j1 = 1024 * q + 512 * b0, 1024 * q + 512 * b1
+            if md[b0] == "V":
+                tt(C("vv", j0, j1), IND(win, off), C("xr%d" % (t % 2), j0, j1), ALU.subtract)
+                act(A(abn, sl(j0 // 256, j1 // 256), sl(0, 256)), C("vv", j0, j1), ACT.Abs)
+            else:
+                act(C("ag", j0, j1), IND(win, off), ACT.Copy)
+                for b in range(b0, b1):
+                    bank = A("SB%d" % flip[0])
+                    flip[0] ^= 1
+                    mm([(bank, A("I1"), C("ag", 1024 * q + 512 * b, 1024 * q + 512 * b + 512), True, False),
+                        (bank, A("xT", sl(128 * q, 128 * q + 128), p=sl(0, 64)), A("NE", sl(512 * b, 512 * b + 512), p=sl(0, 64)), False, True)])
+                    act(A(abn, sl(4 * q + 2 * b, 4 * q + 2 * b + 2), sl(0, 256)), bank, ACT.Abs)
+        if stage == 1 or t < RO - 1:
+            mm([(key, selr(r), A(abn, sl(4 * q, 4 * q + 4), sl(16 * r, 16 * r + 16)), r == 0, r == 15) for r in range(16)])
+
+    xrep(0)
+    for t in range(RO):
+        nc = 16 if 0 < t < RO - 1 else 12
+        n, nq = 16 * nc, nc // 4
+        qn, cn = Q0 + LN * t, CN + LN * t
+        x0 = XW * t
+        liU = "liU%d" % (t % 2)
+        last = t == RO - 1
+        halves = [(0, 8), (8, nc)]
+        gin = ("ax", t - 1)
+        for q in range(nq):
+            if "S" in MODE[(1, t)][2 * q:2 * q + 2] + MODE[(2, t)][2 * q:2 * q + 2]:
+                o = A("PS", sl(256 + 128 * (q % 2), 384 + 128 * (q % 2)), p=sl(0, 64))
+                mm([(o, C("X", x0 + 64 * q, x0 + 64 * q + 64), A("I1"), True, True)])
+                ops[-1]["arr"] = gin if q == 3 else None
+                act(A("xT", sl(128 * q, 128 * q + 128), p=sl(0, 64)), o, ACT.Copy)
+        nwin = A("nbi") if t == 0 else C("NB", 256, 256 + qn - LN)
+        for h, (c0, c1) in enumerate(halves):
+            cp(C("caU", 16 * c0, 16 * c1), IND(nwin, C("qU", c0, c1)))
+        if t == 0:
+            cp(C("caF", 0, n), IND(nwin, C("qU", 0, nc)))
+        else:
+            act(C("caF", 0, n), IND(nwin, C("qU", 0, nc)), ACT.Copy)
+        if t + 1 < RO:
+            xrep(t + 1)
+        for h, (c0, c1) in enumerate(halves):
+            kb = "K%d" % h
+            m = 16 * (c1 - c0)
+            for q in range(c0 // 4, c1 // 4):
+                quarter(1, t, q, C("Kt", 0, qn), "caU", C(kb, 64 * q - 16 * c0, 64 * q - 16 * c0 + 64))
+            scan(C("s1", 16 * c0, 16 * c1), C("dmin", 0, m), C(kb, 0, m), 0.0, ALU.add, ALU.min)
+            ts(C("k1U", c0, c1), C("s1", 16 * c0 + 15, 16 * c1, 16), 15.0, ALU.add)
+            tt(C("sel", 16 * c0, 16 * c1), IND(A("Id"), C("k1U", c0, c1)), C("caF", 16 * c0, 16 * c1), ALU.mult)
+            ql = C(kb, 384, 384 + c1 - c0) if h == 0 else C("K0", 392, 392 + c1 - c0)
+            tolist(ql, "sel", c0, c1)
+            ts(C("qU", c0, c1), ql, 0.0625, ALU.mult)
+            ts(C(liU, 16 * c0, 16 * c1), IND(C("DL", 0, qn), C("qU", c0, c1)), -256.0, ALU.add)
+            if not last:
+                act(C("qL", c0, c1), ql, ACT.Identity, scale=0.0625)
+                mm([(C(kb, 128, 128 + m), A("B1"), C("sel", 16 * c0, 16 * c1), True, True)])
+                act(C("qF", 16 * c0, 16 * c1), C(kb, 128, 128 + m), ACT.Copy)
+                asel(C("qR", 16 * c0, 16 * c1), C("qF", 16 * c0, 16 * c1), [[0, m]], ALU.is_equal, 0.0, 0, 0)
+        for q in range(nq):
+            quarter(2, t, q, C("Ct", 256, 256 + cn), liU, C("M", 64 * q, 64 * q + 64))
+        if not last:
+            dma("Y", C("Kt", qn, qn + LN), C("X", x0, x0 + LN))
+            ops[-1]["arr"] = gin if t > 0 else None
+            dma("Y", C("Ct", 0, LN), C("X", x0, x0 + LN))
+            ops[-1]["arr"] = gin if t > 0 else None
+            act(C("liF", 0, n), IND(C("DL", 0, qn), C("qU", 0, nc)), ACT.Copy)
+            act(C("liC", 0, n), C("liF", 0, n), ACT.Identity, bias=-2048.0)
+            nbq = C("NB", 256 + qn, 256 + qn + n)
+            act(nbq, IND(C("NB", 256, 256 + qn), C("qU", 0, nc)), ACT.Copy)
+            iota(C("nR", LN * t, LN * t + LN), [[1, LN]], 256 + cn, 0)
+            iota(A("qn"), [[1, LN]], qn, 0)
+            if t > 0:
+                dma("Y", A("qpm", sl(0, LN), p=sl(7 + t, 128, 16)), A("At", sl(0, LN), p=sl(7 + t, 128, 16)))
+            dma("Y", A("qpm", sl(0, LN), p=sl(8 + t, 128, 16)), A("qn", sl(0, LN), p=sl(8 + t, 128, 16)))
+            for c in range(nc):
+                ts(A("Eb", c, sl(0, n - 16 * c)), C("qR", 16 * c, n), C("qL", c, c + 1), ALU.is_equal, C("pw", 2, 3), ALU.mult)
+            O = C("K1", 256, 256 + n)
+            mm([(O, A("B1"), A("Eb", sl(0, nc), sl(0, 16)), True, False)] +
+               [(C("K1", 256 + 16 * (c + 1), 256 + n), A("B16"), A("Eb", c, sl(16, n - 16 * c)), False, c == nc - 2) for c in range(nc - 1)])
+            tt(C("wR", 0, n), O, C("thr", 0, n), ALU.is_lt)
+            tolist(C("K0", 416, 416 + nc), "wR", 0, nc)
+            L = lambda name: C(name, 0, nc)
+            act(L("win"), C("K0", 416, 416 + nc), ACT.Identity, scale=16.0)
+            live = C("X", x0 + 256, x0 + 260)
+            if nc == 16:
+                tt(C("win", 12, 16), C("win", 12, 16), live, ALU.mult, arr=gin)
+                tt(C("c1", 0, 4), C("qL", 12, 16), C("clg", 0, 4), ALU.subtract)
+                tt(C("c2", 0, 4), C("c1", 0, 4), live, ALU.mult, arr=gin)
+                tt(C("clg", 0, 4), C("clg", 0, 4), C("c2", 0, 4), ALU.add)
+                cp(C("qU", 12, 16), C("clg", 0, 4))
+            qpl = C("QP", 16 * t, 16 * t + nc)
+            act(L("far"), C("s1", 15, n, 16), ACT.Identity, bias=-8965000.0, scale=1.0e4)
+            act(L("qp"), L("qL"), ACT.Identity, bias=256.0)
+            tt(L("wf"), L("far"), L("qp"), ALU.min)
+            tt(L("a2"), L("wf"), L("win"), ALU.min)
+            tt(L("b0"), qpl, L("win"), ALU.subtract)
+            tt(L("lo"), L("b0"), L("qL"), ALU.max)
+            tt(L("hi"), L("far"), qpl, ALU.min)
+            scan(C("sm", 0, n), C("dmin", 0, n), C("M", 0, n), 0.0, ALU.add, ALU.min)
+            kmin, kmax = C("sm", 15, n, 16), C("sx", 15, n, 16)
+            ts(L("uu"), kmin, -640.5, ALU.add, 1.0e4, ALU.mult)
+            tt(L("n1"), L("uu"), L("a2"), ALU.min)
+            tt(L("n2"), L("n1"), L("LL"), ALU.max)
+            cp(L("tnU"), L("n2"))
+            tt(IND(C("NB", 0, 256 + qn), L("tnU")), nbq, C("qpm", 0, n), ALU.max)
+            dma("Y", A("NB", sl(256 + qn, 256 + qn + n), p=sl(t, 128, 16)), A("qF", sl(0, n), p=sl(t, 128, 16)))
+            scan(C("sx", 0, n), C("dmax", 0, n), C("M", 0, n), 0.0, ALU.add, ALU.max)
+            act(C("uu", 16, 16 + nc), kmin, ACT.Identity, bias=-6405000.0, scale=1.0e4)
+            ts(C("lo", 16, 16 + nc), kmin, 15.0, ALU.add, 655.0, ALU.min)
+            act(C("hi", 16, 16 + nc), kmax, ACT.Identity, bias=4511.0, scale=-1.0)
+            tt(A("d1"), A("uu"), A("hi"), ALU.min)
+            tt(A("d2"), A("d1"), A("lo"), ALU.max)
+            cp(A("tdU"), A("d2"))
+            ixU = C("tdU", 16, 16 + nc)
+            tt(C("mn", 0, n), IND(A("Id"), ixU), C("nR", LN * t, LN * t + n), ALU.mult)
+            tt(IND(C("DL", 0, qn + LN), L("tdU")), C("liF", 0, n), C("mn", 0, n), ALU.max)
+            tt(C("sel2", 0, n), IND(A("Id"), ixU), C("liC", 0, n), ALU.mult)
+            tolist(C("K0", 400, 400 + nc), "sel2", 0, nc)
+            act(L("un"), L("uu"), ACT.Identity, scale=-1.0)
+            act(L("f1"), C("K0", 400, 400 + nc), ACT.Identity, bias=2048.0, scale=0.0625)
+            tt(L("f2"), L("f1"), L("un"), ALU.min)
+            tt(L("f3"), L("f2"), L("LL"), ALU.max)
+            cp(L("cxU"), L("f3"))
+            act(C("Ct", 256 + cn, 256 + cn + n), IND(C("Ct", 0, 256 + cn), L("cxU")), ACT.Copy)
+            if t < RO - 2:
+                ts(C("nvU", 0, 12), C("sm", 15, S, 16), 641.0, ALU.is_ge)
+                tt(A("fR"), IND(A("T01"), C("nvU", 0, 12)), C("wR", 0, S), ALU.mult)
+                scan(A("cum"), A("one"), A("fR"), 0.0, ALU.mult, ALU.add)
+                for c in range(4):
+                    act(A("sj"), A("cum"), ACT.Sign, bias=C("jb", c, c + 1), scale=-1.0, acc=C("acc", c, c + 1))
+                ts(C("srU", 0, 4), C("acc", 0, 4), 0.5, ALU.mult, 96.0, ALU.add)
+                act(C("SX", 72 * t + 64, 72 * t + 68), C("acc", 0, 4), ACT.Sign, bias=192.0, scale=-1.0)
+                act(C("SX", 72 * t, 72 * t + 64), IND(C("X", x0, x0 + S + 16), C("srU", 0, 4)), ACT.Copy, arr=gin if t > 0 else None)
+                add("G", 300, ("ax", t, C("X", x0 + XW + S, x0 + XW + S + 72), C("SX", 72 * t, 72 * t + 72)), [C("SX", 72 * t, 72 * t + 72)], [], kind="rem")
+        for b in range(6):
+            bank = A("D%d" % (b % 2))
+            mm([(bank, A("B1"), A("ab2", sl(2 * b, 2 * b + 2), sl(0, 256)), True, True)])
+            act(C("wr", 512 * b, 512 * b + 512), bank, ACT.Exp, scale=-0.015625)
+            tt(C("pr", 512 * b, 512 * b + 512), IND(C("At", 256, 256 + cn), C(liU, 32 * b, 32 * b + 32)), C("wr", 512 * b, 512 * b + 512), ALU.mult,
+               arr=("aa", t - 2) if t >= 2 else None)
+            if b % 2 == 1:
+                q = b // 2
+                pq = C("Pt", S * t + 64 * q, S * t + 64 * q + 64)
+                if SUM[t][q] == "V":
+                    scan(C("so", 1024 * q, 1024 * q + 1024), A("rs"), C("pr", 1024 * q, 1024 * q + 1024), 0.0, ALU.mult, ALU.add)
+                    if last:
+                        act(pq, C("so", 1024 * q + 15, 1024 * q + 1024, 16), ACT.Copy)
+                    else:
+                        asel(pq, C("so", 1024 * q + 15, 1024 * q + 1024, 16), [[0, 64]], ALU.is_equal, 0.0, 0, 0)
+                else:
+                    o = C("PS", 64 * q, 64 + 64 * q)
+                    for k0 in range(0, 16, 4):
+                        mm([(o, A("If"), C("pr", 1024 * q + k, 1024 * q + 1024, 16), k == 0, k == 15) for k in range(k0, k0 + 4)])
+                        ops[-1]["open"] = (k0 > 0, k0 < 12)
+                    act(pq, o, ACT.Copy)
+        dma("Y", C("yp", S * t, S * t + S), C("Pt", S * t, S * t + S))
+        if not last:
+            mm([(C("M", 256, 256 + S), A("Iy"), C("Y", S * t, S * t + S), True, False),
+                (C("M", 256, 256 + S), A("Ip"), C("Pt", S * t, S * t + S), False, True)])
+            act(A("hh"), C("M", 256, 256 + S), ACT.Copy)
+            an = C("At", 256 + cn, 256 + cn + S)
+            tt(an, IND(C("At", 0, 256 + cn), C("cxU", 0, 12)), A("hh"), ALU.add, arr=("aa", t - 2) if t >= 2 else None)
+            if t < RO - 2:
+                act(C("SA", 64 * t, 64 * t + 64), IND(C("At", 256 + cn, 256 + cn + S + 8), C("srU", 0, 4)), ACT.Copy,
+                    arr=("aa", t - 1) if t > 0 else None)
+                a1 = 256 + cn + LN + S
+                add("G", 300, ("aa", t, C("At", a1, a1 + H), C("SA", 64 * t, 64 * t + 64)), [C("SA", 64 * t, 64 * t + 64)], [], kind="rem")
+    return ops
+
+
+def schedule(ops, bias=None):
+    hist = {}
+    sends = {}
+    for i, o in enumerate(ops):
+        deps, same = set(), set()
+        for write, items in ((False, o["r"]), (True, o["w"])):
+            for name, lo, hi, n1 in items:
+                if name not in SCRATCH:
+                    continue
+                for (l2, h2, j, w2) in hist.get(name, []):
+                    if j != i and l2 < hi and lo < h2 and (write or w2):
+                        if o["eng"] == "P" and ops[j]["eng"] == "P":
+                            same.add(j)
+                        elif write and w2 and name[:2] == "xr" and o["eng"] == ops[j]["eng"] and i - j < 16:
+                            same.add(j)
+                        else:
+                            deps.add(j)
+        for write, items in ((False, o["r"]), (True, o["w"])):
+            for name, lo, hi, n1 in items:
+                if name not in SCRATCH:
+                    continue
+                hl = hist.setdefault(name, [])
+                if write and name[:2] != "xr":
+                    hl[:] = [e for e in hl if not (lo <= e[0] and e[1] <= hi)]
+                hl.append((lo, hi, i, write))
+        o["deps"] = deps
+        o["ord"] = same
+        o["banks"] = sorted(set(x[0] for x in o["r"] + o["w"] if x[0] in SCRATCH and SCRATCH[x[0]][0] == "psum"))
+        if o["kind"] == "rem":
+            sends[o["fn"][:2]] = i
+    n = len(ops)
+    lat = lambda j: DMAL if ops[j]["kind"] != "c" else LAT
+    pre = []
+    for o in ops:
+        p = [(j, lat(j)) for j in o["deps"]] + [(j, 0.0) for j in o["ord"]]
+        if o["arr"] is not None:
+            p.append((sends[o["arr"]], DMAL + 500))
+        pre.append(p)
+    succ = [[] for _ in ops]
+    for i in range(n):
+        for j, l in pre[i]:
+            succ[j].append((i, l))
+    prio = [0.0] * n
+    for i in range(n - 1, -1, -1):
+        tail = DMAL if ops[i]["kind"] != "c" else 0.0
+        prio[i] = ops[i]["cost"] + max([tail] + [l + prio[k] for k, l in succ[i]])
+    left = [len(p) for p in pre]
+    ready = [0.0] * n
+    pool = {e: [] for e in "VSPGY"}
+    for i in range(n):
+        if left[i] == 0:
+            pool[ops[i]["eng"]].append(i)
+    free = {e: 0.0 for e in pool}
+    order = []
+    end = 0.0
+    user = {}
+    held = set()
+
+    def when(k):
+        o = ops[k]
+        r = ready[k]
+        for b in o["banks"]:
+            if b in held and o["eng"] == "P" and not o.get("open", (False, False))[0]:
+                return 1e18
+            for e2, j in user.get(b, {}).items():
+                if e2 != o["eng"]:
+                    r = max(r, ops[j]["t"][1] + LAT)
+        return r
+
+    while len(order) < n:
+        best = None
+        for e, pl in pool.items():
+            if not pl:
+                continue
+            t0 = max(free[e], min(when(i) for i in pl))
+            if best is None or t0 < best[0]:
+                best = (t0, e)
+        t0, e = best
+        i = max((k for k in pool[e] if when(k) <= t0 + AHEAD), key=lambda k: prio[k] + (bias[k] if bias else 0.0))
+        pool[e].remove(i)
+        ready[i] = when(i)
+        for b in ops[i]["banks"]:
+            us = user.setdefault(b, {})
+            ops[i]["deps"].update(j for e2, j in us.items() if e2 != e)
+            us[e] = i
+            if "open" in ops[i]:
+                if ops[i]["open"][1]:
+                    held.add(b)
+                else:
+                    held.discard(b)
+        t1 = max(t0, ready[i]) + ops[i]["cost"]
+        ops[i]["t"] = (t1 - ops[i]["cost"], t1)
+        free[e] = t1
+        end = max(end, t1)
+        order.append(i)
+        for k, l in succ[i]:
+            ready[k] = max(ready[k], t1 + l)
+            left[k] -= 1
+            if left[k] == 0:
+                pool[ops[k]["eng"]].append(k)
+    return order, end
+
+
+def plan():
+    ops = build_ops()
+    order, end = schedule(ops, [BIAS.get(o["eng"] + (o["w"][0][0] if o["w"] else "rem"), 0.0) for o in ops])
+    cnt = {e: 0 for e in "VSPG"}
+    known = {e: {} for e in "VSPGY"}
+    nd = 0
+    for i in order:
+        o = ops[i]
+        e = o["eng"]
+        need = {}
+        for j in o["deps"]:
+            s, v = ops[j]["sig"]
+            if known[e].get(s, 0) < v and need.get(s, (0, 0))[0] < v:
+                need[s] = (v, j)
+        if o["arr"] is not None:
+            s = "%s%d" % o["arr"]
+            if known[e].get(s, 0) < NENG:
+                need[s] = (NENG, None)
+        waits = []
+        for s, (v, j) in sorted(need.items(), key=lambda kv: -1 if kv[1][1] is None else -ops[kv[1][1]]["t"][1]):
+            if known[e].get(s, 0) >= v:
+                continue
+            waits.append((s, v))
+            known[e][s] = v
+            if j is not None:
+                for s2, v2 in ops[j]["clock"].items():
+                    if known[e].get(s2, 0) < v2:
+                        known[e][s2] = v2
+        o["waits"] = waits
+        o["clock"] = dict(known[e])
+        if o["kind"] == "c":
+            cnt[e] += 1
+            o["sig"] = ("e" + e, cnt[e])
+        elif o["kind"] == "dma":
+            o["sig"] = ("d%d" % nd, 16)
+            nd += 1
+        else:
+            o["sig"] = ("lx", 0)
+    return ops, order, cnt, nd, end
+
+
+PLAN = []
+
+
+def rank_program(g, core, T, topo):
+    rank = T.rank_of(core)
+    if rank is None:
+        return
+    if not PLAN:
+        PLAN.append(plan())
+    ops, order, cnt, nd, end = PLAN[0]
+    queue = {"V": g.vector, "S": g.scalar, "P": g.tensor, "G": g, "Y": g.sync}
+    nranks = len(T.cores)
+    sent = 0
+    for i in order:
+        o = ops[i]
+        qe = queue[o["eng"]]
+        for s, v in o["waits"]:
+            qe.wait_ge(T.sem[s], v)
+        if o["kind"] == "rem":
+            name, t, out, src = o["fn"]
+            dst = T.cores[(rank + 1 + t % (nranks - 1)) % nranks]
+            rid, pid, _ = topo.addr(dst)
+            mask = sum(1 << e for e in topo.engines(core, dst)[:NENG])
+            g.remote_dma(ap(T, out), ap(T, src), T.sem["%s%d" % (name, t)], T.sem["lx"], pid, rid, mask)
+            sent += NENG
+        else:
+            o["fn"](g, T).then_inc(T.sem[o["sig"][0]], 16 if o["kind"] == "dma" else 1)
+    for e in "VSPG":
+        g.wait_ge(T.sem["e" + e], cnt[e])
+    for k in range(nd):
+        g.wait_ge(T.sem["d%d" % k], 16)
+    for k in range(4):
+        g.wait_ge(T.sem["ax%d" % k], NENG)
+        g.wait_ge(T.sem["aa%d" % k], NENG)
+    g.wait_ge(T.sem["lx"], sent)

@@ -1,3 +1,4 @@
+import math
 from concourse.bass import DstId, RemoteDMATransfer
 from concourse.mybir import dt, AluOpType, AxisListType, ActivationFunctionType
 
@@ -5,71 +6,88 @@ ALU = AluOpType
 ACT = ActivationFunctionType
 CN, Q0, S, H, RO, LN = 2560, 768, 192, 64, 6, 256
 XW = 272
-IDW = 4512
-BIG = 1.0e6
-MODE = {}
-for _t in range(RO):
-    MODE[(1, _t)] = ['VSSVVSSS', 'VVSSVSSS', 'VVSVVVSS', 'VVSSVSSS', 'VVSVVVSS', 'VVSSVSSS'][_t]
-    MODE[(2, _t)] = ['VVSSVVSS', 'VVSSVVSS', 'VVSSVVSS', 'VVSSVVSS', 'SVSSVVSS', 'VVSSVVSS'][_t]
-SUM = ['VPV', 'VPV', 'VPV', 'VPP', 'VPP', 'VPV']
-BIAS = {'Vdmax': 4400, 'PSB0': 600, 'GI1': 1000, 'SX': 1000, 'Vc1': -400, 'GB1': 1000, 'SliC': 1000, 'VZ': 400, 'Ssj': -1000, 'GQP': -1000,
-        'GPt': 4000, 'YY': -4000, 'Vij': 2400, 'VI16': -2000, 'Vb0': 4000, 'YKt': -2000, 'Vpr': -4000, 'Vf2': 6800, 'Vxr0': -1000,
-        'VliU0': -1000, 'VtnU': -400, 'Vcum': 4000, 'Shh': 5600, 'Vone': -1000, 'Vmn': -1000, 'Vpm': 2000, 'Vk1U': 400, 'Yqpm': 1000,
-        'Vrs': 4000, 'Swin': 400, 'Vn1': 1400, 'SKt': 1000, 'VtdU': 4000, 'VwR': -1000, 'Vsel2': 2000, 'VIf': -1000, 'GnR': -1000,
-        'Vjb': -400, 'Shi': 3000, 'VSX': -2000, 'Vqpm': -1000, 'Yyp': -2000, 'SqF': -400, 'Vd1': 1000, 'Sfar': 2000, 'VIp': -1000,
-        'VCt': -1000, 'YId': 4000, 'YCt': -400, 'Sf1': 400, 'VI1': 400, 'GAt': 12000, 'Vwf': -400, 'SliF': 400, 'Gxr1': -2000, 'Ysti': 2000}
-for _t in range(RO):
-    MODE[(1, _t)] = ['SVSVVSSS', 'VVSSVSSS', 'VVSVVVSS', 'VVSSVSSS', 'VVVSVVSS', 'VVSSVSSS'][_t]
-    MODE[(2, _t)] = ['VVSSVVSS', 'VVSSVVSS', 'VVSSVVSS', 'VVSSVVSS', 'SSVSVVSS', 'SVVSVVSS'][_t]
-SUM = ['VPV', 'VPV', 'VPV', 'VPP', 'VPP', 'PVV']
-BIAS = {'Vdmax': 4400, 'PSB0': -1000, 'GI1': 1000, 'SX': 1000, 'Vc1': -800, 'SliC': 1000, 'VZ': 2400, 'Ssj': 1800, 'GQP': -4000, 'GPt': 7000, 'YY': -10000, 'Vij': 2400, 'VI16': -2000, 'Vb0': 4000, 'YKt': -400, 'Vpr': -4000, 'Vf2': 800, 'Vxr0': -1000, 'VliU0': 1000, 'VtnU': 1600, 'Vcum': 4000, 'Shh': 5600, 'Vmn': -1000, 'Vpm': 2000, 'Vk1U': 2400, 'Yqpm': -1000, 'Vrs': 3600, 'Swin': 3400, 'Vn1': 1400, 'SKt': -11400, 'VtdU': 5600, 'VwR': -2000, 'Vsel2': 6000, 'VIf': -1400, 'GnR': 1000, 'Vjb': 1600, 'Shi': 9000, 'VSX': -2400, 'Vqpm': -600, 'Yyp': -2000, 'SqF': -800, 'Vd1': 1000, 'VIp': 1000, 'VCt': -1000, 'YId': 600, 'YCt': -400, 'Sf1': 400, 'VI1': -1000, 'GAt': 12000, 'Vwf': -1400, 'SliF': 400, 'Gxr1': -5000, 'Ysti': 6000, 'VB16': 1000, 'GNE': -4000, 'VQP': 400, 'VId': -400, 'VT01': -3600, 'Gii': 2000, 'YX': -9000, 'PM': 400, 'Gxr0': 600, 'VliU1': -1000, 'Swr': 1600, 'Vsel': -400, 'Vd2': 2000, 'Ynbi': -4000, 'Vclg': 400, 'Vwin': -3000, 'Vso': -400, 'Vsm': 4000, 'Vf3': 400, 'Grem': 1600, 'SPt': -3000, 'VfR': 3600, 'VsrU': 400, 'YNB': -1000, 'VNB': -4000, 'Gqn': 1000, 'Vseed': 4000, 'SqL': -1000, 'Vdmin': -800, 'VX': 1000, 'Ydli': 1400, 'SCt': -3600, 'Sqp': -400, 'PD0': 400, 'Vn2': -1000, 'Vthr': 2000, 'Sun': -2000, 'Vsx': 1400, 'VIy': -1000, 'Suu': -1000, 'Vtm': 2000}
+SW = 208
+NOV, KB, ZC, IDW = 656, 672, 4528, 4544
+OFF = 2048.0
+VOID = 2097152.0
+BIG = 1099511627776.0
 NENG = 8
+CFG = {
+    "m1": ["VVVSVV", "DDDDVVSS", "DDDDDDSS", "DDDDDDSS", "DDDDDDSS", "DDDDDD"],
+    "m2": ["VVVSVV", "VVVVVVSS", "VVVVVSSS", "VVVVVVSS", "VVVVVSSS", "VSVSSS"],
+    "sum": ["PPP", "PPP", "PPP", "PPP", "PVP", "PVV"],
+    "ny": [2, 0, 0, 0, 6, 6],
+    "half": [12] * 6,
+    "dram": False, "period": 19000.0, "due": [-1e6, 8000.0], "merge": "D", "lam": 0.05, "dw": 512, "pk": 4, "pw": [512] * 6, "da": 512, "flat": False, "apart": True, "caG": False, "early": True, "tiny": "VVV", "ils": 0, "ts": 400, "x0": "VVSVG",
+    "line": (), "ahead": 100.0, "rounds": 0, "noise": 200.0, "seed": 1,
+    "bias": {'period': 19500, 'pace': 1.2, 'init': 4, 'VcaU': -153, 'Sag1': -105, 'Vag1': -100, 'Gag1': -165, 'Sab1': -90, 'PK0': -17, 'PSB': 28, 'Gxr': -50, 'Sag1g': -35, 'VcaF': 9, 'PK118': -30, 'VpU': -36, 'Vvp': 10, 'Sabp': 44, 'PKp': 2, 'Vs1': 1, 'Vk1U': -33, 'Vsel': 65, 'PK116': 11, 'VqU': 72, 'VliU': 80, 'SqL': 86, 'PK1': 42, 'SqF': -5, 'GqR': 53, 'SNQ': 34, 'Sfar': 118, 'Vag2': 63, 'Sag2': 53, 'Sab2': 63, 'PM': 60, 'PD0': 95, 'Swc': 105, 'Ywr': 102, 'YWd': 100, 'Swr': 125, 'Gag2': 53, 'Vov': 46, 'PM24': 20, 'SxT': 46, 'Sab1g': 55, 'PK0g': 108, 'Vvpg': 16, 'Sabpg': 44, 'Vs1g': 18, 'Vk1Ug': 53, 'Vselg': 70, 'VqUg': 57, 'VliUg': 27, 'SqLg': 17, 'SqFg': 59, 'GqRg': -18, 'SNQg': 122, 'Sag2g': -60, 'Sab2g': -32, 'PMg': 55, 'SliF': 165, 'VEb': 75, 'PD1': 75, 'SwR': 105, 'PD116': 62, 'VLO': 175, 'SLO': 98, 'Vsm': 55, 'Vsx': 180, 'VFF': 62, 'SFF': -13, 'Vi2U': 77, 'SHI': 85, 'VfR': 110, 'Vcum': 117, 'Ssj': 82, 'VsrU': 135, 'SSX': 113, 'Grem': 76, 'Vd1': 18, 'Vd2': 134, 'VtdU': 112, 'VNB': 168, 'Vmn': 198, 'VDL': 265, 'Vsel2': 225, 'PK117': 217, 'Vcx': 214, 'VcxU': 227, 'SCt': 196, 'YNB': 120, 'Yqpm': 3, 'YKt': 42, 'YCt': 23, 'Vpr': 290, 'PPS': 285, 'Vso': 290, 'Shh': 263, 'VAt': 285, 'VPt': 368, 'SSA': 285, 'Yyp': 325, 'SPt': 300, 'SCt5': 176, 'Vov4': 21, 'VliU0': 92, 'Vselg0': 100, 'Vsm5': 110, 'Sag14': -65, 'PSB0': 25, 'VAt4': 270, 'PK14': 37, 'PM245': 32, 'Vd24': 84, 'SHI0': 58, 'VcaF4': -31, 'Vsel5': 105, 'Gag10': -158, 'PD14': 115, 'Ssj0': 84, 'Vs1g4': 8, 'Sfar0': 106, 'SqL4': 96, 'Vag25': 68, 'VpU5': -16, 'PK1160': 36, 'SliF4': 125, 'Sab1g0': 97, 'SqLg5': 17, 'VEb0': 80, 'GqRg5': 22, 'Sag15': -103, 'SqFg4': 69, 'Vs14': 1, 'VsrU4': 145, 'GqR0': 53, 'Gxr4': -25, 'Vsx0': 170, 'Vk1Ug4': 15, 'Vpr0': 295, 'SNQg4': 124, 'Vcum4': 107, 'VsrU5': 175, 'PD1160': 52, 'Swr4': 165, 'VfR4': 105},
+}
+
+CFG.update(apart=False, flat=False, caG=True, da=1024, ils=25, due=[-1e6, -1e6], sum=["PVP", "PVP", "VPV", "PVP", "VPV", "PVV"])
+CFG["bias"] = {'period': 21500, 'pace': 0.8, 'init': 7, 'VcaU': -153, 'Sag1': -100, 'Vag1': -95, 'Gag1': -152, 'Sab1': -70, 'PK0': -17, 'PSB': 18, 'Gxr': -70, 'Sag1g': 87, 'VcaF': -31, 'PK118': -35, 'VpU': -36, 'Vvp': 10, 'Sabp': 44, 'PKp': 69, 'Vs1': 4, 'Vk1U': -13, 'Vsel': -17, 'PK116': 1, 'VqU': 72, 'VliU': 70, 'SqL': 98, 'PK1': 40, 'SqF': 17, 'GqR': 101, 'SNQ': -1, 'Sfar': 46, 'Vag2': 65, 'Sag2': 68, 'Sab2': 53, 'PM': 60, 'PD0': 79, 'Swc': 60, 'Ywr': 102, 'YWd': 100, 'Swr': 153, 'Gag2': 53, 'Vov': 66, 'PM24': 72, 'SxT': 66, 'Sab1g': 50, 'PK0g': 108, 'Vvpg': 16, 'Sabpg': 44, 'Vs1g': 28, 'Vk1Ug': 53, 'Vselg': 70, 'VqUg': 25, 'VliUg': 27, 'SqLg': 27, 'SqFg': 59, 'GqRg': -33, 'SNQg': 113, 'Sag2g': -60, 'Sab2g': -32, 'PMg': 50, 'SliF': 167, 'VEb': 49, 'PD1': 134, 'SwR': 147, 'PD116': 32, 'VLO': 175, 'SLO': 98, 'Vsm': 55, 'Vsx': 175, 'VFF': 62, 'SFF': -13, 'Vi2U': 87, 'SHI': 85, 'VfR': 154, 'Vcum': 97, 'Ssj': 72, 'VsrU': 93, 'SSX': 113, 'Grem': 76, 'Vd1': 10, 'Vd2': 136, 'VtdU': 142, 'VNB': 166, 'Vmn': 323, 'VDL': 323, 'Vsel2': 237, 'PK117': 269, 'Vcx': 234, 'VcxU': 187, 'SCt': 208, 'YNB': 138, 'Yqpm': 43, 'YKt': 82, 'YCt': 23, 'Vpr': 290, 'PPS': 280, 'Vso': 290, 'Shh': 258, 'VAt': 315, 'VPt': 410, 'SSA': 305, 'Yyp': 325, 'SPt': 300, 'GcaU': -180, 'VcaUg': -30, 'VHI': 75, 'SliF0': 175, 'Vsx0': 160, 'Vag20': 23, 'VfR0': 115, 'Vsm0': 65, 'Sab10': -85, 'GqR4': 43, 'Vvp4': 20, 'PK05': 13, 'VEb0': 105, 'Sfar0': 96, 'VcxU0': 147, 'Vpr4': 268, 'SSX0': 133, 'Vcx0': 239, 'Vs10': -3, 'Sag20': 58, 'SNQg4': 103, 'Vag24': 85, 'SqL0': 48, 'Sag15': -140, 'VDL0': 327, 'PSB4': 8, 'PK1165': -4}
+CFG.update(ny=[6] * 6, m1=["VVVSVV"] + ["DDDDVVSS"] * 4 + ["DDDDDD"], m2=["VVVSVV"] + ["VVVVVVSS"] * 4 + ["VSVSSS"], sum=["PPP", "PPP", "PPP", "PPP", "PVP", "PVV"])
+CFG["bias"].update({'PD0': 195, 'Vpr': 215, 'Vso': 220, 'period': 19900, 'pace': 1.0, 'init': 10, 'Sag1': -95, 'Gag1': -192, 'Sab1': -30, 'PK0': -14, 'PSB': 16, 'Gxr': -30, 'Sag1g': 52, 'PK118': 15, 'Vvp': -30, 'Sabp': -11, 'PKp': 29, 'Vs1': 9, 'Vk1U': -33, 'VliU': 60, 'SqL': 95, 'PK1': 15, 'GqR': 106, 'SNQ': -36, 'Vag2': 55, 'Sag2': 21, 'Sab2': 91, 'PM': 80, 'Swr': 195, 'Vov': 76, 'PM24': 112, 'SxT': 16, 'PK0g': 98, 'Vk1Ug': 13, 'VqUg': 30, 'SqLg': 67, 'SqFg': 64, 'GqRg': -73, 'SNQg': 123, 'Sag2g': -62, 'Sab2g': -17, 'VEb': 69, 'SwR': 117, 'PD116': -48, 'Vsx': 170, 'Vcum': 147, 'Ssj': 47, 'SSX': 133, 'Grem': 96, 'Vd1': -20, 'VNB': 88, 'PK117': 274, 'Vcx': 274, 'VcxU': 177, 'SCt': 228, 'Yqpm': -17, 'YKt': 115, 'PPS': 360, 'Shh': 261, 'VAt': 352, 'SSA': 365, 'GcaU': -207, 'VcaUg': -15, 'VHI': 63, 'Vs10': -1, 'PSB0': -22, 'VFF0': 55, 'YCt0': 43, 'VqUg4': 5, 'PKp5': 29, 'Vsm4': 53, 'SliF4': 177, 'Sag25': 63, 'Gxr4': -32, 'SSA0': 325, 'Yyp0': 323, 'PPS0': 370, 'Vk1U0': -38, 'Vmn0': 313, 'Sab15': -50})
+CFG.update(apart=True, m1=["VVVSVV"] + ["SSDDVVSS"] * 4 + ["DDDDSS"], ils=30, seed=5)
+CFG["bias"].update({'period': 19500, 'pace': 1.2, 'init': 14, 'Sag1': -89, 'Gag1': -187, 'PK0': -19, 'PSB': 31, 'Gxr': 58, 'Sag1g': 62, 'VcaF': -26, 'PK118': 17, 'VpU': -56, 'Vvp': -50, 'Sabp': 12, 'PKp': 84, 'Vs1': -11, 'Vk1U': -31, 'Vsel': 20, 'PK116': -41, 'VliU': 70, 'SqL': 115, 'PK1': 55, 'GqR': 156, 'SNQ': -41, 'Sfar': 75, 'Sag2': 26, 'Sab2': 63, 'PM': 55, 'Swr': 197, 'SxT': -4, 'Sab1g': 70, 'PK0g': 96, 'Vk1Ug': 53, 'Vselg': 50, 'VqUg': 32, 'VliUg': 37, 'SqLg': 55, 'SqFg': 71, 'GqRg': -68, 'SNQg': 113, 'Sab2g': 23, 'PMg': 45, 'SliF': 139, 'VEb': 52, 'SwR': 75, 'PD116': -21, 'VLO': 172, 'Vsm': 18, 'Vsx': 118, 'Vi2U': 62, 'VfR': 57, 'Vcum': 172, 'Ssj': 88, 'VsrU': 10, 'SSX': 82, 'Grem': 120, 'Vd1': 0, 'Vd2': 96, 'VtdU': 90, 'VNB': 86, 'Vmn': 280, 'VDL': 345, 'Vsel2': 294, 'VcxU': 119, 'SCt': 208, 'YNB': 116, 'YKt': 75, 'Vpr': 223, 'PPS': 310, 'Shh': 214, 'VAt': 350, 'VPt': 313, 'SSA': 375, 'Yyp': 303, 'GcaU': -187, 'VcaUg': -53, 'VHI': 98, 'SliF0': 185, 'Vpr4': 258, 'Sag20': 63, 'SNQg4': 63, 'Vag24': 95, 'Sag15': -130, 'SSA0': 365, 'Sab15': -60, 'VEg': 90, 'PD1g': 85, 'SwRg': 90, 'Vsmg': 90, 'Vi2Ug': 92, 'SSX4': 100, 'Vsel0': -20, 'VcaF4': -51, 'SqFg4': 71, 'Vi2U0': 32, 'Vpr0': 173, 'Vcx4': 284, 'Swr4': 152, 'Grem4': 90, 'Sab24': 86, 'Sab1g4': 65, 'Vmn4': 275, 'VqU5': 70, 'Gxr0': 38, 'Yqpm0': -37, 'PD1164': -48, 'VqU0': 67, 'YNB0': 126, 'VFF4': 82})
+CFG.update(m1=["VVVSVV"] + ["SSSSVVSS"] * 4 + ["SSSVSS"], sum=["PVP", "PVP", "PVP", "PVP", "PVP", "PVV"], seed=2)
+CFG["bias"].update({'period': 19900, 'init': 12, 'Sag1': -29, 'Vag1': -85, 'Sab1': -25, 'PK0': 61, 'PSB': 26, 'Gxr': 78, 'VcaF': -31, 'PK118': 52, 'VpU': -51, 'VqU': 52, 'VliU': 48, 'SqL': 113, 'PK1': 15, 'SqF': 55, 'SNQ': -49, 'Sfar': 165, 'Vag2': 53, 'Sag2': 46, 'Sab2': 65, 'PM': 53, 'PD0': 115, 'Swr': 207, 'Vov': 86, 'PM24': 72, 'Sab1g': 85, 'Vs1g': 48, 'VliUg': 57, 'GqRg': -60, 'SNQg': 133, 'Sag2g': -22, 'Sab2g': 13, 'PMg': 55, 'SliF': 134, 'SwR': 45, 'Vsm': 13, 'Vsx': 103, 'VFF': 22, 'Vi2U': 107, 'Vcum': 270, 'Grem': 127, 'Vd2': 148, 'VtdU': 70, 'VNB': 81, 'VDL': 305, 'Vsel2': 254, 'SCt': 193, 'YNB': 114, 'YKt': 85, 'Shh': 176, 'VPt': 328, 'SSA': 475, 'Yyp': 261, 'VcaUg': -29, 'VHI': 138, 'PKp5': 31, 'Sab15': -50, 'VEg': 46, 'Swr4': 157, 'Sab24': 106, 'Vmn4': 285, 'VFF4': 102, 'Sabp0': 2, 'VtdU4': 80, 'Yqpm4': -27, 'Vd20': 108, 'Vso5': 215, 'Vs15': -16, 'Vso4': 218, 'VcaUg4': 11, 'PM4': 33})
 
 SCRATCH = {
     "Kt": ("sbuf", [128, 2048], "bfloat16"), "Ct": ("sbuf", [128, 4096], "bfloat16"), "At": ("sbuf", [128, 4096], "float32"),
-    "NB": ("sbuf", [128, 2304], "float32"), "DL": ("sbuf", [128, 2048], "float32"),
+    "NB": ("sbuf", [128, 2048], "float32"), "DL": ("sbuf", [128, 2048], "float32"),
     "nbi": ("sbuf", [128, 768], "int32"), "dli": ("sbuf", [128, 768], "int32"), "sti": ("sbuf", [128, 16], "int32"),
-    "X": ("sbuf", [128, RO * XW], "bfloat16"), "Y": ("sbuf", [128, RO * S], "bfloat16"), "Pt": ("sbuf", [128, RO * S], "float32"),
-    "Id": ("sbuf", [128, IDW], "bfloat16"), "Z": ("sbuf", [128, 144], "bfloat16"), "B1": ("sbuf", [128, 128], "bfloat16"),
-    "B16": ("sbuf", [128, 128], "bfloat16"), "I1": ("sbuf", [128, 128], "bfloat16"), "Iy": ("sbuf", [128, 128], "bfloat16"),
-    "Ip": ("sbuf", [128, 128], "float32"), "If": ("sbuf", [128, 128], "float32"), "NE": ("sbuf", [128, 1024], "bfloat16"), "xT": ("sbuf", [128, 4 * 128], "bfloat16"),
+    "X": ("sbuf", [128, RO * XW], "bfloat16"), "XS": ("sbuf", [128, 4 * SW], "bfloat16"),
+    "Y": ("sbuf", [128, RO * S], "bfloat16"), "Pt": ("sbuf", [128, RO * S], "float32"),
+    "Id": ("sbuf", [128, IDW], "bfloat16"), "NV": ("sbuf", [128, KB], "bfloat16"),
+    "Z": ("sbuf", [128, 144], "bfloat16"), "Zw": ("sbuf", [128, 144], "bfloat16"),
+    "If": ("sbuf", [128, 128], "float32"), "NE": ("sbuf", [128, 1024], "bfloat16"), "xT": ("sbuf", [128, 4 * 128], "bfloat16"),
     "xr0": ("sbuf", [128, 3072], "bfloat16"), "xr1": ("sbuf", [128, 3072], "bfloat16"),
-    "ab1": ("sbuf", [128, 16, 256], "bfloat16"), "ab2": ("sbuf", [128, 16, 256], "bfloat16"), "ag": ("sbuf", [128, 4096], "bfloat16"),
-    "vv": ("sbuf", [128, 3072], "bfloat16"),
-    "wr": ("sbuf", [128, 3072], "float32"), "pr": ("sbuf", [128, 3072], "float32"), "so": ("sbuf", [128, 3072], "float32"),
-    "Eb": ("sbuf", [128, 16, 256], "bfloat16"),
-    "caU": ("sbuf", [128, 256], "uint16"), "caF": ("sbuf", [128, 256], "float32"), "sel": ("sbuf", [128, 256], "float16"),
-    "liU0": ("sbuf", [128, 256], "uint16"), "liU1": ("sbuf", [128, 256], "uint16"),
-    "liF": ("sbuf", [128, 256], "float32"), "liC": ("sbuf", [128, 256], "float32"), "sel2": ("sbuf", [128, 256], "float16"),
+    "ab1": ("sbuf", [128, 64, 64], "bfloat16"), "ab2": ("sbuf", [128, 64, 64], "bfloat16"),
+    "ag1": ("sbuf", [128, 4096], "bfloat16"), "ag2": ("sbuf", [128, 4096], "bfloat16"), "xr2": ("sbuf", [128, 3072], "bfloat16"),
+    "caS": ("sbuf", [128, 256], "float32"), "vp": ("sbuf", [128, 256], "bfloat16"), "abp": ("sbuf", [128, 256], "bfloat16"),
+    "wr0": ("sbuf", [128, 3072], "float32"), "wr1": ("sbuf", [128, 3072], "float32"), "wc": ("sbuf", [128, 192], "float32"),
+    "Wd": ("dram", [8, 3072], "float32"),
+    "pr": ("sbuf", [128, 3072], "float32"), "so": ("sbuf", [128, 1024], "float32"),
+    "Eb": ("sbuf", [128, 16, 256], "bfloat16"), "Eg": ("sbuf", [128, 16, 64], "bfloat16"),
+    "caU": ("sbuf", [128, 256], "uint16"), "caF": ("sbuf", [128, 256], "float16"), "sel": ("sbuf", [128, 256], "float16"),
+    "liU0": ("sbuf", [128, 256], "uint16"), "liU1": ("sbuf", [128, 256], "uint16"), "liU2": ("sbuf", [128, 256], "uint16"),
+    "liF": ("sbuf", [128, 256], "float32"), "sel2": ("sbuf", [128, 256], "float16"), "NQ": ("sbuf", [128, 256], "float32"),
     "mn": ("sbuf", [128, 256], "float32"), "qR": ("sbuf", [128, 256], "float16"), "qF": ("sbuf", [128, 256], "float32"),
-    "qpm": ("sbuf", [128, 256], "float32"), "nR": ("sbuf", [128, 1280], "float32"), "wR": ("sbuf", [128, 256], "bfloat16"),
-    "fR": ("sbuf", [128, 192], "bfloat16"), "cum": ("sbuf", [128, 192], "bfloat16"), "sj": ("sbuf", [128, 192], "bfloat16"),
+    "qpm": ("sbuf", [128, 256], "float32"), "nR": ("sbuf", [128, 1280], "float32"),
+    "wR": ("sbuf", [128, 256], "bfloat16"),
+    "fR": ("sbuf", [128, 192], "bfloat16"), "cum": ("sbuf", [128, 192], "bfloat16"), "sj": ("sbuf", [128, 768], "bfloat16"),
     "one": ("sbuf", [128, 192], "bfloat16"), "hh": ("sbuf", [128, 192], "float32"),
     "s1": ("sbuf", [128, 256], "float32"), "sm": ("sbuf", [128, 256], "float32"), "sx": ("sbuf", [128, 256], "float32"),
-    "dmin": ("sbuf", [128, 256], "float32"), "dmax": ("sbuf", [128, 256], "float32"), "rs": ("sbuf", [128, 1024], "bfloat16"),
-    "qn": ("sbuf", [128, 256], "float32"),
-    "thr": ("sbuf", [128, 256], "float32"), "seed": ("sbuf", [128, 256], "float32"), "half": ("sbuf", [128, 256], "float32"),
-    "ii": ("sbuf", [128, 16], "int32"), "ij": ("sbuf", [128, 16], "int32"), "I16": ("sbuf", [128, 16], "float32"),
-    "tm": ("sbuf", [128, 16], "float32"), "pw": ("sbuf", [128, 4], "float32"),
-    "pm": ("sbuf", [128, 4], "float32"), "LL": ("sbuf", [128, 80], "float32"), "QP": ("sbuf", [128, 80], "float32"),
-    "jb": ("sbuf", [128, 4], "float32"), "T01": ("sbuf", [128, 16], "bfloat16"),
+    "dmin": ("sbuf", [128, 256], "bfloat16"), "dmax": ("sbuf", [128, 256], "bfloat16"), "rs": ("sbuf", [128, 1024], "bfloat16"),
+    "thr": ("sbuf", [128, 256], "bfloat16"), "seed": ("sbuf", [128, 256], "bfloat16"), "half": ("sbuf", [128, 256], "bfloat16"),
+    "w2": ("sbuf", [128, 256], "bfloat16"),
+    "ii": ("sbuf", [128, 16], "int32"), "ij": ("sbuf", [128, 16], "int32"),
+    "pw": ("sbuf", [128, 4], "float32"), "pm": ("sbuf", [128, 4], "float32"), "LL": ("sbuf", [128, 80], "float32"),
+    "QM": ("sbuf", [128, 80], "float16"), "HI": ("sbuf", [128, 5, 48], "float32"), "ov": ("sbuf", [128, 4], "float16"),
+    "jb": ("sbuf", [128, 4], "float32"), "acc": ("sbuf", [128, 4], "float32"),
     "SX": ("sbuf", [128, 4 * 72], "bfloat16"), "SA": ("sbuf", [128, 4 * 64], "float32"),
     "K0": ("psum", [128, 512], "float32"), "K1": ("psum", [128, 512], "float32"), "M": ("psum", [128, 512], "float32"),
     "SB0": ("psum", [128, 512], "float32"), "SB1": ("psum", [128, 512], "float32"), "D0": ("psum", [128, 512], "float32"),
     "D1": ("psum", [128, 512], "float32"), "PS": ("psum", [128, 512], "float32"),
 }
-for _n in ("k1U", "qU", "tnU", "cxU", "nvU", "srU"):
+for _n in ("B1", "B16", "Bv", "I1", "NI", "IX"):
+    SCRATCH[_n] = ("sbuf", [128, 128], "bfloat16")
+for _t in range(1, RO):
+    SCRATCH["Zr%d" % _t] = ("sbuf", [128, 144], "bfloat16")
+SCRATCH["cxU"] = ("sbuf", [128, 80], "uint16")
+for _n in ("k1U", "qU", "i2U", "srU", "pU"):
     SCRATCH[_n] = ("sbuf", [128, 16], "uint16")
-for _n in ("qL", "clg", "c1", "c2", "win", "far", "wf", "qp", "a2", "b0", "un", "n1", "n2", "f1", "f2", "f3", "acc"):
+SCRATCH["far"] = SCRATCH["AB"] = ("sbuf", [128, 32], "float32")
+for _n in ("qL", "nf", "cx", "LC", "I16", "tm"):
     SCRATCH[_n] = ("sbuf", [128, 16], "float32")
-for _n in ("uu", "lo", "hi", "d1", "d2"):
-    SCRATCH[_n] = ("sbuf", [128, 32], "float32")
-SCRATCH["tdU"] = ("sbuf", [128, 32], "uint16")
-NDMA = 56
+for _n in ("FF", "LO", "d1", "d2"):
+    SCRATCH[_n] = ("sbuf", [128, 48], "float32")
+SCRATCH["tdU"] = ("sbuf", [128, 48], "uint16")
+NDMA = 80
 SEMAPHORES = ["eV", "eS", "eP", "eG"] + ["d%d" % i for i in range(NDMA)] + ["ax%d" % i for i in range(4)] + ["aa%d" % i for i in range(4)] + ["lx"]
 
 BYTES = {"float32": 4, "int32": 4, "bfloat16": 2, "float16": 2, "uint16": 2}
-CG, CSC, CYC, PEC, LAT, DMAL, AHEAD = 1.55, 3.8, 0.83, 0.42, 100.0, 2200.0, 60.0
+COST = {"CG": 1.5, "CSC": 3.8, "CYC": 0.83, "PEC": 0.46, "LAT": 130.0, "OV": 0.0, "RL": 3500.0, "DMAL": 2300.0, "ZL": 10000.0, "GD": 900.0, "AL": 5000.0}
 
 
 def sl(a, b, s=None):
@@ -128,8 +146,10 @@ def wide(x):
 
 def build_ops():
     ops = []
+    step = [-1]
+    CG, CSC, CYC, PEC, DMAL = (COST[k] for k in ("CG", "CSC", "CYC", "PEC", "DMAL"))
 
-    def add(eng, cost, fn, reads, writes, kind="c", arr=None):
+    def add(eng, cost, fn, reads, writes, kind="c", arr=None, lat=None, n=1):
         rd = [y for x in reads for y in parts(x)]
         wr = []
         for x in writes:
@@ -138,25 +158,25 @@ def build_ops():
                 rd.append(x[2])
             else:
                 wr.append(x)
-        ops.append({"eng": eng, "cost": cost, "fn": fn, "r": [span(x) for x in rd], "w": [span(x) for x in wr], "kind": kind, "arr": arr})
-
-    def count(out, ins):
-        if out[0] == "ind":
-            return span(ins[0])[3]
-        return span(out)[3]
+        if lat is None:
+            lat = COST["LAT"] if kind == "c" else DMAL
+        if eng in "VS" and kind == "c":
+            cost += COST["OV"]
+        ops.append({"eng": eng, "cost": cost, "fn": fn, "r": [span(x) for x in rd], "w": [span(x) for x in wr], "kind": kind,
+                    "arr": arr, "lat": lat, "n": n, "step": step[0]})
 
     def vcost(out, ins, f=None):
-        n = count(out, ins)
         if out[0] == "ind":
-            return 50 + n * CSC * CYC
+            return 50 + span(ins[0])[3] * CSC * CYC
+        n = span(out)[3]
         if ins and ins[0][0] == "ind":
             return 50 + n * CG * CYC
         if f is None:
             f = 0.5 if all(wide(x) == 2 for x in [out] + ins) else 1.0
         return 30 + max(64, n * f) * CYC
 
-    def cp(out, a, arr=None):
-        add("V", vcost(out, [a]), lambda g, T: g.vector.tensor_copy(ap(T, out), ap(T, a)), [a], [out], arr=arr)
+    def cp(out, a):
+        add("V", vcost(out, [a]), lambda g, T: g.vector.tensor_copy(ap(T, out), ap(T, a)), [a], [out])
 
     def ms(out, v):
         add("V", vcost(out, []), lambda g, T: g.vector.memset(ap(T, out), v), [], [out])
@@ -178,7 +198,7 @@ def build_ops():
     def red(out, a):
         add("V", 90, lambda g, T: g.vector.tensor_reduce(ap(T, out), ap(T, a), AxisListType.X, ALU.add), [a], [out])
 
-    def act(out, a, func, bias=None, scale=None, acc=None, arr=None):
+    def act(out, a, func, bias=None, scale=None, acc=None, arr=None, more=0.0):
         n = span(out)[3]
         cost = 65 + n * CG * CYC if a[0] == "ind" else 30 + max(64, n) * CYC + (20 if acc else 0)
 
@@ -191,9 +211,9 @@ def build_ops():
             if acc is not None:
                 kw["accum_out"] = ap(T, acc)
             return g.scalar.activation(ap(T, out), ap(T, a), func, **kw)
-        add("S", cost, fn, [a, bias, scale], [out] + ([acc] if acc else []), arr=arr)
+        add("S", cost + more, fn, [a, bias, scale], [out] + ([acc] if acc else []), arr=arr)
 
-    def mm(items):
+    def mm(items, arr=None):
         cost = sum(max(64, span(o)[3]) * (4 if wide(r) == 4 else 1) for o, l, r, s0, s1 in items) * PEC + 60
 
         def fn(g, T):
@@ -201,16 +221,16 @@ def build_ops():
             for o, l, r, s0, s1 in items:
                 ins = g.tensor.matmul(ap(T, o), ap(T, l), ap(T, r), s0, s1)
             return ins
-        add("P", cost, fn, [x for it in items for x in it[1:3]], [it[0] for it in items])
+        add("P", cost, fn, [x for it in items for x in it[1:3]], [it[0] for it in items], arr=arr)
 
-    def dma(eng, out, a, cost=60.0):
-        if eng == "G":
-            fn = lambda g, T: g.dma_start(ap(T, out), ap(T, a))
-        elif eng == "S":
-            fn = lambda g, T: g.scalar.dma_start(ap(T, out), ap(T, a))
-        else:
-            fn = lambda g, T: g.sync.dma_start(ap(T, out), ap(T, a))
-        add(eng, cost, fn, [a], [out], kind="dma")
+    def dmas(eng, pairs, cost=60.0, arr=None, lat=None):
+        def fn(g, T):
+            qe = g if eng == "G" else g.scalar if eng == "S" else g.sync
+            return [qe.dma_start(ap(T, o), ap(T, a)) for o, a in pairs]
+        add(eng, cost * len(pairs), fn, [a for o, a in pairs], [o for o, a in pairs], kind="dma", arr=arr, lat=lat, n=len(pairs))
+
+    def dma(eng, out, a, cost=60.0, arr=None):
+        dmas(eng, [(out, a)], cost, arr)
 
     def iota(out, pat, base, cm):
         n = span(out)[3]
@@ -223,11 +243,21 @@ def build_ops():
     def asel(out, a, pat, op, fill, base, cm):
         add("G", 170 + 2 * span(out)[3] * CYC, lambda g, T: g.affine_select(ap(T, out), ap(T, a), pat, op, fill, base, cm), [a], [out])
 
-    def selr(r):
-        return C("Z", 15 - r, 143 - r)
+    def gcp(out, a):
+        asel(out, a, [[0, span(out)[3]]], ALU.is_equal, 0.0, 0, 0)
 
-    def tolist(out, src, c0, c1):
-        mm([(out, selr(r), C(src, 16 * c0 + r, 16 * c1, 16), r == 0, r == 15) for r in range(16)])
+    def fill(out, v):
+        iota(out, [[0, span(out)[3]]], v, 0)
+
+    def selr(r, z="Z"):
+        return C(z, 15 - r, 143 - r)
+
+    def tolist(out, src, c0, c1, z="Z", more=()):
+        it = [(out, selr(r, z), C(src, 16 * c0 + r, 16 * c1, 16), r == 0, r == 15) for r in range(16)]
+        mm(it[:1] + list(more) + it[1:])
+
+    def rows(name, j0, j1):
+        return A(name, sl(j0 // 64, j1 // 64), sl(0, 64))
 
     dma("Y", A("sti"), A("st"))
     dma("Y", A("nbi"), A("nb"))
@@ -236,262 +266,491 @@ def build_ops():
     dma("Y", A("dli"), A("dl"))
     dma("Y", C("Ct", 256, 256 + CN), A("cc"))
     dma("G", C("At", 256, 256 + CN), A("aa"), 300.0)
-    for t in range(1, RO):
-        dma("Y", C("X", XW * t, XW * t + S), C("xs", S * t, S * t + S))
+    for t in range(RO):
+        if t > 0:
+            dma("Y", C("X", XW * t, XW * t + S), C("xs", S * t, S * t + S))
+        if t < RO - 2:
+            dma("Y", C("XS", SW * t, SW * t + S), C("xs", S * t, S * t + S))
+            fill(C("XS", SW * t + S, SW * t + SW), int(VOID))
     dma("Y", A("Y"), A("ys"))
     iota(A("ii"), [[-1, 16]], 16, 1)
     ts(A("ij"), A("ii"), 15, ALU.bitwise_and)
     ts(A("I16"), A("ij"), 0.0, ALU.is_equal)
     ts(C("pm", 0, 1), C("ij", 0, 1), 1.0, ALU.mult)
-    cp(C("Id", 0, 16), A("I16"))
+    ts(C("Id", KB, KB + 16), A("I16"), 6144.0, ALU.mult, -OFF, ALU.add)
     w = 16
     while w < 512:
-        cp(C("Id", w, 2 * w), C("Id", 0, w))
+        cp(C("Id", KB + w, KB + 2 * w), C("Id", KB, KB + w))
         w *= 2
-    while w < IDW:
-        n = min(512, IDW - w)
-        dma("Y", C("Id", w, w + n), C("Id", 0, n))
-        w += n
+    pieces = [(KB + a, min(512, ZC - KB - a)) for a in range(512, ZC - KB, 512)] + [(0, 512), (512, NOV - 512)]
+    dmas("Y", [(C("Id", a, a + n), C("Id", KB, KB + n)) for a, n in pieces])
+    ms(C("Id", NOV, KB), -OFF)
+    ts(C("Id", ZC, IDW), A("I16"), OFF, ALU.mult, -OFF, ALU.add)
+    iota(A("NV"), [[3, KB]], 1 - 3 * NOV, 0)
     ms(A("B1"), 1.0)
     asel(A("B1"), A("B1"), [[-16, 8], [0, 16]], ALU.is_ge, 0.0, 0, 1)
     asel(A("B1"), A("B1"), [[16, 8], [0, 16]], ALU.is_ge, 0.0, 15, -1)
     ms(A("Z"), 0.0)
     ts(C("Z", 15, 143, 16), C("B1", 0, 128, 16), 16.0, ALU.mult)
+    act(A("Zw"), A("Z"), ACT.Identity, scale=-8.0)
     ms(A("I1"), 1.0)
     asel(A("I1"), A("I1"), [[-1, 128]], ALU.is_equal, 0.0, 0, 1)
-    ms(A("NE", p=sl(0, 64)), -1.0)
+    fill(A("NE", p=sl(0, 64)), -1)
     asel(A("NE", p=sl(0, 64)), A("NE", p=sl(0, 64)), [[-1, 64], [0, 16]], ALU.is_equal, 0.0, 0, 1)
-    ts(A("B16"), A("B1"), 65536.0, ALU.mult)
-    ts(A("Iy"), A("I1"), 0.25, ALU.mult)
-    ts(A("Ip"), A("I1"), -0.25, ALU.mult)
-    cp(A("If"), A("I1"))
+    for name, src, f in (("B16", "B1", 65536.0), ("Bv", "B1", 1.0 / 256), ("NI", "I1", -1.0), ("IX", "I1", 16.0), ("If", "I1", 1.0)):
+        act(A(name), A(src), ACT.Identity, scale=f)
     ms(A("dmin"), -1.0)
     ms(C("dmin", 0, 256, 16), BIG)
-    ms(A("dmax"), 1.0)
-    ms(C("dmax", 0, 256, 16), -BIG)
-    ms(A("rs"), 1.0)
-    ms(C("rs", 0, 1024, 16), 0.0)
-    ms(A("seed"), 0.0)
-    ms(C("seed", 0, 256, 16), 2.5 * 32768.0)
-    ms(A("half"), 0.5)
-    scan(A("thr"), A("half"), A("seed"), 0.0, ALU.mult, ALU.max)
-    tt(A("tm"), C("thr", 0, 16), A("I16"), ALU.mult)
-    red(C("pw", 1, 2), A("tm"))
-    ts(C("pw", 0, 1), C("pw", 1, 2), 0.4, ALU.mult, 8388608.0, ALU.add)
-    ts(C("pw", 2, 3), C("pw", 0, 1), -8388608.0, ALU.add)
-    iota(A("QP"), [[16, 80]], 0, 0)
-    ts(A("LL"), A("QP"), C("pm", 0, 1), ALU.add)
-    ts(A("QP"), A("LL"), float(Q0), ALU.add)
-    ts(A("jb"), C("LL", 0, 4), 0.5, ALU.add)
-    ms(A("qpm"), 0.0)
-    ms(A("T01"), 1.0)
-    ms(C("T01", 0, 1), 0.0)
-    ms(A("one"), 1.0)
-    ms(A("SX"), 0.0)
-    ms(C("At", 0, 256), 0.0)
-    ms(C("At", 256 + CN + S, 256 + CN + LN), 0.0)
-    ms(C("Ct", 256 + CN + S, 256 + CN + LN), 0.0)
-    ms(C("X", S, XW), 0.0)
-    ms(C("NB", 256 + Q0 + S, 256 + Q0 + LN), 0.0)
-    ms(C("DL", Q0 + S, Q0 + LN), 0.0)
-    for name in ("uu", "lo", "hi"):
-        ms(A(name), 0.0)
+    act(A("dmax"), A("dmin"), ACT.Identity, scale=-1.0)
+    if "V" in "".join(CFG["sum"]):
+        act(C("rs", 0, 256), A("dmin"), ACT.Relu, scale=-1.0)
+        dmas("Y", [(C("rs", a, a + 256), C("rs", 0, 256)) for a in (256, 512, 768)])
+    iota(A("w2"), [[0, 16], [-1, 16]], 15, 0)
+    act(A("thr"), A("w2"), ACT.Exp, bias=math.log(2.5), scale=math.log(2.0), more=1300.0)
+    act(C("half", 0, 1), C("pm", 0, 1), ACT.Exp, bias=15 * math.log(2.0), scale=-math.log(2.0))
+    act(C("pw", 0, 1), C("half", 0, 1), ACT.Copy)
+    iota(A("HI", sl(0, 5), sl(32, 48)), [[256, 5], [16, 16]], Q0, 0)
+    for a in (0, 16):
+        act(A("HI", sl(0, 5), sl(a, a + 16)), A("HI", sl(0, 5), sl(32, 48)), ACT.Identity, bias=C("pm", 0, 1))
+    ts(A("QM"), A("HI", sl(0, 5), sl(0, 16)), -OFF, ALU.add)
+    act(A("LC"), A("HI", 0, sl(0, 16)), ACT.Identity, bias=-16.0 * (Q0 + 16 * OFF), scale=16.0)
+    act(A("jb"), A("HI", 0, sl(0, 4)), ACT.Identity, bias=0.5 - Q0)
+    for t in range(RO - 1):
+        iota(C("nR", LN * t, LN * t + LN), [[1, LN]], Q0 + LN * t, 0)
+    fill(A("qpm"), 0)
+    fill(A("one"), 1)
+    dma("Y", C("At", 0, 256), A("qpm"))
+    dmas("Y", [(C("At", 256 + CN + S, 256 + CN + LN), C("qpm", 0, H)), (C("qF", S, LN), C("qpm", 0, H)), (C("DL", Q0 + S, Q0 + LN), C("qpm", 0, H)),
+               (A("FF"), C("qpm", 0, 48)), (A("LO"), C("qpm", 0, 48)), (A("far"), C("qpm", 0, 32))])
+    fill(C("X", S, XW), 0)
+    dmas("Y", [(C("Ct", 256 + CN + S, 256 + CN + LN), C("X", S, LN))] + [(C("SX", 72 * t + 64, 72 * t + 72), C("X", S, S + 8)) for t in range(4)])
+    for t in range(1, RO):
+        act(A("Zr%d" % t), A("Z"), ACT.Identity, scale=C("I16", 7 + t, 8 + t))
     cp(A("qU"), A("sti"))
-    cp(C("clg", 0, 4), C("sti", 12, 16))
-    cp(C("NB", 256, 256 + Q0), A("nbi"))
-    ts(C("DL", 0, Q0), A("dli"), 256.0, ALU.add)
+    cp(C("qL", 12, 16), C("sti", 12, 16))
+    cp(C("NB", 0, Q0), A("nbi"))
+    ts(C("DL", 0, Q0), A("dli"), 256.0 - OFF, ALU.add)
 
     def xrep(t):
-        nv = max(MODE[(1, t)].rfind("V"), MODE[(2, t)].rfind("V")) + 1
-        xr = "xr%d" % (t % 2)
+        nv = 6
+        xr = "xr%d" % (t % 3)
         for k in range(16):
             o, a = C(xr, k, 512 * nv, 16), C("X", XW * t, XW * t + 32 * nv)
-            if t == 0:
+            if t == 0 and CFG["x0"][k % len(CFG["x0"])] == "V":
                 cp(o, a)
+            elif t == 0 and CFG["x0"][k % len(CFG["x0"])] == "S":
+                act(o, a, ACT.Copy)
             else:
-                asel(o, a, [[0, 32 * nv]], ALU.is_equal, 0.0, 0, 0)
+                gcp(o, a)
 
     flip = [0]
 
     def quarter(stage, t, q, win, lst, key):
         abn = "ab%d" % stage
-        md = MODE[(stage, t)][2 * q:2 * q + 2]
-        for b0, b1 in ([(0, 2)] if md[0] == md[1] else [(0, 1), (1, 2)]):
+        xr = "xr%d" % (t % 3)
+        ag = "ag%d" % stage
+        md = CFG["m%d" % stage][t][2 * q:2 * q + 2]
+        for b0, b1 in ([(0, 2)] if md[0] == md[1] and md[0] in CFG["merge"] else [(0, 1), (1, 2)]):
             off = C(lst, 64 * q + 32 * b0, 64 * q + 32 * b1)
             j0, j1 = 1024 * q + 512 * b0, 1024 * q + 512 * b1
             if md[b0] == "V":
-                tt(C("vv", j0, j1), IND(win, off), C("xr%d" % (t % 2), j0, j1), ALU.subtract)
-                act(A(abn, sl(j0 // 256, j1 // 256), sl(0, 256)), C("vv", j0, j1), ACT.Abs)
+                tt(C(ag, j0, j1), IND(win, off), C(xr, j0, j1), ALU.subtract)
+                act(rows(abn, j0, j1), C(ag, j0, j1), ACT.Abs)
+            elif md[b0] == "D":
+                w = CFG["dw"]
+                for j in range(j0, j1, w):
+                    act(C(ag, j, j + w), IND(win, C(lst, j // 16, (j + w) // 16)), ACT.Identity, scale=-1.0)
+                o, a = C(ag, j0, j1), C(xr, j0, j1)
+                add("G", COST["GD"], lambda g, T, o=o, a=a: [g.dma_start(ap(T, o), ap(T, a), accum_op=ALU.add)], [a, o], [o], kind="dma", lat=COST["AL"])
+                for j in range(j0, j1, CFG["da"]):
+                    act(rows(abn, j, j + CFG["da"]), C(ag, j, j + CFG["da"]), ACT.Abs)
             else:
-                act(C("ag", j0, j1), IND(win, off), ACT.Copy)
+                act(C(ag, j0, j1), IND(win, off), ACT.Copy)
                 for b in range(b0, b1):
                     bank = A("SB%d" % flip[0])
                     flip[0] ^= 1
-                    mm([(bank, A("I1"), C("ag", 1024 * q + 512 * b, 1024 * q + 512 * b + 512), True, False),
-                        (bank, A("xT", sl(128 * q, 128 * q + 128), p=sl(0, 64)), A("NE", sl(512 * b, 512 * b + 512), p=sl(0, 64)), False, True)])
-                    act(A(abn, sl(4 * q + 2 * b, 4 * q + 2 * b + 2), sl(0, 256)), bank, ACT.Abs)
+                    j = 1024 * q + 512 * b
+                    if q == 3 or md[b] == "T":
+                        sub = (bank, A("xT", sl(128 * q, 128 * q + 128), p=sl(0, 64)), A("NE", sl(512 * b, 512 * b + 512), p=sl(0, 64)), False, True)
+                    else:
+                        sub = (bank, A("NI"), C(xr, j, j + 512), False, True)
+                    mm([(bank, A("I1"), C(ag, j, j + 512), True, False), sub])
+                    act(rows(abn, j, j + 512), bank, ACT.Abs)
         if stage == 1 or t < RO - 1:
-            mm([(key, selr(r), A(abn, sl(4 * q, 4 * q + 4), sl(16 * r, 16 * r + 16)), r == 0, r == 15) for r in range(16)])
+            mm([(key, selr(r), A(abn, sl(16 * q + r // 4, 16 * q + 16, 4), sl(16 * (r % 4), 16 * (r % 4) + 16)), r == 0, r == 15) for r in range(16)])
 
     xrep(0)
+    exp_seen = [True]
     for t in range(RO):
+        step[0] = t
         nc = 16 if 0 < t < RO - 1 else 12
         n, nq = 16 * nc, nc // 4
         qn, cn = Q0 + LN * t, CN + LN * t
         x0 = XW * t
-        liU = "liU%d" % (t % 2)
+        liU = "liU%d" % (t % 3)
         last = t == RO - 1
-        halves = [(0, 8), (8, nc)]
-        gin = ("ax", t - 1)
+        hc = CFG["half"][t]
+        halves = [(0, hc), (hc, nc)] if hc < nc else [(0, nc)]
+        gin = ("ax", t - 1) if t > 0 else None
+        L = lambda name, a=0: C(name, a, a + nc)
         for q in range(nq):
-            if "S" in MODE[(1, t)][2 * q:2 * q + 2] + MODE[(2, t)][2 * q:2 * q + 2]:
-                o = A("PS", sl(256 + 128 * (q % 2), 384 + 128 * (q % 2)), p=sl(0, 64))
-                mm([(o, C("X", x0 + 64 * q, x0 + 64 * q + 64), A("I1"), True, True)])
-                ops[-1]["arr"] = gin if q == 3 else None
+            if q == 3 or "T" in CFG["m1"][t][2 * q:2 * q + 2] + CFG["m2"][t][2 * q:2 * q + 2]:
+                o = A("M", sl(256 + 128 * (q % 2), 384 + 128 * (q % 2)), p=sl(0, 64))
+                mm([(o, C("X", x0 + 64 * q, x0 + 64 * q + 64), A("I1"), True, True)], arr=gin if q == 3 else None)
                 act(A("xT", sl(128 * q, 128 * q + 128), p=sl(0, 64)), o, ACT.Copy)
-        nwin = A("nbi") if t == 0 else C("NB", 256, 256 + qn - LN)
-        for h, (c0, c1) in enumerate(halves):
-            cp(C("caU", 16 * c0, 16 * c1), IND(nwin, C("qU", c0, c1)))
         if t == 0:
-            cp(C("caF", 0, n), IND(nwin, C("qU", 0, nc)))
+            cp(C("caU", 0, n), IND(A("nbi"), C("qU", 0, nc)))
+            cp(C("caF", 0, n), IND(A("nbi"), C("qU", 0, nc)))
+        elif not CFG["early"]:
+            for c0, c1 in halves:
+                cp(C("caU", 16 * c0, 16 * c1), IND(C("NB", 0, qn - LN), C("qU", c0, c1)))
+            act(C("caS", 0, n), IND(C("NB", 0, qn - LN), C("qU", 0, nc)), ACT.Copy)
         else:
-            act(C("caF", 0, n), IND(nwin, C("qU", 0, nc)), ACT.Copy)
+            (gcp if CFG["caG"] else cp)(C("caU", 0, S), C("NQ", 0, S))
+            cp(C("caF", 0, n), IND(C("NB", 0, qn - LN), C("qU", 0, nc)))
+            if nc == 16:
+                cp(C("caU", S, n), IND(C("NB", 0, qn - LN), C("qU", 12, 16)))
+            tolist(C("K1", 288, 300), "caF", 0, 12, "Zr%d" % t)
+            ts(C("pU", 0, 12), C("K1", 288, 300), 0.0625, ALU.mult)
+        if nc == 16:
+            tt(A("ov"), C("qL", 12, 16), C("X", x0 + 256, x0 + 260), ALU.mult, arr=gin)
         if t + 1 < RO:
             xrep(t + 1)
+        for q in range(nq):
+            quarter(1, t, q, C("Kt", 0, max(Q0, qn - LN) if CFG["early"] and q < 3 else qn), "caU", C("K0", 64 * q, 64 * q + 64))
         for h, (c0, c1) in enumerate(halves):
-            kb = "K%d" % h
-            m = 16 * (c1 - c0)
-            for q in range(c0 // 4, c1 // 4):
-                quarter(1, t, q, C("Kt", 0, qn), "caU", C(kb, 64 * q - 16 * c0, 64 * q - 16 * c0 + 64))
-            scan(C("s1", 16 * c0, 16 * c1), C("dmin", 0, m), C(kb, 0, m), 0.0, ALU.add, ALU.min)
-            ts(C("k1U", c0, c1), C("s1", 16 * c0 + 15, 16 * c1, 16), 15.0, ALU.add)
-            tt(C("sel", 16 * c0, 16 * c1), IND(A("Id"), C("k1U", c0, c1)), C("caF", 16 * c0, 16 * c1), ALU.mult)
-            ql = C(kb, 384, 384 + c1 - c0) if h == 0 else C("K0", 392, 392 + c1 - c0)
-            tolist(ql, "sel", c0, c1)
-            ts(C("qU", c0, c1), ql, 0.0625, ALU.mult)
-            ts(C(liU, 16 * c0, 16 * c1), IND(C("DL", 0, qn), C("qU", c0, c1)), -256.0, ALU.add)
+            a0, a1 = 16 * c0, 16 * c1
+            if t > 0 and CFG["early"] and c0 < 12:
+                c2 = min(c1, 12)
+                tt(C("vp", a0, 16 * c2), IND(C("Kt", 0, qn), C("pU", c0, c2)), C("X", x0 + a0, x0 + 16 * c2), ALU.subtract)
+                act(C("abp", a0, 16 * c2), C("vp", a0, 16 * c2), ACT.Abs)
+                tolist(C("K0", a0 + 7 + t, 16 * c2, 16), "abp", c0, c2)
+            scan(C("s1", a0, a1), C("dmin", a0, a1), C("K0", a0, a1), 0.0, ALU.add, ALU.min)
+            ts(C("k1U", c0, c1), C("s1", a0 + 15, a1, 16), 15.0 + KB, ALU.add, float(ZC), ALU.min)
+            tt(C("sel", a0, a1), IND(A("Id"), C("k1U", c0, c1)), C("caF" if t == 0 or CFG["early"] else "caS", a0, a1), ALU.min)
+            ql = C("K1", 256 + c0, 256 + c1)
+            tolist(ql, "sel", c0, c1, more=[(C("K1", 268, 272), A("IX"), A("ov"), False, False)] if c1 == 16 else [])
+            ts(C("qU", c0, c1), ql, 0.0625, ALU.mult, 15 * OFF, ALU.add)
+            ts(C(liU, a0, a1), IND(C("DL", 0, qn), C("qU", c0, c1)), OFF - 256.0, ALU.add)
             if not last:
-                act(C("qL", c0, c1), ql, ACT.Identity, scale=0.0625)
-                mm([(C(kb, 128, 128 + m), A("B1"), C("sel", 16 * c0, 16 * c1), True, True)])
-                act(C("qF", 16 * c0, 16 * c1), C(kb, 128, 128 + m), ACT.Copy)
-                asel(C("qR", 16 * c0, 16 * c1), C("qF", 16 * c0, 16 * c1), [[0, m]], ALU.is_equal, 0.0, 0, 0)
+                act(C("qL", c0, c1), ql, ACT.Identity, bias=15 * OFF, scale=0.0625)
+                mm([(C("K1", a0, a1), A("B1"), C("sel", a0, a1), True, True)])
+                act(C("qF", a0, a1), C("K1", a0, a1), ACT.Identity, bias=15 * OFF)
+                gcp(C("qR", a0, a1), C("qF", a0, a1))
         for q in range(nq):
             quarter(2, t, q, C("Ct", 256, 256 + cn), liU, C("M", 64 * q, 64 * q + 64))
         if not last:
-            dma("Y", C("Kt", qn, qn + LN), C("X", x0, x0 + LN))
-            ops[-1]["arr"] = gin if t > 0 else None
-            dma("Y", C("Ct", 0, LN), C("X", x0, x0 + LN))
-            ops[-1]["arr"] = gin if t > 0 else None
+            dma("Y", C("Kt", qn, qn + LN), C("X", x0, x0 + LN), arr=gin)
+            dma("Y", C("Ct", 0, LN), C("X", x0, x0 + LN), arr=gin)
             act(C("liF", 0, n), IND(C("DL", 0, qn), C("qU", 0, nc)), ACT.Copy)
-            act(C("liC", 0, n), C("liF", 0, n), ACT.Identity, bias=-2048.0)
-            nbq = C("NB", 256 + qn, 256 + qn + n)
-            act(nbq, IND(C("NB", 256, 256 + qn), C("qU", 0, nc)), ACT.Copy)
-            iota(C("nR", LN * t, LN * t + LN), [[1, LN]], 256 + cn, 0)
-            iota(A("qn"), [[1, LN]], qn, 0)
+            for c0, c1 in ((0, 12), (12, 16)) if nc == 16 and hc < nc and CFG["early"] else ((0, 16),):
+                act(C("NQ", 16 * c0, 16 * c1), IND(C("NB", 0, qn), C("qU", c0, c1)), ACT.Copy)
             if t > 0:
                 dma("Y", A("qpm", sl(0, LN), p=sl(7 + t, 128, 16)), A("At", sl(0, LN), p=sl(7 + t, 128, 16)))
-            dma("Y", A("qpm", sl(0, LN), p=sl(8 + t, 128, 16)), A("qn", sl(0, LN), p=sl(8 + t, 128, 16)))
-            for c in range(nc):
-                ts(A("Eb", c, sl(0, n - 16 * c)), C("qR", 16 * c, n), C("qL", c, c + 1), ALU.is_equal, C("pw", 2, 3), ALU.mult)
-            O = C("K1", 256, 256 + n)
-            mm([(O, A("B1"), A("Eb", sl(0, nc), sl(0, 16)), True, False)] +
-               [(C("K1", 256 + 16 * (c + 1), 256 + n), A("B16"), A("Eb", c, sl(16, n - 16 * c)), False, c == nc - 2) for c in range(nc - 1)])
-            tt(C("wR", 0, n), O, C("thr", 0, n), ALU.is_lt)
-            tolist(C("K0", 416, 416 + nc), "wR", 0, nc)
-            L = lambda name: C(name, 0, nc)
-            act(L("win"), C("K0", 416, 416 + nc), ACT.Identity, scale=16.0)
-            live = C("X", x0 + 256, x0 + 260)
-            if nc == 16:
-                tt(C("win", 12, 16), C("win", 12, 16), live, ALU.mult, arr=gin)
-                tt(C("c1", 0, 4), C("qL", 12, 16), C("clg", 0, 4), ALU.subtract)
-                tt(C("c2", 0, 4), C("c1", 0, 4), live, ALU.mult, arr=gin)
-                tt(C("clg", 0, 4), C("clg", 0, 4), C("c2", 0, 4), ALU.add)
-                cp(C("qU", 12, 16), C("clg", 0, 4))
-            qpl = C("QP", 16 * t, 16 * t + nc)
+            dma("Y", A("qpm", sl(0, LN), p=sl(8 + t, 128, 16)), A("nR", sl(LN * t, LN * t + LN), p=sl(8 + t, 128, 16)))
+            cuts = [(0, 12), (12, 16)] if CFG["apart"] and 0 < t < RO - 2 else [(0, nc)]
+            for c0, c1 in cuts:
+                a0, a1 = 16 * c0, 16 * c1
+                eb = "Eg" if c0 else "Eb"
+                part = lambda c, a: A(eb, c, sl(a - max(a0, 16 * c), a1 - max(a0, 16 * c)))
+                for c in range(c1):
+                    a = max(a0, 16 * c)
+                    ts(part(c, a), C("qR", a, a1), C("qL", c, c + 1), ALU.is_equal, C("pw", 0, 1), ALU.mult)
+                O = C("D1", a0, a1)
+                mm([(O, A("NI"), C("thr", a0, a1), True, False)] +
+                   ([(C("D1", S, LN), A("Bv"), C("X", x0 + S, x0 + LN), False, False)] if c1 == 16 else []) +
+                   [(O, A("B1"), A(eb, sl(c0, c1), sl(0, 16)), False, False)] +
+                   [(C("D1", max(a0, 16 * c + 16), a1), A("B16"), part(c, max(a0, 16 * c + 16)), False, c == c1 - 2) for c in range(c1 - 1)],
+                   arr=gin if c1 == 16 else None)
+                act(C("wR", a0, a1), O, ACT.Sign, scale=-1.0)
+            W = C("D1", 256, 256 + nc)
+            tolist(W, "wR", 0, nc, "Zw", more=[(W, A("I1"), C("QM", 16 * t, 16 * t + nc), False, False)])
+            tt(L("LO"), W, L("qL"), ALU.max)
             act(L("far"), C("s1", 15, n, 16), ACT.Identity, bias=-8965000.0, scale=1.0e4)
-            act(L("qp"), L("qL"), ACT.Identity, bias=256.0)
-            tt(L("wf"), L("far"), L("qp"), ALU.min)
-            tt(L("a2"), L("wf"), L("win"), ALU.min)
-            tt(L("b0"), qpl, L("win"), ALU.subtract)
-            tt(L("lo"), L("b0"), L("qL"), ALU.max)
-            tt(L("hi"), L("far"), qpl, ALU.min)
-            scan(C("sm", 0, n), C("dmin", 0, n), C("M", 0, n), 0.0, ALU.add, ALU.min)
-            kmin, kmax = C("sm", 15, n, 16), C("sx", 15, n, 16)
-            ts(L("uu"), kmin, -640.5, ALU.add, 1.0e4, ALU.mult)
-            tt(L("n1"), L("uu"), L("a2"), ALU.min)
-            tt(L("n2"), L("n1"), L("LL"), ALU.max)
-            cp(L("tnU"), L("n2"))
-            tt(IND(C("NB", 0, 256 + qn), L("tnU")), nbq, C("qpm", 0, n), ALU.max)
-            dma("Y", A("NB", sl(256 + qn, 256 + qn + n), p=sl(t, 128, 16)), A("qF", sl(0, n), p=sl(t, 128, 16)))
+            if CFG["flat"]:
+                act(L("far", 16), C("s1", 15, n, 16), ACT.Identity, bias=8965000.0, scale=-1.0e4)
+                tt(A("AB"), A("far"), A("HI", t, sl(0, 32)), ALU.min)
+                tt(L("nf"), L("AB", 16), L("qL"), ALU.max)
+                dma("Y", A("HI", t, sl(0, 16)), C("AB", 0, 16))
+                tt(L("LO", 16), W, L("nf"), ALU.max)
+            elif CFG["tiny"][0] == "S":
+                act(L("LO", 16), L("LO"), ACT.Copy)
+            else:
+                tt(L("LO", 16), W, L("qL"), ALU.max)
+            for c0, c1 in cuts:
+                scan(C("sm", 16 * c0, 16 * c1), C("dmin", 16 * c0, 16 * c1), C("M", 16 * c0, 16 * c1), 0.0, ALU.add, ALU.min)
+                ts(C("i2U", c0, c1), C("sm", 16 * c0 + 15, 16 * c1, 16), 15.0, ALU.add, float(NOV), ALU.min)
             scan(C("sx", 0, n), C("dmax", 0, n), C("M", 0, n), 0.0, ALU.add, ALU.max)
-            act(C("uu", 16, 16 + nc), kmin, ACT.Identity, bias=-6405000.0, scale=1.0e4)
-            ts(C("lo", 16, 16 + nc), kmin, 15.0, ALU.add, 655.0, ALU.min)
-            act(C("hi", 16, 16 + nc), kmax, ACT.Identity, bias=4511.0, scale=-1.0)
-            tt(A("d1"), A("uu"), A("hi"), ALU.min)
-            tt(A("d2"), A("d1"), A("lo"), ALU.max)
+            kmin, kmax = C("sm", 15, n, 16), C("sx", 15, n, 16)
+            ts(L("FF", 32), kmin, -640.5, ALU.add, 1.0e4, ALU.mult)
+            if CFG["flat"]:
+                act(L("FF"), kmin, ACT.Identity, bias=-6405000.0, scale=1.0e4) if CFG["tiny"][1] == "S" else ts(L("FF"), kmin, -640.5, ALU.add, 1.0e4, ALU.mult)
+                ts(L("FF", 16), kmin, -640.5, ALU.add, -1.0e4, ALU.mult)
+            else:
+                tt(L("FF"), L("FF", 32), L("far"), ALU.min)
+                if CFG["tiny"][1] == "S":
+                    act(L("FF", 16), L("FF"), ACT.Identity, scale=-1.0)
+                else:
+                    ts(L("FF", 16), L("FF"), -1.0, ALU.mult)
+            ts(L("LO", 32), kmin, 15.0, ALU.add, float(NOV), ALU.min)
+            if CFG["tiny"][2] == "S":
+                act(A("HI", t, sl(32, 32 + nc)), kmax, ACT.Identity, bias=ZC - 1.0, scale=-1.0)
+            else:
+                ts(A("HI", t, sl(32, 32 + nc)), kmax, -1.0, ALU.mult, ZC - 1.0, ALU.add)
+            tt(A("d1"), A("FF"), A("HI", t, sl(0, 48)), ALU.min)
+            tt(A("d2"), A("d1"), A("LO"), ALU.max)
             cp(A("tdU"), A("d2"))
-            ixU = C("tdU", 16, 16 + nc)
-            tt(C("mn", 0, n), IND(A("Id"), ixU), C("nR", LN * t, LN * t + n), ALU.mult)
-            tt(IND(C("DL", 0, qn + LN), L("tdU")), C("liF", 0, n), C("mn", 0, n), ALU.max)
-            tt(C("sel2", 0, n), IND(A("Id"), ixU), C("liC", 0, n), ALU.mult)
-            tolist(C("K0", 400, 400 + nc), "sel2", 0, nc)
-            act(L("un"), L("uu"), ACT.Identity, scale=-1.0)
-            act(L("f1"), C("K0", 400, 400 + nc), ACT.Identity, bias=2048.0, scale=0.0625)
-            tt(L("f2"), L("f1"), L("un"), ALU.min)
-            tt(L("f3"), L("f2"), L("LL"), ALU.max)
-            cp(L("cxU"), L("f3"))
-            act(C("Ct", 256 + cn, 256 + cn + n), IND(C("Ct", 0, 256 + cn), L("cxU")), ACT.Copy)
+            ops[-1]["due"] = CFG["due"][0] + CFG["period"] * (RO - 2 - t)
+            tt(IND(C("NB", 0, qn + LN), L("tdU", 16)), C("NQ", 0, n), C("qpm", 0, n), ALU.max)
             if t < RO - 2:
-                ts(C("nvU", 0, 12), C("sm", 15, S, 16), 641.0, ALU.is_ge)
-                tt(A("fR"), IND(A("T01"), C("nvU", 0, 12)), C("wR", 0, S), ALU.mult)
+                dma("Y", C("NB", qn, qn + LN), A("NQ"))
+                dma("Y", A("NB", sl(qn, qn + LN), p=sl(t, 128, 16)), A("qF", sl(0, LN), p=sl(t, 128, 16)))
+            tt(C("mn", 0, n), IND(A("Id"), L("tdU", 32)), C("nR", LN * t, LN * t + n), ALU.min)
+            tt(IND(C("DL", 0, qn + LN), L("tdU")), C("liF", 0, n), C("mn", 0, n), ALU.max)
+            tt(C("sel2", 0, n), IND(A("Id"), L("i2U")), C("liF", 0, n), ALU.min)
+            tolist(C("K1", 272, 272 + nc), "sel2", 0, nc)
+            tt(L("cx"), C("K1", 272, 272 + nc), L("LC"), ALU.max)
+            ts(L("cxU", 16 * t), L("cx"), 0.0625, ALU.mult, 16 * OFF, ALU.add)
+            act(C("Ct", 256 + cn, 256 + cn + n), IND(C("Ct", 0, 256 + cn), L("cxU", 16 * t)), ACT.Copy)
+            if t < RO - 2:
+                tt(A("fR"), IND(A("NV"), C("i2U", 0, 12)), C("wR", 0, S), ALU.is_equal)
                 scan(A("cum"), A("one"), A("fR"), 0.0, ALU.mult, ALU.add)
                 for c in range(4):
-                    act(A("sj"), A("cum"), ACT.Sign, bias=C("jb", c, c + 1), scale=-1.0, acc=C("acc", c, c + 1))
-                ts(C("srU", 0, 4), C("acc", 0, 4), 0.5, ALU.mult, 96.0, ALU.add)
-                act(C("SX", 72 * t + 64, 72 * t + 68), C("acc", 0, 4), ACT.Sign, bias=192.0, scale=-1.0)
-                act(C("SX", 72 * t, 72 * t + 64), IND(C("X", x0, x0 + S + 16), C("srU", 0, 4)), ACT.Copy, arr=gin if t > 0 else None)
+                    act(C("sj", S * c, S * c + S), A("cum"), ACT.Sign, bias=C("jb", c, c + 1), scale=-1.0, acc=C("acc", c, c + 1))
+                ts(C("srU", 4 * t, 4 * t + 4), A("acc"), 0.5, ALU.mult, 96.0, ALU.add)
+                act(C("SX", 72 * t + 64, 72 * t + 68), A("acc"), ACT.Relu, bias=-191.0)
+                act(C("SX", 72 * t, 72 * t + 64), IND(C("XS", SW * t, SW * t + SW), C("srU", 4 * t, 4 * t + 4)), ACT.Copy)
                 add("G", 300, ("ax", t, C("X", x0 + XW + S, x0 + XW + S + 72), C("SX", 72 * t, 72 * t + 72)), [C("SX", 72 * t, 72 * t + 72)], [], kind="rem")
+        wr = "wr%d" % (t % 2)
+        ny = CFG["ny"][t]
+        if ny < 6:
+            w = S - 32 * ny
+            mm([(C("D0", 0, w), selr(r), rows("ab2", 512 * ny + w * r, 512 * ny + w * r + w), r == 0, r == 15) for r in range(16)])
+            act(C("wc", 0, w), C("D0", 0, w), ACT.Exp, scale=-1.0 / 1024, more=0.0 if exp_seen[0] else 1300.0)
+            exp_seen[0] = True
+            src = C("wc", 0, w)
+            if CFG["dram"]:
+                src = C("Wd", 0, 16 * w)
+                dma("Y", src, C("wc", 0, w))
+            dmas("Y", [(A(wr, sl(512 * ny, 3072), p=sl(f, 128, 16)), src) for f in range(16)], lat=COST["ZL"] * w / S)
         for b in range(6):
-            bank = A("D%d" % (b % 2))
-            mm([(bank, A("B1"), A("ab2", sl(2 * b, 2 * b + 2), sl(0, 256)), True, True)])
-            act(C("wr", 512 * b, 512 * b + 512), bank, ACT.Exp, scale=-0.015625)
-            tt(C("pr", 512 * b, 512 * b + 512), IND(C("At", 256, 256 + cn), C(liU, 32 * b, 32 * b + 32)), C("wr", 512 * b, 512 * b + 512), ALU.mult,
-               arr=("aa", t - 2) if t >= 2 else None)
+            if b < ny:
+                bank = A("D%d" % (b % 2))
+                mm([(bank, A("B1"), rows("ab2", 512 * b, 512 * b + 512), True, True)])
+                act(C(wr, 512 * b, 512 * b + 512), bank, ACT.Exp, scale=-0.015625, more=0.0 if exp_seen[0] else 1300.0)
+                exp_seen[0] = True
+            for j in range(512 * b, 512 * b + 512, 512) if CFG["pw"][t] == 512 else [512 * b - 512] * (b % 2):
+                j1 = j + CFG["pw"][t]
+                tt(C("pr", j, j1), IND(C("At", 256, 256 + cn), C(liU, j // 16, j1 // 16)), C(wr, j, j1), ALU.mult, arr=("aa", t - 2) if t >= 2 else None)
             if b % 2 == 1:
                 q = b // 2
-                pq = C("Pt", S * t + 64 * q, S * t + 64 * q + 64)
-                if SUM[t][q] == "V":
-                    scan(C("so", 1024 * q, 1024 * q + 1024), A("rs"), C("pr", 1024 * q, 1024 * q + 1024), 0.0, ALU.mult, ALU.add)
-                    if last:
-                        act(pq, C("so", 1024 * q + 15, 1024 * q + 1024, 16), ACT.Copy)
-                    else:
-                        asel(pq, C("so", 1024 * q + 15, 1024 * q + 1024, 16), [[0, 64]], ALU.is_equal, 0.0, 0, 0)
+                o = C("PS", 64 * q, 64 + 64 * q)
+                y = [] if last else [(o, A("NI"), C("Y", S * t + 64 * q, S * t + 64 * q + 64), True, False)]
+                if CFG["sum"][t][q] == "V":
+                    scan(A("so"), A("rs"), C("pr", 1024 * q, 1024 * q + 1024), 0.0, ALU.mult, ALU.add)
+                    mm(y + [(o, A("If"), C("so", 15, 1024, 16), last, True)])
+                    ops[-1]["chain"] = "PS"
                 else:
-                    o = C("PS", 64 * q, 64 + 64 * q)
-                    for k0 in range(0, 16, 4):
-                        mm([(o, A("If"), C("pr", 1024 * q + k, 1024 * q + 1024, 16), k == 0, k == 15) for k in range(k0, k0 + 4)])
-                        ops[-1]["open"] = (k0 > 0, k0 < 12)
-                    act(pq, o, ACT.Copy)
-        dma("Y", C("yp", S * t, S * t + S), C("Pt", S * t, S * t + S))
+                    for k0 in range(0, 16, CFG["pk"]):
+                        mm((y if k0 == 0 else []) + [(o, A("If"), C("pr", 1024 * q + k, 1024 * q + 1024, 16), last and k == 0, k == 15) for k in range(k0, k0 + CFG["pk"])])
+                        ops[-1]["chain"] = "PS"
+                if last:
+                    act(C("Pt", S * t + 64 * q, S * t + 64 * q + 64), o, ACT.Copy)
+                    dma("Y", C("yp", S * t + 64 * q, S * t + 64 * q + 64), C("Pt", S * t + 64 * q, S * t + 64 * q + 64))
         if not last:
-            mm([(C("M", 256, 256 + S), A("Iy"), C("Y", S * t, S * t + S), True, False),
-                (C("M", 256, 256 + S), A("Ip"), C("Pt", S * t, S * t + S), False, True)])
-            act(A("hh"), C("M", 256, 256 + S), ACT.Copy)
+            act(A("hh"), C("PS", 0, S), ACT.Identity, scale=-0.25)
+            tt(C("Pt", S * t, S * t + S), C("PS", 0, S), C("Y", S * t, S * t + S), ALU.add)
+            dma("Y", C("yp", S * t, S * t + S), C("Pt", S * t, S * t + S))
             an = C("At", 256 + cn, 256 + cn + S)
-            tt(an, IND(C("At", 0, 256 + cn), C("cxU", 0, 12)), A("hh"), ALU.add, arr=("aa", t - 2) if t >= 2 else None)
+            tt(an, IND(C("At", 0, 256 + cn), C("cxU", 16 * t, 16 * t + 12)), A("hh"), ALU.add, arr=("aa", t - 2) if t >= 2 else None)
+            ops[-1]["due"] = CFG["due"][1] + CFG["period"] * (RO - 2 - t)
             if t < RO - 2:
-                act(C("SA", 64 * t, 64 * t + 64), IND(C("At", 256 + cn, 256 + cn + S + 8), C("srU", 0, 4)), ACT.Copy,
+                act(C("SA", 64 * t, 64 * t + 64), IND(C("At", 256 + cn, 256 + cn + S + 8), C("srU", 4 * t, 4 * t + 4)), ACT.Copy,
                     arr=("aa", t - 1) if t > 0 else None)
                 a1 = 256 + cn + LN + S
                 add("G", 300, ("aa", t, C("At", a1, a1 + H), C("SA", 64 * t, 64 * t + 64)), [C("SA", 64 * t, 64 * t + 64)], [], kind="rem")
     return ops
 
 
-def schedule(ops, bias=None):
+def polish(ops, pre, succ, order, cost, tail, rounds):
+    n, LAT = len(ops), COST["LAT"]
+    eng, banks = [o["eng"] for o in ops], [o["banks"] for o in ops]
+    before, after = [set(j for j, l in p) for p in pre], [set(j for j, l in p) for p in succ]
+    seed = [CFG["seed"]]
+
+    def rnd():
+        seed[0] = (seed[0] * 1103515245 + 12345) % 2147483648
+        return seed[0] / 2147483648.0
+
+    def run(order):
+        t1, why, last, user, end, top = [0.0] * n, [-1] * n, {}, {}, 0.0, 0
+        for i in order:
+            e, r, w = eng[i], 0.0, -1
+            for j, l in pre[i]:
+                if t1[j] + l > r:
+                    r, w = t1[j] + l, -2 - j
+            j = last.get(e)
+            if j is not None and t1[j] >= r:
+                r, w = t1[j], j
+            for b in banks[i]:
+                u = user.setdefault(b, {})
+                for e2, j in u.items():
+                    if e2 != e and t1[j] + LAT > r:
+                        r, w = t1[j] + LAT, j
+                u[e] = i
+            last[e], why[i], t1[i] = i, w, r + cost[i]
+            if t1[i] + tail[i] > end:
+                end, top = t1[i] + tail[i], i
+        return end, why, top, t1
+
+    cur, why, top, t1 = run(order)
+    best, it = (cur, order, t1), 0
+    while it < rounds:
+        arcs, i = [], top
+        while why[i] != -1:
+            if why[i] >= 0:
+                arcs.append((why[i], i))
+            i = why[i] if why[i] >= 0 else -2 - why[i]
+        for _ in range(30):
+            it += 1
+            u, v = arcs[int(rnd() * len(arcs))]
+            pu, pv = order.index(u), order.index(v)
+            if rnd() < 0.2:
+                k = pu - 1
+                while k >= 0 and eng[order[k]] != eng[v]:
+                    k -= 1
+                if k >= 0:
+                    pu, u = k, order[k]
+            seg = order[pu:pv + 1]
+            if rnd() < 0.5:
+                need = {v}
+                for x in reversed(seg[:-1]):
+                    if after[x] & need:
+                        need.add(x)
+                if u in need:
+                    continue
+                new = [x for x in seg if x in need] + [x for x in seg if x not in need]
+            else:
+                need = {u}
+                for x in seg[1:]:
+                    if before[x] & need:
+                        need.add(x)
+                if v in need:
+                    continue
+                new = [x for x in seg if x not in need] + [x for x in seg if x in need]
+            cand = order[:pu] + new + order[pv + 1:]
+            c, w2, top2, t2 = run(cand)
+            if c <= cur + CFG["noise"] * max(0.05, 1 - it / rounds) * rnd():
+                cand.sort(key=lambda x: t2[x] - cost[x])
+                order, cur, why, top = cand, c, w2, top2
+                if c < best[0]:
+                    best = (c, cand, t2)
+                break
+    return best[0], best[1], [best[2][i] - cost[i] for i in range(n)]
+
+
+def swaps(ops, pre, succ, order, cost, tail, rounds, rnd):
+    n, LAT = len(ops), COST["LAT"]
+    eng, banks = [o["eng"] for o in ops], [o["banks"] for o in ops]
+    after = [set(j for j, l in p) for p in succ]
+
+    def heads(order):
+        t1, rj, pe, ne, bp, last, user, end = [0.0] * n, [0.0] * n, [-1] * n, [-1] * n, [()] * n, {}, {}, 0.0
+        for i in order:
+            e, r = eng[i], 0.0
+            for j, l in pre[i]:
+                if t1[j] + l > r:
+                    r = t1[j] + l
+            if banks[i]:
+                bp[i] = []
+                for b in banks[i]:
+                    u = user.setdefault(b, {})
+                    for e2, j in u.items():
+                        if e2 != e:
+                            bp[i].append(j)
+                            r = max(r, t1[j] + LAT)
+                    u[e] = i
+            rj[i] = r
+            j = last.get(e, -1)
+            pe[i] = j
+            if j >= 0:
+                ne[j] = i
+                if t1[j] > r:
+                    r = t1[j]
+            last[e] = i
+            t1[i] = r + cost[i]
+            if t1[i] + tail[i] > end:
+                end = t1[i] + tail[i]
+        return end, t1, rj, pe, ne, bp
+
+    def tails(order, ne, bp):
+        q, qj = [0.0] * n, list(tail)
+        for i in reversed(order):
+            x = qj[i]
+            for k, l in succ[i]:
+                if l + cost[k] + q[k] > x:
+                    x = l + cost[k] + q[k]
+            qj[i] = x
+            k = ne[i]
+            if k >= 0 and cost[k] + q[k] > x:
+                x = cost[k] + q[k]
+            q[i] = x
+            for j in bp[i]:
+                qj[j] = max(qj[j], LAT + cost[i] + x)
+        return q, qj
+
+    end, t1, rj, pe, ne, bp = heads(order)
+    best, barred = (end, t1), {}
+    for it in range(rounds):
+        q, qj = tails(order, ne, bp)
+        cands = []
+        for v in order:
+            if t1[v] + q[v] < end - 1e-3:
+                continue
+            u, sv = pe[v], t1[v] - cost[v]
+            if u >= 0 and abs(t1[u] - sv) < 1e-3 and v not in after[u]:
+                p, nx = pe[u], ne[v]
+                rv = max(rj[v], t1[p] if p >= 0 else 0.0)
+                ru = max(rj[u], rv + cost[v])
+                qu = max(qj[u], cost[nx] + q[nx] if nx >= 0 else 0.0)
+                cands.append((max(rv + cost[v] + max(qj[v], cost[u] + qu), ru + cost[u] + qu) + 30 * rnd(), u, v))
+            for u in bp[v]:
+                if abs(t1[u] + LAT - sv) < 1e-3 and v not in after[u]:
+                    cands.append((end + 150 * rnd() - 30, u, v))
+        pos = {x: k for k, x in enumerate(order)}
+        for est, u, v in sorted(cands):
+            if barred.get((u, v), 0) > it and est >= best[0]:
+                continue
+            seg, need, line = order[pos[u]:pos[v] + 1], {v}, set()
+            for x in reversed(seg[:-1]):
+                if after[x] & need or x in line or (eng[x] == eng[v] and eng[u] != eng[v]):
+                    need.add(x)
+                    line.add(pe[x])
+            if u in need:
+                continue
+            barred[(v, u)] = it + 12 + int(12 * rnd())
+            order = order[:pos[u]] + [x for x in seg if x in need] + [x for x in seg if x not in need] + order[pos[v] + 1:]
+            break
+        else:
+            barred.clear()
+        end, t1, rj, pe, ne, bp = heads(order)
+        order.sort(key=lambda x: t1[x] - cost[x])
+        if end < best[0]:
+            best = (end, t1)
+    return best[0], [best[1][i] - cost[i] for i in range(n)]
+
+
+def schedule(ops, rounds):
+    LAT, DMAL = COST["LAT"], COST["DMAL"]
     hist = {}
     sends = {}
+    prev = {}
     for i, o in enumerate(ops):
         deps, same = set(), set()
+        if "chain" in o:
+            if o["chain"] in prev:
+                same.add(prev[o["chain"]])
+            prev[o["chain"]] = i
         for write, items in ((False, o["r"]), (True, o["w"])):
             for name, lo, hi, n1 in items:
                 if name not in SCRATCH:
@@ -500,8 +759,8 @@ def schedule(ops, bias=None):
                     if j != i and l2 < hi and lo < h2 and (write or w2):
                         if o["eng"] == "P" and ops[j]["eng"] == "P":
                             same.add(j)
-                        elif write and w2 and name[:2] == "xr" and o["eng"] == ops[j]["eng"] and i - j < 16:
-                            same.add(j)
+                        elif write and w2 and name[:2] == "xr" and i - j < 16:
+                            pass
                         else:
                             deps.add(j)
         for write, items in ((False, o["r"]), (True, o["w"])):
@@ -513,89 +772,196 @@ def schedule(ops, bias=None):
                     hl[:] = [e for e in hl if not (lo <= e[0] and e[1] <= hi)]
                 hl.append((lo, hi, i, write))
         o["deps"] = deps
+        o["pure"] = set(deps)
         o["ord"] = same
         o["banks"] = sorted(set(x[0] for x in o["r"] + o["w"] if x[0] in SCRATCH and SCRATCH[x[0]][0] == "psum"))
         if o["kind"] == "rem":
             sends[o["fn"][:2]] = i
     n = len(ops)
-    lat = lambda j: DMAL if ops[j]["kind"] != "c" else LAT
     pre = []
     for o in ops:
-        p = [(j, lat(j)) for j in o["deps"]] + [(j, 0.0) for j in o["ord"]]
+        p = [(j, ops[j]["lat"]) for j in o["deps"]] + [(j, 0.0) for j in o["ord"]]
         if o["arr"] is not None:
-            p.append((sends[o["arr"]], DMAL + 500))
+            p.append((sends[o["arr"]], COST["RL"]))
         pre.append(p)
     succ = [[] for _ in ops]
     for i in range(n):
         for j, l in pre[i]:
             succ[j].append((i, l))
-    prio = [0.0] * n
-    for i in range(n - 1, -1, -1):
-        tail = DMAL if ops[i]["kind"] != "c" else 0.0
-        prio[i] = ops[i]["cost"] + max([tail] + [l + prio[k] for k, l in succ[i]])
-    left = [len(p) for p in pre]
-    ready = [0.0] * n
-    pool = {e: [] for e in "VSPGY"}
-    for i in range(n):
-        if left[i] == 0:
-            pool[ops[i]["eng"]].append(i)
-    free = {e: 0.0 for e in pool}
-    order = []
-    end = 0.0
+    cost = [o["cost"] for o in ops]
+    tail = [max(o["lat"] if o["kind"] != "c" else 0.0, o.get("due", 0.0)) for o in ops]
+
+    def place(rank, before, after, first):
+        left = [len(p) for p in before]
+        ready = list(first)
+        pool = {e: [] for e in "VSPGY"}
+        for i in range(n):
+            if left[i] == 0:
+                pool[ops[i]["eng"]].append(i)
+        free = {e: 0.0 for e in pool}
+        user = {}
+        t0 = [0.0] * n
+        ahead = CFG["ahead"]
+
+        def when(k):
+            r = ready[k]
+            for b in ops[k]["banks"]:
+                for e2, t in user.get(b, {}).items():
+                    if e2 != ops[k]["eng"] and t + LAT > r:
+                        r = t + LAT
+            return r
+
+        for _ in range(n):
+            best = None
+            for e, pl in pool.items():
+                if pl:
+                    w = [when(k) for k in pl]
+                    t = max(free[e], min(w))
+                    if best is None or t < best[0]:
+                        best = (t, e, w)
+            t, e, w = best
+            r, i = min(((r, k) for r, k in zip(w, pool[e]) if r <= t + ahead), key=lambda x: rank[x[1]])
+            pool[e].remove(i)
+            t = max(t, r)
+            t0[i] = t
+            free[e] = t + cost[i]
+            for b in ops[i]["banks"]:
+                user.setdefault(b, {})[e] = t + cost[i]
+            for k, l in after[i]:
+                ready[k] = max(ready[k], t + cost[i] + l)
+                left[k] -= 1
+                if left[k] == 0:
+                    pool[ops[k]["eng"]].append(k)
+        return t0
+
+    def place1(rank, before, after, first):
+        left = [len(p) for p in before]
+        ready = list(first)
+        pool = [i for i in range(n) if left[i] == 0]
+        line = {}
+        t0 = [0.0] * n
+        while pool:
+            i = min(pool, key=lambda k: rank[k])
+            pool.remove(i)
+            o, t, c = ops[i], ready[i], cost[i]
+            moved = True
+            while moved:
+                moved = False
+                for res in [o["eng"]] + o["banks"]:
+                    pad = 0.0 if res == o["eng"] else LAT
+                    for a, b, e in reversed(line.get(res, ())):
+                        if b + 3000.0 < t:
+                            break
+                        if (pad == 0.0 or e != o["eng"]) and a - pad < t + c and t < b + pad:
+                            t = b + pad
+                            moved = True
+            t0[i] = t
+            for res in [o["eng"]] + o["banks"]:
+                ln = line.setdefault(res, [])
+                k = len(ln)
+                while k > 0 and ln[k - 1][0] > t:
+                    k -= 1
+                ln.insert(k, (t, t + c, o["eng"]))
+            for k, l in after[i]:
+                ready[k] = max(ready[k], t + c + l)
+                left[k] -= 1
+                if left[k] == 0:
+                    pool.append(k)
+        return t0
+
+    def length(t0):
+        return max(t0[i] + cost[i] + tail[i] for i in range(n))
+
+    zero = [0.0] * n
+    key = []
+    guests = {"caU": S, "ag1": 3072, "ab1": 3072, "ag2": 3072, "ab2": 3072, "K0": S, "M": S, "vp": S, "abp": S, "s1": S, "sel": S, "qF": S,
+              "qR": S, "NQ": S, "liU": S, "k1U": 12, "qU": 12, "qL": 12, "i2U": 12, "sm": S, "wR": S, "D1": S}
+    for o in ops:
+        name, lo = o["w"][0][:2] if o["w"] else ("rem", 0)
+        name = name.rstrip("012") if name[:2] in ("xr", "wr", "li", "SB") else name
+        if name == "K0" and lo % 64:
+            name = "Kp"
+        if name in ("K1", "D1", "M") and lo >= 256:
+            name += str(lo // 16)
+        key.append(o["eng"] + name + ("g" if lo >= guests.get(name, 1 << 30) else ""))
+
+    def ranks(bias):
+        prio = [0.0] * n
+        nxt = {}
+        for i in range(n - 1, -1, -1):
+            kind = (key[i], ops[i]["step"])
+            due = bias.get("due" + key[i])
+            due = 0.0 if due is None or kind[1] < 0 else due + bias["period"] * (RO - 2 - kind[1])
+            prio[i] = cost[i] + bias.get(key[i], 0.0) + max([tail[i], due, nxt.get(kind, 0.0)] + [l + prio[k] for k, l in succ[i]])
+            if key[i][1:] in CFG["line"]:
+                nxt[kind] = prio[i] - bias.get(key[i], 0.0)
+        return [-p for p in prio]
+
+    def ranks(ph):
+        rank, seen = [0.0] * n, {}
+        for i in range(n):
+            kind = (key[i], ops[i]["step"])
+            if kind[1] >= 0:
+                c = seen.get(kind, 0.0)
+                seen[kind] = c + cost[i] * ph["pace"]
+                rank[i] = ph["period"] * kind[1] + 100.0 * ph.get(key[i] + str(kind[1]), ph.get(key[i], 0)) + c
+        for i in range(n - 1, -1, -1):
+            if ops[i]["step"] < 0:
+                rank[i] = min([1e9] + [rank[k] - l for k, l in succ[i]]) - cost[i] - 100.0 * ph["init"]
+        return rank
+
+    if CFG.get("hook"):
+        marks = [i for i in range(n) if key[i] in ("VtdU", "Shh")]
+
+        def value(b):
+            t0 = place(ranks(b), pre, succ, zero)
+            return length(t0) + CFG["lam"] * sum(t0[i] for i in marks)
+        CFG["hook"](value, key)
+    t0 = place(ranks(CFG["bias"]), pre, succ, zero)
+    seed = [CFG["seed"]]
+
+    def rnd():
+        seed[0] = (seed[0] * 1103515245 + 12345) % 2147483648
+        return seed[0] / 2147483648.0
+
+    best = cur = (length(t0), t0)
+    for it in range(CFG["ils"]):
+        c = cur
+        for k in range(6):
+            a = 400.0 * rnd() * (k < 4)
+            back = place1([-(c[1][i] + cost[i]) + a * rnd() for i in range(n)], succ, pre, tail)
+            f = place1([-(back[i] + cost[i]) + a * rnd() for i in range(n)], pre, succ, zero)
+            if length(f) < c[0] + 500 or k == 0:
+                c = (length(f), f)
+        c = swaps(ops, pre, succ, sorted(range(n), key=lambda i: c[1][i]), cost, tail, CFG["ts"], rnd)
+        if c[0] < cur[0] + 400:
+            cur = c
+        if c[0] < best[0]:
+            best = c
+    t0 = best[1]
+    if CFG.get("hook3"):
+        t0 = CFG["hook3"](place, place1, t0, pre, succ, zero, tail, cost, length, ops)
+    order = sorted(range(n), key=lambda i: t0[i])
+    if CFG.get("hook2"):
+        order = CFG["hook2"](ops, pre, succ, order, cost, tail)
+    end, order, t0 = polish(ops, pre, succ, order, cost, tail, rounds)
     user = {}
-    held = set()
-
-    def when(k):
-        o = ops[k]
-        r = ready[k]
+    for i in order:
+        o = ops[i]
+        o["t"] = (t0[i], t0[i] + cost[i])
         for b in o["banks"]:
-            if b in held and o["eng"] == "P" and not o.get("open", (False, False))[0]:
-                return 1e18
-            for e2, j in user.get(b, {}).items():
-                if e2 != o["eng"]:
-                    r = max(r, ops[j]["t"][1] + LAT)
-        return r
-
-    while len(order) < n:
-        best = None
-        for e, pl in pool.items():
-            if not pl:
-                continue
-            t0 = max(free[e], min(when(i) for i in pl))
-            if best is None or t0 < best[0]:
-                best = (t0, e)
-        t0, e = best
-        i = max((k for k in pool[e] if when(k) <= t0 + AHEAD), key=lambda k: prio[k] + (bias[k] if bias else 0.0))
-        pool[e].remove(i)
-        ready[i] = when(i)
-        for b in ops[i]["banks"]:
             us = user.setdefault(b, {})
-            ops[i]["deps"].update(j for e2, j in us.items() if e2 != e)
-            us[e] = i
-            if "open" in ops[i]:
-                if ops[i]["open"][1]:
-                    held.add(b)
-                else:
-                    held.discard(b)
-        t1 = max(t0, ready[i]) + ops[i]["cost"]
-        ops[i]["t"] = (t1 - ops[i]["cost"], t1)
-        free[e] = t1
-        end = max(end, t1)
-        order.append(i)
-        for k, l in succ[i]:
-            ready[k] = max(ready[k], t1 + l)
-            left[k] -= 1
-            if left[k] == 0:
-                pool[ops[k]["eng"]].append(k)
+            o["deps"].update(j for e2, j in us.items() if e2 != o["eng"])
+            us[o["eng"]] = i
     return order, end
 
 
 def plan():
     ops = build_ops()
-    order, end = schedule(ops, [BIAS.get(o["eng"] + (o["w"][0][0] if o["w"] else "rem"), 0.0) for o in ops])
+    order, end = schedule(ops, CFG["rounds"])
     cnt = {e: 0 for e in "VSPG"}
     known = {e: {} for e in "VSPGY"}
-    nd = 0
+    nd = []
     for i in order:
         o = ops[i]
         e = o["eng"]
@@ -624,8 +990,8 @@ def plan():
             cnt[e] += 1
             o["sig"] = ("e" + e, cnt[e])
         elif o["kind"] == "dma":
-            o["sig"] = ("d%d" % nd, 16)
-            nd += 1
+            o["sig"] = ("d%d" % len(nd), 16 * o["n"])
+            nd.append(16 * o["n"])
         else:
             o["sig"] = ("lx", 0)
     return ops, order, cnt, nd, end
@@ -656,12 +1022,15 @@ def rank_program(g, core, T, topo):
             mask = sum(1 << e for e in topo.engines(core, dst)[:NENG])
             g.remote_dma(ap(T, out), ap(T, src), T.sem["%s%d" % (name, t)], T.sem["lx"], pid, rid, mask)
             sent += NENG
+        elif o["kind"] == "dma":
+            for ins in o["fn"](g, T):
+                ins.then_inc(T.sem[o["sig"][0]], 16)
         else:
-            o["fn"](g, T).then_inc(T.sem[o["sig"][0]], 16 if o["kind"] == "dma" else 1)
+            o["fn"](g, T).then_inc(T.sem[o["sig"][0]], 1)
     for e in "VSPG":
         g.wait_ge(T.sem["e" + e], cnt[e])
-    for k in range(nd):
-        g.wait_ge(T.sem["d%d" % k], 16)
+    for k, v in enumerate(nd):
+        g.wait_ge(T.sem["d%d" % k], v)
     for k in range(4):
         g.wait_ge(T.sem["ax%d" % k], NENG)
         g.wait_ge(T.sem["aa%d" % k], NENG)

import math
from concourse.bass import DstId, RemoteDMATransfer
from concourse.mybir import dt, AluOpType, AxisListType, ActivationFunctionType

ALU = AluOpType
ACT = ActivationFunctionType
CN, Q0, S, H, RO, LN = 2560, 768, 192, 64, 6, 256
XW = 272
SW = 208
NOV, KB, ZC, IDW = 656, 672, 4528, 4544
OFF = 2048.0
VOID = 2097152.0
BIG = 1099511627776.0
NENG = 8
CFG = {
    "m1": ["VVVSVV", "DDDDVVSS", "DDDDDDSS", "DDDDDDSS", "DDDDDDSS", "DDDDDD"],
    "m2": ["VVVSVV", "VVVVVVSS", "VVVVVSSS", "VVVVVVSS", "VVVVVSSS", "VSVSSS"],
    "sum": ["PPP", "PPP", "PPP", "PPP", "PVP", "PVV"],
    "ny": [2, 0, 0, 0, 6, 6],
    "half": [12] * 6,
    "dram": False, "period": 19000.0, "due": [-1e6, 8000.0], "merge": "D", "lam": 0.05, "dw": 512, "pk": 4, "pw": [512] * 6, "da": 512, "flat": False, "apart": True, "caG": False, "early": True, "tiny": "VVV", "ils": 0, "ts": 400, "x0": "VVSVG",
    "line": (), "ahead": 100.0, "rounds": 0, "noise": 200.0, "seed": 1,
    "bias": {'period': 19500, 'pace': 1.2, 'init': 4, 'VcaU': -153, 'Sag1': -105, 'Vag1': -100, 'Gag1': -165, 'Sab1': -90, 'PK0': -17, 'PSB': 28, 'Gxr': -50, 'Sag1g': -35, 'VcaF': 9, 'PK118': -30, 'VpU': -36, 'Vvp': 10, 'Sabp': 44, 'PKp': 2, 'Vs1': 1, 'Vk1U': -33, 'Vsel': 65, 'PK116': 11, 'VqU': 72, 'VliU': 80, 'SqL': 86, 'PK1': 42, 'SqF': -5, 'GqR': 53, 'SNQ': 34, 'Sfar': 118, 'Vag2': 63, 'Sag2': 53, 'Sab2': 63, 'PM': 60, 'PD0': 95, 'Swc': 105, 'Ywr': 102, 'YWd': 100, 'Swr': 125, 'Gag2': 53, 'Vov': 46, 'PM24': 20, 'SxT': 46, 'Sab1g': 55, 'PK0g': 108, 'Vvpg': 16, 'Sabpg': 44, 'Vs1g': 18, 'Vk1Ug': 53, 'Vselg': 70, 'VqUg': 57, 'VliUg': 27, 'SqLg': 17, 'SqFg': 59, 'GqRg': -18, 'SNQg': 122, 'Sag2g': -60, 'Sab2g': -32, 'PMg': 55, 'SliF': 165, 'VEb': 75, 'PD1': 75, 'SwR': 105, 'PD116': 62, 'VLO': 175, 'SLO': 98, 'Vsm': 55, 'Vsx': 180, 'VFF': 62, 'SFF': -13, 'Vi2U': 77, 'SHI': 85, 'VfR': 110, 'Vcum': 117, 'Ssj': 82, 'VsrU': 135, 'SSX': 113, 'Grem': 76, 'Vd1': 18, 'Vd2': 134, 'VtdU': 112, 'VNB': 168, 'Vmn': 198, 'VDL': 265, 'Vsel2': 225, 'PK117': 217, 'Vcx': 214, 'VcxU': 227, 'SCt': 196, 'YNB': 120, 'Yqpm': 3, 'YKt': 42, 'YCt': 23, 'Vpr': 290, 'PPS': 285, 'Vso': 290, 'Shh': 263, 'VAt': 285, 'VPt': 368, 'SSA': 285, 'Yyp': 325, 'SPt': 300, 'SCt5': 176, 'Vov4': 21, 'VliU0': 92, 'Vselg0': 100, 'Vsm5': 110, 'Sag14': -65, 'PSB0': 25, 'VAt4': 270, 'PK14': 37, 'PM245': 32, 'Vd24': 84, 'SHI0': 58, 'VcaF4': -31, 'Vsel5': 105, 'Gag10': -158, 'PD14': 115, 'Ssj0': 84, 'Vs1g4': 8, 'Sfar0': 106, 'SqL4': 96, 'Vag25': 68, 'VpU5': -16, 'PK1160': 36, 'SliF4': 125, 'Sab1g0': 97, 'SqLg5': 17, 'VEb0': 80, 'GqRg5': 22, 'Sag15': -103, 'SqFg4': 69, 'Vs14': 1, 'VsrU4': 145, 'GqR0': 53, 'Gxr4': -25, 'Vsx0': 170, 'Vk1Ug4': 15, 'Vpr0': 295, 'SNQg4': 124, 'Vcum4': 107, 'VsrU5': 175, 'PD1160': 52, 'Swr4': 165, 'VfR4': 105},
}

CFG.update(apart=False, flat=False, caG=True, da=1024, ils=25, due=[-1e6, -1e6], sum=["PVP", "PVP", "VPV", "PVP", "VPV", "PVV"])
CFG["bias"] = {'period': 21500, 'pace': 0.8, 'init': 7, 'VcaU': -153, 'Sag1': -100, 'Vag1': -95, 'Gag1': -152, 'Sab1': -70, 'PK0': -17, 'PSB': 18, 'Gxr': -70, 'Sag1g': 87, 'VcaF': -31, 'PK118': -35, 'VpU': -36, 'Vvp': 10, 'Sabp': 44, 'PKp': 69, 'Vs1': 4, 'Vk1U': -13, 'Vsel': -17, 'PK116': 1, 'VqU': 72, 'VliU': 70, 'SqL': 98, 'PK1': 40, 'SqF': 17, 'GqR': 101, 'SNQ': -1, 'Sfar': 46, 'Vag2': 65, 'Sag2': 68, 'Sab2': 53, 'PM': 60, 'PD0': 79, 'Swc': 60, 'Ywr': 102, 'YWd': 100, 'Swr': 153, 'Gag2': 53, 'Vov': 66, 'PM24': 72, 'SxT': 66, 'Sab1g': 50, 'PK0g': 108, 'Vvpg': 16, 'Sabpg': 44, 'Vs1g': 28, 'Vk1Ug': 53, 'Vselg': 70, 'VqUg': 25, 'VliUg': 27, 'SqLg': 27, 'SqFg': 59, 'GqRg': -33, 'SNQg': 113, 'Sag2g': -60, 'Sab2g': -32, 'PMg': 50, 'SliF': 167, 'VEb': 49, 'PD1': 134, 'SwR': 147, 'PD116': 32, 'VLO': 175, 'SLO': 98, 'Vsm': 55, 'Vsx': 175, 'VFF': 62, 'SFF': -13, 'Vi2U': 87, 'SHI': 85, 'VfR': 154, 'Vcum': 97, 'Ssj': 72, 'VsrU': 93, 'SSX': 113, 'Grem': 76, 'Vd1': 10, 'Vd2': 136, 'VtdU': 142, 'VNB': 166, 'Vmn': 323, 'VDL': 323, 'Vsel2': 237, 'PK117': 269, 'Vcx': 234, 'VcxU': 187, 'SCt': 208, 'YNB': 138, 'Yqpm': 43, 'YKt': 82, 'YCt': 23, 'Vpr': 290, 'PPS': 280, 'Vso': 290, 'Shh': 258, 'VAt': 315, 'VPt': 410, 'SSA': 305, 'Yyp': 325, 'SPt': 300, 'GcaU': -180, 'VcaUg': -30, 'VHI': 75, 'SliF0': 175, 'Vsx0': 160, 'Vag20': 23, 'VfR0': 115, 'Vsm0': 65, 'Sab10': -85, 'GqR4': 43, 'Vvp4': 20, 'PK05': 13, 'VEb0': 105, 'Sfar0': 96, 'VcxU0': 147, 'Vpr4': 268, 'SSX0': 133, 'Vcx0': 239, 'Vs10': -3, 'Sag20': 58, 'SNQg4': 103, 'Vag24': 85, 'SqL0': 48, 'Sag15': -140, 'VDL0': 327, 'PSB4': 8, 'PK1165': -4}
CFG.update(ny=[6] * 6, m1=["VVVSVV"] + ["DDDDVVSS"] * 4 + ["DDDDDD"], m2=["VVVSVV"] + ["VVVVVVSS"] * 4 + ["VSVSSS"], sum=["PPP", "PPP", "PPP", "PPP", "PVP", "PVV"])
CFG["bias"].update({'PD0': 195, 'Vpr': 215, 'Vso': 220, 'period': 19900, 'pace': 1.0, 'init': 10, 'Sag1': -95, 'Gag1': -192, 'Sab1': -30, 'PK0': -14, 'PSB': 16, 'Gxr': -30, 'Sag1g': 52, 'PK118': 15, 'Vvp': -30, 'Sabp': -11, 'PKp': 29, 'Vs1': 9, 'Vk1U': -33, 'VliU': 60, 'SqL': 95, 'PK1': 15, 'GqR': 106, 'SNQ': -36, 'Vag2': 55, 'Sag2': 21, 'Sab2': 91, 'PM': 80, 'Swr': 195, 'Vov': 76, 'PM24': 112, 'SxT': 16, 'PK0g': 98, 'Vk1Ug': 13, 'VqUg': 30, 'SqLg': 67, 'SqFg': 64, 'GqRg': -73, 'SNQg': 123, 'Sag2g': -62, 'Sab2g': -17, 'VEb': 69, 'SwR': 117, 'PD116': -48, 'Vsx': 170, 'Vcum': 147, 'Ssj': 47, 'SSX': 133, 'Grem': 96, 'Vd1': -20, 'VNB': 88, 'PK117': 274, 'Vcx': 274, 'VcxU': 177, 'SCt': 228, 'Yqpm': -17, 'YKt': 115, 'PPS': 360, 'Shh': 261, 'VAt': 352, 'SSA': 365, 'GcaU': -207, 'VcaUg': -15, 'VHI': 63, 'Vs10': -1, 'PSB0': -22, 'VFF0': 55, 'YCt0': 43, 'VqUg4': 5, 'PKp5': 29, 'Vsm4': 53, 'SliF4': 177, 'Sag25': 63, 'Gxr4': -32, 'SSA0': 325, 'Yyp0': 323, 'PPS0': 370, 'Vk1U0': -38, 'Vmn0': 313, 'Sab15': -50})
CFG.update(apart=True, m1=["VVVSVV"] + ["SSDDVVSS"] * 4 + ["DDDDSS"], ils=30, seed=5)
CFG["bias"].update({'period': 19500, 'pace': 1.2, 'init': 14, 'Sag1': -89, 'Gag1': -187, 'PK0': -19, 'PSB': 31, 'Gxr': 58, 'Sag1g': 62, 'VcaF': -26, 'PK118': 17, 'VpU': -56, 'Vvp': -50, 'Sabp': 12, 'PKp': 84, 'Vs1': -11, 'Vk1U': -31, 'Vsel': 20, 'PK116': -41, 'VliU': 70, 'SqL': 115, 'PK1': 55, 'GqR': 156, 'SNQ': -41, 'Sfar': 75, 'Sag2': 26, 'Sab2': 63, 'PM': 55, 'Swr': 197, 'SxT': -4, 'Sab1g': 70, 'PK0g': 96, 'Vk1Ug': 53, 'Vselg': 50, 'VqUg': 32, 'VliUg': 37, 'SqLg': 55, 'SqFg': 71, 'GqRg': -68, 'SNQg': 113, 'Sab2g': 23, 'PMg': 45, 'SliF': 139, 'VEb': 52, 'SwR': 75, 'PD116': -21, 'VLO': 172, 'Vsm': 18, 'Vsx': 118, 'Vi2U': 62, 'VfR': 57, 'Vcum': 172, 'Ssj': 88, 'VsrU': 10, 'SSX': 82, 'Grem': 120, 'Vd1': 0, 'Vd2': 96, 'VtdU': 90, 'VNB': 86, 'Vmn': 280, 'VDL': 345, 'Vsel2': 294, 'VcxU': 119, 'SCt': 208, 'YNB': 116, 'YKt': 75, 'Vpr': 223, 'PPS': 310, 'Shh': 214, 'VAt': 350, 'VPt': 313, 'SSA': 375, 'Yyp': 303, 'GcaU': -187, 'VcaUg': -53, 'VHI': 98, 'SliF0': 185, 'Vpr4': 258, 'Sag20': 63, 'SNQg4': 63, 'Vag24': 95, 'Sag15': -130, 'SSA0': 365, 'Sab15': -60, 'VEg': 90, 'PD1g': 85, 'SwRg': 90, 'Vsmg': 90, 'Vi2Ug': 92, 'SSX4': 100, 'Vsel0': -20, 'VcaF4': -51, 'SqFg4': 71, 'Vi2U0': 32, 'Vpr0': 173, 'Vcx4': 284, 'Swr4': 152, 'Grem4': 90, 'Sab24': 86, 'Sab1g4': 65, 'Vmn4': 275, 'VqU5': 70, 'Gxr0': 38, 'Yqpm0': -37, 'PD1164': -48, 'VqU0': 67, 'YNB0': 126, 'VFF4': 82})
CFG.update(m1=["VVVSVV"] + ["SSSSVVSS"] * 4 + ["SSSVSS"], sum=["PVP", "PVP", "PVP", "PVP", "PVP", "PVV"], seed=2)
CFG["bias"].update({'period': 19900, 'init': 12, 'Sag1': -29, 'Vag1': -85, 'Sab1': -25, 'PK0': 61, 'PSB': 26, 'Gxr': 78, 'VcaF': -31, 'PK118': 52, 'VpU': -51, 'VqU': 52, 'VliU': 48, 'SqL': 113, 'PK1': 15, 'SqF': 55, 'SNQ': -49, 'Sfar': 165, 'Vag2': 53, 'Sag2': 46, 'Sab2': 65, 'PM': 53, 'PD0': 115, 'Swr': 207, 'Vov': 86, 'PM24': 72, 'Sab1g': 85, 'Vs1g': 48, 'VliUg': 57, 'GqRg': -60, 'SNQg': 133, 'Sag2g': -22, 'Sab2g': 13, 'PMg': 55, 'SliF': 134, 'SwR': 45, 'Vsm': 13, 'Vsx': 103, 'VFF': 22, 'Vi2U': 107, 'Vcum': 270, 'Grem': 127, 'Vd2': 148, 'VtdU': 70, 'VNB': 81, 'VDL': 305, 'Vsel2': 254, 'SCt': 193, 'YNB': 114, 'YKt': 85, 'Shh': 176, 'VPt': 328, 'SSA': 475, 'Yyp': 261, 'VcaUg': -29, 'VHI': 138, 'PKp5': 31, 'Sab15': -50, 'VEg': 46, 'Swr4': 157, 'Sab24': 106, 'Vmn4': 285, 'VFF4': 102, 'Sabp0': 2, 'VtdU4': 80, 'Yqpm4': -27, 'Vd20': 108, 'Vso5': 215, 'Vs15': -16, 'Vso4': 218, 'VcaUg4': 11, 'PM4': 33})

SCRATCH = {
    "Kt": ("sbuf", [128, 2048], "bfloat16"), "Ct": ("sbuf", [128, 4096], "bfloat16"), "At": ("sbuf", [128, 4096], "float32"),
    "NB": ("sbuf", [128, 2048], "float32"), "DL": ("sbuf", [128, 2048], "float32"),
    "nbi": ("sbuf", [128, 768], "int32"), "dli": ("sbuf", [128, 768], "int32"), "sti": ("sbuf", [128, 16], "int32"),
    "X": ("sbuf", [128, RO * XW], "bfloat16"), "XS": ("sbuf", [128, 4 * SW], "bfloat16"),
    "Y": ("sbuf", [128, RO * S], "bfloat16"), "Pt": ("sbuf", [128, RO * S], "float32"),
    "Id": ("sbuf", [128, IDW], "bfloat16"), "NV": ("sbuf", [128, KB], "bfloat16"),
    "Z": ("sbuf", [128, 144], "bfloat16"), "Zw": ("sbuf", [128, 144], "bfloat16"),
    "If": ("sbuf", [128, 128], "float32"), "NE": ("sbuf", [128, 1024], "bfloat16"), "xT": ("sbuf", [128, 4 * 128], "bfloat16"),
    "xr0": ("sbuf", [128, 3072], "bfloat16"), "xr1": ("sbuf", [128, 3072], "bfloat16"),
    "ab1": ("sbuf", [128, 64, 64], "bfloat16"), "ab2": ("sbuf", [128, 64, 64], "bfloat16"),
    "ag1": ("sbuf", [128, 4096], "bfloat16"), "ag2": ("sbuf", [128, 4096], "bfloat16"), "xr2": ("sbuf", [128, 3072], "bfloat16"),
    "caS": ("sbuf", [128, 256], "float32"), "vp": ("sbuf", [128, 256], "bfloat16"), "abp": ("sbuf", [128, 256], "bfloat16"),
    "wr0": ("sbuf", [128, 3072], "float32"), "wr1": ("sbuf", [128, 3072], "float32"), "wc": ("sbuf", [128, 192], "float32"),
    "Wd": ("dram", [8, 3072], "float32"),
    "pr": ("sbuf", [128, 3072], "float32"), "so": ("sbuf", [128, 1024], "float32"),
    "Eb": ("sbuf", [128, 16, 256], "bfloat16"), "Eg": ("sbuf", [128, 16, 64], "bfloat16"),
    "caU": ("sbuf", [128, 256], "uint16"), "caF": ("sbuf", [128, 256], "float16"), "sel": ("sbuf", [128, 256], "float16"),
    "liU0": ("sbuf", [128, 256], "uint16"), "liU1": ("sbuf", [128, 256], "uint16"), "liU2": ("sbuf", [128, 256], "uint16"),
    "liF": ("sbuf", [128, 256], "float32"), "sel2": ("sbuf", [128, 256], "float16"), "NQ": ("sbuf", [128, 256], "float32"),
    "mn": ("sbuf", [128, 256], "float32"), "qR": ("sbuf", [128, 256], "float16"), "qF": ("sbuf", [128, 256], "float32"),
    "qpm": ("sbuf", [128, 256], "float32"), "nR": ("sbuf", [128, 1280], "float32"),
    "wR": ("sbuf", [128, 256], "bfloat16"),
    "fR": ("sbuf", [128, 192], "bfloat16"), "cum": ("sbuf", [128, 192], "bfloat16"), "sj": ("sbuf", [128, 768], "bfloat16"),
    "one": ("sbuf", [128, 192], "bfloat16"), "hh": ("sbuf", [128, 192], "float32"),
    "s1": ("sbuf", [128, 256], "float32"), "sm": ("sbuf", [128, 256], "float32"), "sx": ("sbuf", [128, 256], "float32"),
    "dmin": ("sbuf", [128, 256], "bfloat16"), "dmax": ("sbuf", [128, 256], "bfloat16"), "rs": ("sbuf", [128, 1024], "bfloat16"),
    "thr": ("sbuf", [128, 256], "bfloat16"), "seed": ("sbuf", [128, 256], "bfloat16"), "half": ("sbuf", [128, 256], "bfloat16"),
    "w2": ("sbuf", [128, 256], "bfloat16"),
    "ii": ("sbuf", [128, 16], "int32"), "ij": ("sbuf", [128, 16], "int32"),
    "pw": ("sbuf", [128, 4], "float32"), "pm": ("sbuf", [128, 4], "float32"), "LL": ("sbuf", [128, 80], "float32"),
    "QM": ("sbuf", [128, 80], "float16"), "HI": ("sbuf", [128, 5, 48], "float32"), "ov": ("sbuf", [128, 4], "float16"),
    "jb": ("sbuf", [128, 4], "float32"), "acc": ("sbuf", [128, 4], "float32"),
    "SX": ("sbuf", [128, 4 * 72], "bfloat16"), "SA": ("sbuf", [128, 4 * 64], "float32"),
    "K0": ("psum", [128, 512], "float32"), "K1": ("psum", [128, 512], "float32"), "M": ("psum", [128, 512], "float32"),
    "SB0": ("psum", [128, 512], "float32"), "SB1": ("psum", [128, 512], "float32"), "D0": ("psum", [128, 512], "float32"),
    "D1": ("psum", [128, 512], "float32"), "PS": ("psum", [128, 512], "float32"),
}
for _n in ("B1", "B16", "Bv", "I1", "NI", "IX"):
    SCRATCH[_n] = ("sbuf", [128, 128], "bfloat16")
for _t in range(1, RO):
    SCRATCH["Zr%d" % _t] = ("sbuf", [128, 144], "bfloat16")
SCRATCH["cxU"] = ("sbuf", [128, 80], "uint16")
for _n in ("k1U", "qU", "i2U", "srU", "pU"):
    SCRATCH[_n] = ("sbuf", [128, 16], "uint16")
SCRATCH["far"] = SCRATCH["AB"] = ("sbuf", [128, 32], "float32")
for _n in ("qL", "nf", "cx", "LC", "I16", "tm"):
    SCRATCH[_n] = ("sbuf", [128, 16], "float32")
for _n in ("FF", "LO", "d1", "d2"):
    SCRATCH[_n] = ("sbuf", [128, 48], "float32")
SCRATCH["tdU"] = ("sbuf", [128, 48], "uint16")
NDMA = 80
SEMAPHORES = ["eV", "eS", "eP", "eG"] + ["d%d" % i for i in range(NDMA)] + ["ax%d" % i for i in range(4)] + ["aa%d" % i for i in range(4)] + ["lx"]

BYTES = {"float32": 4, "int32": 4, "bfloat16": 2, "float16": 2, "uint16": 2}
COST = {"CG": 1.5, "CSC": 3.8, "CYC": 0.83, "PEC": 0.46, "LAT": 130.0, "OV": 0.0, "RL": 3500.0, "DMAL": 2300.0, "ZL": 10000.0, "GD": 900.0, "AL": 5000.0}


def sl(a, b, s=None):
    return slice(a, b, s)


def A(name, *idx, p=None):
    return ("ap", name, p, idx)


def C(name, a, b, s=None):
    return A(name, sl(a, b, s))


def IND(win, off):
    return ("ind", win, off)


def span(x):
    name, idx = x[1], x[3]
    if name not in SCRATCH:
        return name, 0, 1 << 30, 0
    where, shape, _ = SCRATCH[name]
    lo, hi, n, stride = 0, 0, 1, 1
    dims = shape[1:]
    for d in range(len(dims) - 1, -1, -1):
        i = idx[d] if d < len(idx) else slice(None)
        r = range(dims[d])[i] if isinstance(i, slice) else range(i, i + 1)
        lo += r[0] * stride
        hi += r[-1] * stride
        n *= len(r)
        stride *= dims[d]
    return name, lo, hi + 1, n


def ap(T, x):
    if not isinstance(x, tuple):
        return x
    if x[0] == "ind":
        return ap(T, x[1]).indirect(ap(T, x[2]))
    ps = x[2] if x[2] is not None else slice(None)
    if not x[3]:
        return T[x[1]][ps]
    return T[x[1]][(ps,) + tuple(x[3])]


def parts(x):
    if not isinstance(x, tuple):
        return []
    return [x[1], x[2]] if x[0] == "ind" else [x]


def wide(x):
    return BYTES[SCRATCH[x[1]][2]]


def build_ops():
    ops = []
    step = [-1]
    CG, CSC, CYC, PEC, DMAL = (COST[k] for k in ("CG", "CSC", "CYC", "PEC", "DMAL"))

    def add(eng, cost, fn, reads, writes, kind="c", arr=None, lat=None, n=1):
        rd = [y for x in reads for y in parts(x)]
        wr = []
        for x in writes:
            if x[0] == "ind":
                wr.append(x[1])
                rd.append(x[2])
            else:
                wr.append(x)
        if lat is None:
            lat = COST["LAT"] if kind == "c" else DMAL
        if eng in "VS" and kind == "c":
            cost += COST["OV"]
        ops.append({"eng": eng, "cost": cost, "fn": fn, "r": [span(x) for x in rd], "w": [span(x) for x in wr], "kind": kind,
                    "arr": arr, "lat": lat, "n": n, "step": step[0]})

    def vcost(out, ins, f=None):
        if out[0] == "ind":
            return 50 + span(ins[0])[3] * CSC * CYC
        n = span(out)[3]
        if ins and ins[0][0] == "ind":
            return 50 + n * CG * CYC
        if f is None:
            f = 0.5 if all(wide(x) == 2 for x in [out] + ins) else 1.0
        return 30 + max(64, n * f) * CYC

    def cp(out, a):
        add("V", vcost(out, [a]), lambda g, T: g.vector.tensor_copy(ap(T, out), ap(T, a)), [a], [out])

    def ms(out, v):
        add("V", vcost(out, []), lambda g, T: g.vector.memset(ap(T, out), v), [], [out])

    def ts(out, a, s1, op0, s2=None, op1=None):
        if op1 is None:
            fn = lambda g, T: g.vector.tensor_scalar(ap(T, out), ap(T, a), ap(T, s1), None, op0)
        else:
            fn = lambda g, T: g.vector.tensor_scalar(ap(T, out), ap(T, a), ap(T, s1), ap(T, s2), op0, op1)
        add("V", vcost(out, [a]), fn, [a, s1, s2], [out])

    def tt(out, a, b, op, arr=None):
        f = 2.0 if a[0] == "ind" or (SCRATCH[a[1]][0] == "sbuf" and SCRATCH[b[1]][0] == "sbuf") else 1.0
        add("V", vcost(out, [a, b], f), lambda g, T: g.vector.tensor_tensor(ap(T, out), ap(T, a), ap(T, b), op), [a, b], [out], arr=arr)

    def scan(out, d0, d1, init, op0, op1):
        add("V", vcost(out, [d0, d1]), lambda g, T: g.vector.tensor_tensor_scan(ap(T, out), ap(T, d0), ap(T, d1), init, op0, op1), [d0, d1], [out])

    def red(out, a):
        add("V", 90, lambda g, T: g.vector.tensor_reduce(ap(T, out), ap(T, a), AxisListType.X, ALU.add), [a], [out])

    def act(out, a, func, bias=None, scale=None, acc=None, arr=None, more=0.0):
        n = span(out)[3]
        cost = 65 + n * CG * CYC if a[0] == "ind" else 30 + max(64, n) * CYC + (20 if acc else 0)

        def fn(g, T):
            kw = {}
            if bias is not None:
                kw["bias"] = ap(T, bias)
            if scale is not None:
                kw["scale"] = ap(T, scale)
            if acc is not None:
                kw["accum_out"] = ap(T, acc)
            return g.scalar.activation(ap(T, out), ap(T, a), func, **kw)
        add("S", cost + more, fn, [a, bias, scale], [out] + ([acc] if acc else []), arr=arr)

    def mm(items, arr=None):
        cost = sum(max(64, span(o)[3]) * (4 if wide(r) == 4 else 1) for o, l, r, s0, s1 in items) * PEC + 60

        def fn(g, T):
            ins = None
            for o, l, r, s0, s1 in items:
                ins = g.tensor.matmul(ap(T, o), ap(T, l), ap(T, r), s0, s1)
            return ins
        add("P", cost, fn, [x for it in items for x in it[1:3]], [it[0] for it in items], arr=arr)

    def dmas(eng, pairs, cost=60.0, arr=None, lat=None):
        def fn(g, T):
            qe = g if eng == "G" else g.scalar if eng == "S" else g.sync
            return [qe.dma_start(ap(T, o), ap(T, a)) for o, a in pairs]
        add(eng, cost * len(pairs), fn, [a for o, a in pairs], [o for o, a in pairs], kind="dma", arr=arr, lat=lat, n=len(pairs))

    def dma(eng, out, a, cost=60.0, arr=None):
        dmas(eng, [(out, a)], cost, arr)

    def iota(out, pat, base, cm):
        n = span(out)[3]
        if SCRATCH[out[1]][2] == "int32":
            fn = lambda g, T: g.iota(ap(T, out), pat, base, cm)
        else:
            fn = lambda g, T: g.iota(ap(T, out), pat, base, cm, allow_small_or_imprecise_dtypes=True)
        add("G", 130 + 2 * n * CYC, fn, [], [out])

    def asel(out, a, pat, op, fill, base, cm):
        add("G", 170 + 2 * span(out)[3] * CYC, lambda g, T: g.affine_select(ap(T, out), ap(T, a), pat, op, fill, base, cm), [a], [out])

    def gcp(out, a):
        asel(out, a, [[0, span(out)[3]]], ALU.is_equal, 0.0, 0, 0)

    def fill(out, v):
        iota(out, [[0, span(out)[3]]], v, 0)

    def selr(r, z="Z"):
        return C(z, 15 - r, 143 - r)

    def tolist(out, src, c0, c1, z="Z", more=()):
        it = [(out, selr(r, z), C(src, 16 * c0 + r, 16 * c1, 16), r == 0, r == 15) for r in range(16)]
        mm(it[:1] + list(more) + it[1:])

    def rows(name, j0, j1):
        return A(name, sl(j0 // 64, j1 // 64), sl(0, 64))

    dma("Y", A("sti"), A("st"))
    dma("Y", A("nbi"), A("nb"))
    dma("S", C("X", 0, S), C("xs", 0, S))
    dma("S", C("Kt", 0, Q0), A("kq"))
    dma("Y", A("dli"), A("dl"))
    dma("Y", C("Ct", 256, 256 + CN), A("cc"))
    dma("G", C("At", 256, 256 + CN), A("aa"), 300.0)
    for t in range(RO):
        if t > 0:
            dma("Y", C("X", XW * t, XW * t + S), C("xs", S * t, S * t + S))
        if t < RO - 2:
            dma("Y", C("XS", SW * t, SW * t + S), C("xs", S * t, S * t + S))
            fill(C("XS", SW * t + S, SW * t + SW), int(VOID))
    dma("Y", A("Y"), A("ys"))
    iota(A("ii"), [[-1, 16]], 16, 1)
    ts(A("ij"), A("ii"), 15, ALU.bitwise_and)
    ts(A("I16"), A("ij"), 0.0, ALU.is_equal)
    ts(C("pm", 0, 1), C("ij", 0, 1), 1.0, ALU.mult)
    ts(C("Id", KB, KB + 16), A("I16"), 6144.0, ALU.mult, -OFF, ALU.add)
    w = 16
    while w < 512:
        cp(C("Id", KB + w, KB + 2 * w), C("Id", KB, KB + w))
        w *= 2
    pieces = [(KB + a, min(512, ZC - KB - a)) for a in range(512, ZC - KB, 512)] + [(0, 512), (512, NOV - 512)]
    dmas("Y", [(C("Id", a, a + n), C("Id", KB, KB + n)) for a, n in pieces])
    ms(C("Id", NOV, KB), -OFF)
    ts(C("Id", ZC, IDW), A("I16"), OFF, ALU.mult, -OFF, ALU.add)
    iota(A("NV"), [[3, KB]], 1 - 3 * NOV, 0)
    ms(A("B1"), 1.0)
    asel(A("B1"), A("B1"), [[-16, 8], [0, 16]], ALU.is_ge, 0.0, 0, 1)
    asel(A("B1"), A("B1"), [[16, 8], [0, 16]], ALU.is_ge, 0.0, 15, -1)
    ms(A("Z"), 0.0)
    ts(C("Z", 15, 143, 16), C("B1", 0, 128, 16), 16.0, ALU.mult)
    act(A("Zw"), A("Z"), ACT.Identity, scale=-8.0)
    ms(A("I1"), 1.0)
    asel(A("I1"), A("I1"), [[-1, 128]], ALU.is_equal, 0.0, 0, 1)
    fill(A("NE", p=sl(0, 64)), -1)
    asel(A("NE", p=sl(0, 64)), A("NE", p=sl(0, 64)), [[-1, 64], [0, 16]], ALU.is_equal, 0.0, 0, 1)
    for name, src, f in (("B16", "B1", 65536.0), ("Bv", "B1", 1.0 / 256), ("NI", "I1", -1.0), ("IX", "I1", 16.0), ("If", "I1", 1.0)):
        act(A(name), A(src), ACT.Identity, scale=f)
    ms(A("dmin"), -1.0)
    ms(C("dmin", 0, 256, 16), BIG)
    act(A("dmax"), A("dmin"), ACT.Identity, scale=-1.0)
    if "V" in "".join(CFG["sum"]):
        act(C("rs", 0, 256), A("dmin"), ACT.Relu, scale=-1.0)
        dmas("Y", [(C("rs", a, a + 256), C("rs", 0, 256)) for a in (256, 512, 768)])
    iota(A("w2"), [[0, 16], [-1, 16]], 15, 0)
    act(A("thr"), A("w2"), ACT.Exp, bias=math.log(2.5), scale=math.log(2.0), more=1300.0)
    act(C("half", 0, 1), C("pm", 0, 1), ACT.Exp, bias=15 * math.log(2.0), scale=-math.log(2.0))
    act(C("pw", 0, 1), C("half", 0, 1), ACT.Copy)
    iota(A("HI", sl(0, 5), sl(32, 48)), [[256, 5], [16, 16]], Q0, 0)
    for a in (0, 16):
        act(A("HI", sl(0, 5), sl(a, a + 16)), A("HI", sl(0, 5), sl(32, 48)), ACT.Identity, bias=C("pm", 0, 1))
    ts(A("QM"), A("HI", sl(0, 5), sl(0, 16)), -OFF, ALU.add)
    act(A("LC"), A("HI", 0, sl(0, 16)), ACT.Identity, bias=-16.0 * (Q0 + 16 * OFF), scale=16.0)
    act(A("jb"), A("HI", 0, sl(0, 4)), ACT.Identity, bias=0.5 - Q0)
    for t in range(RO - 1):
        iota(C("nR", LN * t, LN * t + LN), [[1, LN]], Q0 + LN * t, 0)
    fill(A("qpm"), 0)
    fill(A("one"), 1)
    dma("Y", C("At", 0, 256), A("qpm"))
    dmas("Y", [(C("At", 256 + CN + S, 256 + CN + LN), C("qpm", 0, H)), (C("qF", S, LN), C("qpm", 0, H)), (C("DL", Q0 + S, Q0 + LN), C("qpm", 0, H)),
               (A("FF"), C("qpm", 0, 48)), (A("LO"), C("qpm", 0, 48)), (A("far"), C("qpm", 0, 32))])
    fill(C("X", S, XW), 0)
    dmas("Y", [(C("Ct", 256 + CN + S, 256 + CN + LN), C("X", S, LN))] + [(C("SX", 72 * t + 64, 72 * t + 72), C("X", S, S + 8)) for t in range(4)])
    for t in range(1, RO):
        act(A("Zr%d" % t), A("Z"), ACT.Identity, scale=C("I16", 7 + t, 8 + t))
    cp(A("qU"), A("sti"))
    cp(C("qL", 12, 16), C("sti", 12, 16))
    cp(C("NB", 0, Q0), A("nbi"))
    ts(C("DL", 0, Q0), A("dli"), 256.0 - OFF, ALU.add)

    def xrep(t):
        nv = 6
        xr = "xr%d" % (t % 3)
        for k in range(16):
            o, a = C(xr, k, 512 * nv, 16), C("X", XW * t, XW * t + 32 * nv)
            if t == 0 and CFG["x0"][k % len(CFG["x0"])] == "V":
                cp(o, a)
            elif t == 0 and CFG["x0"][k % len(CFG["x0"])] == "S":
                act(o, a, ACT.Copy)
            else:
                gcp(o, a)

    flip = [0]

    def quarter(stage, t, q, win, lst, key):
        abn = "ab%d" % stage
        xr = "xr%d" % (t % 3)
        ag = "ag%d" % stage
        md = CFG["m%d" % stage][t][2 * q:2 * q + 2]
        for b0, b1 in ([(0, 2)] if md[0] == md[1] and md[0] in CFG["merge"] else [(0, 1), (1, 2)]):
            off = C(lst, 64 * q + 32 * b0, 64 * q + 32 * b1)
            j0, j1 = 1024 * q + 512 * b0, 1024 * q + 512 * b1
            if md[b0] == "V":
                tt(C(ag, j0, j1), IND(win, off), C(xr, j0, j1), ALU.subtract)
                act(rows(abn, j0, j1), C(ag, j0, j1), ACT.Abs)
            elif md[b0] == "D":
                w = CFG["dw"]
                for j in range(j0, j1, w):
                    act(C(ag, j, j + w), IND(win, C(lst, j // 16, (j + w) // 16)), ACT.Identity, scale=-1.0)
                o, a = C(ag, j0, j1), C(xr, j0, j1)
                add("G", COST["GD"], lambda g, T, o=o, a=a: [g.dma_start(ap(T, o), ap(T, a), accum_op=ALU.add)], [a, o], [o], kind="dma", lat=COST["AL"])
                for j in range(j0, j1, CFG["da"]):
                    act(rows(abn, j, j + CFG["da"]), C(ag, j, j + CFG["da"]), ACT.Abs)
            else:
                act(C(ag, j0, j1), IND(win, off), ACT.Copy)
                for b in range(b0, b1):
                    bank = A("SB%d" % flip[0])
                    flip[0] ^= 1
                    j = 1024 * q + 512 * b
                    if q == 3 or md[b] == "T":
                        sub = (bank, A("xT", sl(128 * q, 128 * q + 128), p=sl(0, 64)), A("NE", sl(512 * b, 512 * b + 512), p=sl(0, 64)), False, True)
                    else:
                        sub = (bank, A("NI"), C(xr, j, j + 512), False, True)
                    mm([(bank, A("I1"), C(ag, j, j + 512), True, False), sub])
                    act(rows(abn, j, j + 512), bank, ACT.Abs)
        if stage == 1 or t < RO - 1:
            mm([(key, selr(r), A(abn, sl(16 * q + r // 4, 16 * q + 16, 4), sl(16 * (r % 4), 16 * (r % 4) + 16)), r == 0, r == 15) for r in range(16)])

    xrep(0)
    exp_seen = [True]
    for t in range(RO):
        step[0] = t
        nc = 16 if 0 < t < RO - 1 else 12
        n, nq = 16 * nc, nc // 4
        qn, cn = Q0 + LN * t, CN + LN * t
        x0 = XW * t
        liU = "liU%d" % (t % 3)
        last = t == RO - 1
        hc = CFG["half"][t]
        halves = [(0, hc), (hc, nc)] if hc < nc else [(0, nc)]
        gin = ("ax", t - 1) if t > 0 else None
        L = lambda name, a=0: C(name, a, a + nc)
        for q in range(nq):
            if q == 3 or "T" in CFG["m1"][t][2 * q:2 * q + 2] + CFG["m2"][t][2 * q:2 * q + 2]:
                o = A("M", sl(256 + 128 * (q % 2), 384 + 128 * (q % 2)), p=sl(0, 64))
                mm([(o, C("X", x0 + 64 * q, x0 + 64 * q + 64), A("I1"), True, True)], arr=gin if q == 3 else None)
                act(A("xT", sl(128 * q, 128 * q + 128), p=sl(0, 64)), o, ACT.Copy)
        if t == 0:
            cp(C("caU", 0, n), IND(A("nbi"), C("qU", 0, nc)))
            cp(C("caF", 0, n), IND(A("nbi"), C("qU", 0, nc)))
        elif not CFG["early"]:
            for c0, c1 in halves:
                cp(C("caU", 16 * c0, 16 * c1), IND(C("NB", 0, qn - LN), C("qU", c0, c1)))
            act(C("caS", 0, n), IND(C("NB", 0, qn - LN), C("qU", 0, nc)), ACT.Copy)
        else:
            (gcp if CFG["caG"] else cp)(C("caU", 0, S), C("NQ", 0, S))
            cp(C("caF", 0, n), IND(C("NB", 0, qn - LN), C("qU", 0, nc)))
            if nc == 16:
                cp(C("caU", S, n), IND(C("NB", 0, qn - LN), C("qU", 12, 16)))
            tolist(C("K1", 288, 300), "caF", 0, 12, "Zr%d" % t)
            ts(C("pU", 0, 12), C("K1", 288, 300), 0.0625, ALU.mult)
        if nc == 16:
            tt(A("ov"), C("qL", 12, 16), C("X", x0 + 256, x0 + 260), ALU.mult, arr=gin)
        if t + 1 < RO:
            xrep(t + 1)
        for q in range(nq):
            quarter(1, t, q, C("Kt", 0, max(Q0, qn - LN) if CFG["early"] and q < 3 else qn), "caU", C("K0", 64 * q, 64 * q + 64))
        for h, (c0, c1) in enumerate(halves):
            a0, a1 = 16 * c0, 16 * c1
            if t > 0 and CFG["early"] and c0 < 12:
                c2 = min(c1, 12)
                tt(C("vp", a0, 16 * c2), IND(C("Kt", 0, qn), C("pU", c0, c2)), C("X", x0 + a0, x0 + 16 * c2), ALU.subtract)
                act(C("abp", a0, 16 * c2), C("vp", a0, 16 * c2), ACT.Abs)
                tolist(C("K0", a0 + 7 + t, 16 * c2, 16), "abp", c0, c2)
            scan(C("s1", a0, a1), C("dmin", a0, a1), C("K0", a0, a1), 0.0, ALU.add, ALU.min)
            ts(C("k1U", c0, c1), C("s1", a0 + 15, a1, 16), 15.0 + KB, ALU.add, float(ZC), ALU.min)
            tt(C("sel", a0, a1), IND(A("Id"), C("k1U", c0, c1)), C("caF" if t == 0 or CFG["early"] else "caS", a0, a1), ALU.min)
            ql = C("K1", 256 + c0, 256 + c1)
            tolist(ql, "sel", c0, c1, more=[(C("K1", 268, 272), A("IX"), A("ov"), False, False)] if c1 == 16 else [])
            ts(C("qU", c0, c1), ql, 0.0625, ALU.mult, 15 * OFF, ALU.add)
            ts(C(liU, a0, a1), IND(C("DL", 0, qn), C("qU", c0, c1)), OFF - 256.0, ALU.add)
            if not last:
                act(C("qL", c0, c1), ql, ACT.Identity, bias=15 * OFF, scale=0.0625)
                mm([(C("K1", a0, a1), A("B1"), C("sel", a0, a1), True, True)])
                act(C("qF", a0, a1), C("K1", a0, a1), ACT.Identity, bias=15 * OFF)
                gcp(C("qR", a0, a1), C("qF", a0, a1))
        for q in range(nq):
            quarter(2, t, q, C("Ct", 256, 256 + cn), liU, C("M", 64 * q, 64 * q + 64))
        if not last:
            dma("Y", C("Kt", qn, qn + LN), C("X", x0, x0 + LN), arr=gin)
            dma("Y", C("Ct", 0, LN), C("X", x0, x0 + LN), arr=gin)
            act(C("liF", 0, n), IND(C("DL", 0, qn), C("qU", 0, nc)), ACT.Copy)
            for c0, c1 in ((0, 12), (12, 16)) if nc == 16 and hc < nc and CFG["early"] else ((0, 16),):
                act(C("NQ", 16 * c0, 16 * c1), IND(C("NB", 0, qn), C("qU", c0, c1)), ACT.Copy)
            if t > 0:
                dma("Y", A("qpm", sl(0, LN), p=sl(7 + t, 128, 16)), A("At", sl(0, LN), p=sl(7 + t, 128, 16)))
            dma("Y", A("qpm", sl(0, LN), p=sl(8 + t, 128, 16)), A("nR", sl(LN * t, LN * t + LN), p=sl(8 + t, 128, 16)))
            cuts = [(0, 12), (12, 16)] if CFG["apart"] and 0 < t < RO - 2 else [(0, nc)]
            for c0, c1 in cuts:
                a0, a1 = 16 * c0, 16 * c1
                eb = "Eg" if c0 else "Eb"
                part = lambda c, a: A(eb, c, sl(a - max(a0, 16 * c), a1 - max(a0, 16 * c)))
                for c in range(c1):
                    a = max(a0, 16 * c)
                    ts(part(c, a), C("qR", a, a1), C("qL", c, c + 1), ALU.is_equal, C("pw", 0, 1), ALU.mult)
                O = C("D1", a0, a1)
                mm([(O, A("NI"), C("thr", a0, a1), True, False)] +
                   ([(C("D1", S, LN), A("Bv"), C("X", x0 + S, x0 + LN), False, False)] if c1 == 16 else []) +
                   [(O, A("B1"), A(eb, sl(c0, c1), sl(0, 16)), False, False)] +
                   [(C("D1", max(a0, 16 * c + 16), a1), A("B16"), part(c, max(a0, 16 * c + 16)), False, c == c1 - 2) for c in range(c1 - 1)],
                   arr=gin if c1 == 16 else None)
                act(C("wR", a0, a1), O, ACT.Sign, scale=-1.0)
            W = C("D1", 256, 256 + nc)
            tolist(W, "wR", 0, nc, "Zw", more=[(W, A("I1"), C("QM", 16 * t, 16 * t + nc), False, False)])
            tt(L("LO"), W, L("qL"), ALU.max)
            act(L("far"), C("s1", 15, n, 16), ACT.Identity, bias=-8965000.0, scale=1.0e4)
            if CFG["flat"]:
                act(L("far", 16), C("s1", 15, n, 16), ACT.Identity, bias=8965000.0, scale=-1.0e4)
                tt(A("AB"), A("far"), A("HI", t, sl(0, 32)), ALU.min)
                tt(L("nf"), L("AB", 16), L("qL"), ALU.max)
                dma("Y", A("HI", t, sl(0, 16)), C("AB", 0, 16))
                tt(L("LO", 16), W, L("nf"), ALU.max)
            elif CFG["tiny"][0] == "S":
                act(L("LO", 16), L("LO"), ACT.Copy)
            else:
                tt(L("LO", 16), W, L("qL"), ALU.max)
            for c0, c1 in cuts:
                scan(C("sm", 16 * c0, 16 * c1), C("dmin", 16 * c0, 16 * c1), C("M", 16 * c0, 16 * c1), 0.0, ALU.add, ALU.min)
                ts(C("i2U", c0, c1), C("sm", 16 * c0 + 15, 16 * c1, 16), 15.0, ALU.add, float(NOV), ALU.min)
            scan(C("sx", 0, n), C("dmax", 0, n), C("M", 0, n), 0.0, ALU.add, ALU.max)
            kmin, kmax = C("sm", 15, n, 16), C("sx", 15, n, 16)
            ts(L("FF", 32), kmin, -640.5, ALU.add, 1.0e4, ALU.mult)
            if CFG["flat"]:
                act(L("FF"), kmin, ACT.Identity, bias=-6405000.0, scale=1.0e4) if CFG["tiny"][1] == "S" else ts(L("FF"), kmin, -640.5, ALU.add, 1.0e4, ALU.mult)
                ts(L("FF", 16), kmin, -640.5, ALU.add, -1.0e4, ALU.mult)
            else:
                tt(L("FF"), L("FF", 32), L("far"), ALU.min)
                if CFG["tiny"][1] == "S":
                    act(L("FF", 16), L("FF"), ACT.Identity, scale=-1.0)
                else:
                    ts(L("FF", 16), L("FF"), -1.0, ALU.mult)
            ts(L("LO", 32), kmin, 15.0, ALU.add, float(NOV), ALU.min)
            if CFG["tiny"][2] == "S":
                act(A("HI", t, sl(32, 32 + nc)), kmax, ACT.Identity, bias=ZC - 1.0, scale=-1.0)
            else:
                ts(A("HI", t, sl(32, 32 + nc)), kmax, -1.0, ALU.mult, ZC - 1.0, ALU.add)
            tt(A("d1"), A("FF"), A("HI", t, sl(0, 48)), ALU.min)
            tt(A("d2"), A("d1"), A("LO"), ALU.max)
            cp(A("tdU"), A("d2"))
            ops[-1]["due"] = CFG["due"][0] + CFG["period"] * (RO - 2 - t)
            tt(IND(C("NB", 0, qn + LN), L("tdU", 16)), C("NQ", 0, n), C("qpm", 0, n), ALU.max)
            if t < RO - 2:
                dma("Y", C("NB", qn, qn + LN), A("NQ"))
                dma("Y", A("NB", sl(qn, qn + LN), p=sl(t, 128, 16)), A("qF", sl(0, LN), p=sl(t, 128, 16)))
            tt(C("mn", 0, n), IND(A("Id"), L("tdU", 32)), C("nR", LN * t, LN * t + n), ALU.min)
            tt(IND(C("DL", 0, qn + LN), L("tdU")), C("liF", 0, n), C("mn", 0, n), ALU.max)
            tt(C("sel2", 0, n), IND(A("Id"), L("i2U")), C("liF", 0, n), ALU.min)
            tolist(C("K1", 272, 272 + nc), "sel2", 0, nc)
            tt(L("cx"), C("K1", 272, 272 + nc), L("LC"), ALU.max)
            ts(L("cxU", 16 * t), L("cx"), 0.0625, ALU.mult, 16 * OFF, ALU.add)
            act(C("Ct", 256 + cn, 256 + cn + n), IND(C("Ct", 0, 256 + cn), L("cxU", 16 * t)), ACT.Copy)
            if t < RO - 2:
                tt(A("fR"), IND(A("NV"), C("i2U", 0, 12)), C("wR", 0, S), ALU.is_equal)
                scan(A("cum"), A("one"), A("fR"), 0.0, ALU.mult, ALU.add)
                for c in range(4):
                    act(C("sj", S * c, S * c + S), A("cum"), ACT.Sign, bias=C("jb", c, c + 1), scale=-1.0, acc=C("acc", c, c + 1))
                ts(C("srU", 4 * t, 4 * t + 4), A("acc"), 0.5, ALU.mult, 96.0, ALU.add)
                act(C("SX", 72 * t + 64, 72 * t + 68), A("acc"), ACT.Relu, bias=-191.0)
                act(C("SX", 72 * t, 72 * t + 64), IND(C("XS", SW * t, SW * t + SW), C("srU", 4 * t, 4 * t + 4)), ACT.Copy)
                add("G", 300, ("ax", t, C("X", x0 + XW + S, x0 + XW + S + 72), C("SX", 72 * t, 72 * t + 72)), [C("SX", 72 * t, 72 * t + 72)], [], kind="rem")
        wr = "wr%d" % (t % 2)
        ny = CFG["ny"][t]
        if ny < 6:
            w = S - 32 * ny
            mm([(C("D0", 0, w), selr(r), rows("ab2", 512 * ny + w * r, 512 * ny + w * r + w), r == 0, r == 15) for r in range(16)])
            act(C("wc", 0, w), C("D0", 0, w), ACT.Exp, scale=-1.0 / 1024, more=0.0 if exp_seen[0] else 1300.0)
            exp_seen[0] = True
            src = C("wc", 0, w)
            if CFG["dram"]:
                src = C("Wd", 0, 16 * w)
                dma("Y", src, C("wc", 0, w))
            dmas("Y", [(A(wr, sl(512 * ny, 3072), p=sl(f, 128, 16)), src) for f in range(16)], lat=COST["ZL"] * w / S)
        for b in range(6):
            if b < ny:
                bank = A("D%d" % (b % 2))
                mm([(bank, A("B1"), rows("ab2", 512 * b, 512 * b + 512), True, True)])
                act(C(wr, 512 * b, 512 * b + 512), bank, ACT.Exp, scale=-0.015625, more=0.0 if exp_seen[0] else 1300.0)
                exp_seen[0] = True
            for j in range(512 * b, 512 * b + 512, 512) if CFG["pw"][t] == 512 else [512 * b - 512] * (b % 2):
                j1 = j + CFG["pw"][t]
                tt(C("pr", j, j1), IND(C("At", 256, 256 + cn), C(liU, j // 16, j1 // 16)), C(wr, j, j1), ALU.mult, arr=("aa", t - 2) if t >= 2 else None)
            if b % 2 == 1:
                q = b // 2
                o = C("PS", 64 * q, 64 + 64 * q)
                y = [] if last else [(o, A("NI"), C("Y", S * t + 64 * q, S * t + 64 * q + 64), True, False)]
                if CFG["sum"][t][q] == "V":
                    scan(A("so"), A("rs"), C("pr", 1024 * q, 1024 * q + 1024), 0.0, ALU.mult, ALU.add)
                    mm(y + [(o, A("If"), C("so", 15, 1024, 16), last, True)])
                    ops[-1]["chain"] = "PS"
                else:
                    for k0 in range(0, 16, CFG["pk"]):
                        mm((y if k0 == 0 else []) + [(o, A("If"), C("pr", 1024 * q + k, 1024 * q + 1024, 16), last and k == 0, k == 15) for k in range(k0, k0 + CFG["pk"])])
                        ops[-1]["chain"] = "PS"
                if last:
                    act(C("Pt", S * t + 64 * q, S * t + 64 * q + 64), o, ACT.Copy)
                    dma("Y", C("yp", S * t + 64 * q, S * t + 64 * q + 64), C("Pt", S * t + 64 * q, S * t + 64 * q + 64))
        if not last:
            act(A("hh"), C("PS", 0, S), ACT.Identity, scale=-0.25)
            tt(C("Pt", S * t, S * t + S), C("PS", 0, S), C("Y", S * t, S * t + S), ALU.add)
            dma("Y", C("yp", S * t, S * t + S), C("Pt", S * t, S * t + S))
            an = C("At", 256 + cn, 256 + cn + S)
            tt(an, IND(C("At", 0, 256 + cn), C("cxU", 16 * t, 16 * t + 12)), A("hh"), ALU.add, arr=("aa", t - 2) if t >= 2 else None)
            ops[-1]["due"] = CFG["due"][1] + CFG["period"] * (RO - 2 - t)
            if t < RO - 2:
                act(C("SA", 64 * t, 64 * t + 64), IND(C("At", 256 + cn, 256 + cn + S + 8), C("srU", 4 * t, 4 * t + 4)), ACT.Copy,
                    arr=("aa", t - 1) if t > 0 else None)
                a1 = 256 + cn + LN + S
                add("G", 300, ("aa", t, C("At", a1, a1 + H), C("SA", 64 * t, 64 * t + 64)), [C("SA", 64 * t, 64 * t + 64)], [], kind="rem")
    return ops


def polish(ops, pre, succ, order, cost, tail, rounds):
    n, LAT = len(ops), COST["LAT"]
    eng, banks = [o["eng"] for o in ops], [o["banks"] for o in ops]
    before, after = [set(j for j, l in p) for p in pre], [set(j for j, l in p) for p in succ]
    seed = [CFG["seed"]]

    def rnd():
        seed[0] = (seed[0] * 1103515245 + 12345) % 2147483648
        return seed[0] / 2147483648.0

    def run(order):
        t1, why, last, user, end, top = [0.0] * n, [-1] * n, {}, {}, 0.0, 0
        for i in order:
            e, r, w = eng[i], 0.0, -1
            for j, l in pre[i]:
                if t1[j] + l > r:
                    r, w = t1[j] + l, -2 - j
            j = last.get(e)
            if j is not None and t1[j] >= r:
                r, w = t1[j], j
            for b in banks[i]:
                u = user.setdefault(b, {})
                for e2, j in u.items():
                    if e2 != e and t1[j] + LAT > r:
                        r, w = t1[j] + LAT, j
                u[e] = i
            last[e], why[i], t1[i] = i, w, r + cost[i]
            if t1[i] + tail[i] > end:
                end, top = t1[i] + tail[i], i
        return end, why, top, t1

    cur, why, top, t1 = run(order)
    best, it = (cur, order, t1), 0
    while it < rounds:
        arcs, i = [], top
        while why[i] != -1:
            if why[i] >= 0:
                arcs.append((why[i], i))
            i = why[i] if why[i] >= 0 else -2 - why[i]
        for _ in range(30):
            it += 1
            u, v = arcs[int(rnd() * len(arcs))]
            pu, pv = order.index(u), order.index(v)
            if rnd() < 0.2:
                k = pu - 1
                while k >= 0 and eng[order[k]] != eng[v]:
                    k -= 1
                if k >= 0:
                    pu, u = k, order[k]
            seg = order[pu:pv + 1]
            if rnd() < 0.5:
                need = {v}
                for x in reversed(seg[:-1]):
                    if after[x] & need:
                        need.add(x)
                if u in need:
                    continue
                new = [x for x in seg if x in need] + [x for x in seg if x not in need]
            else:
                need = {u}
                for x in seg[1:]:
                    if before[x] & need:
                        need.add(x)
                if v in need:
                    continue
                new = [x for x in seg if x not in need] + [x for x in seg if x in need]
            cand = order[:pu] + new + order[pv + 1:]
            c, w2, top2, t2 = run(cand)
            if c <= cur + CFG["noise"] * max(0.05, 1 - it / rounds) * rnd():
                cand.sort(key=lambda x: t2[x] - cost[x])
                order, cur, why, top = cand, c, w2, top2
                if c < best[0]:
                    best = (c, cand, t2)
                break
    return best[0], best[1], [best[2][i] - cost[i] for i in range(n)]


def swaps(ops, pre, succ, order, cost, tail, rounds, rnd):
    n, LAT = len(ops), COST["LAT"]
    eng, banks = [o["eng"] for o in ops], [o["banks"] for o in ops]
    after = [set(j for j, l in p) for p in succ]

    def heads(order):
        t1, rj, pe, ne, bp, last, user, end = [0.0] * n, [0.0] * n, [-1] * n, [-1] * n, [()] * n, {}, {}, 0.0
        for i in order:
            e, r = eng[i], 0.0
            for j, l in pre[i]:
                if t1[j] + l > r:
                    r = t1[j] + l
            if banks[i]:
                bp[i] = []
                for b in banks[i]:
                    u = user.setdefault(b, {})
                    for e2, j in u.items():
                        if e2 != e:
                            bp[i].append(j)
                            r = max(r, t1[j] + LAT)
                    u[e] = i
            rj[i] = r
            j = last.get(e, -1)
            pe[i] = j
            if j >= 0:
                ne[j] = i
                if t1[j] > r:
                    r = t1[j]
            last[e] = i
            t1[i] = r + cost[i]
            if t1[i] + tail[i] > end:
                end = t1[i] + tail[i]
        return end, t1, rj, pe, ne, bp

    def tails(order, ne, bp):
        q, qj = [0.0] * n, list(tail)
        for i in reversed(order):
            x = qj[i]
            for k, l in succ[i]:
                if l + cost[k] + q[k] > x:
                    x = l + cost[k] + q[k]
            qj[i] = x
            k = ne[i]
            if k >= 0 and cost[k] + q[k] > x:
                x = cost[k] + q[k]
            q[i] = x
            for j in bp[i]:
                qj[j] = max(qj[j], LAT + cost[i] + x)
        return q, qj

    end, t1, rj, pe, ne, bp = heads(order)
    best, barred = (end, t1), {}
    for it in range(rounds):
        q, qj = tails(order, ne, bp)
        cands = []
        for v in order:
            if t1[v] + q[v] < end - 1e-3:
                continue
            u, sv = pe[v], t1[v] - cost[v]
            if u >= 0 and abs(t1[u] - sv) < 1e-3 and v not in after[u]:
                p, nx = pe[u], ne[v]
                rv = max(rj[v], t1[p] if p >= 0 else 0.0)
                ru = max(rj[u], rv + cost[v])
                qu = max(qj[u], cost[nx] + q[nx] if nx >= 0 else 0.0)
                cands.append((max(rv + cost[v] + max(qj[v], cost[u] + qu), ru + cost[u] + qu) + 30 * rnd(), u, v))
            for u in bp[v]:
                if abs(t1[u] + LAT - sv) < 1e-3 and v not in after[u]:
                    cands.append((end + 150 * rnd() - 30, u, v))
        pos = {x: k for k, x in enumerate(order)}
        for est, u, v in sorted(cands):
            if barred.get((u, v), 0) > it and est >= best[0]:
                continue
            seg, need, line = order[pos[u]:pos[v] + 1], {v}, set()
            for x in reversed(seg[:-1]):
                if after[x] & need or x in line or (eng[x] == eng[v] and eng[u] != eng[v]):
                    need.add(x)
                    line.add(pe[x])
            if u in need:
                continue
            barred[(v, u)] = it + 12 + int(12 * rnd())
            order = order[:pos[u]] + [x for x in seg if x in need] + [x for x in seg if x not in need] + order[pos[v] + 1:]
            break
        else:
            barred.clear()
        end, t1, rj, pe, ne, bp = heads(order)
        order.sort(key=lambda x: t1[x] - cost[x])
        if end < best[0]:
            best = (end, t1)
    return best[0], [best[1][i] - cost[i] for i in range(n)]


def schedule(ops, rounds):
    LAT, DMAL = COST["LAT"], COST["DMAL"]
    hist = {}
    sends = {}
    prev = {}
    for i, o in enumerate(ops):
        deps, same = set(), set()
        if "chain" in o:
            if o["chain"] in prev:
                same.add(prev[o["chain"]])
            prev[o["chain"]] = i
        for write, items in ((False, o["r"]), (True, o["w"])):
            for name, lo, hi, n1 in items:
                if name not in SCRATCH:
                    continue
                for (l2, h2, j, w2) in hist.get(name, []):
                    if j != i and l2 < hi and lo < h2 and (write or w2):
                        if o["eng"] == "P" and ops[j]["eng"] == "P":
                            same.add(j)
                        elif write and w2 and name[:2] == "xr" and i - j < 16:
                            pass
                        else:
                            deps.add(j)
        for write, items in ((False, o["r"]), (True, o["w"])):
            for name, lo, hi, n1 in items:
                if name not in SCRATCH:
                    continue
                hl = hist.setdefault(name, [])
                if write and name[:2] != "xr":
                    hl[:] = [e for e in hl if not (lo <= e[0] and e[1] <= hi)]
                hl.append((lo, hi, i, write))
        o["deps"] = deps
        o["pure"] = set(deps)
        o["ord"] = same
        o["banks"] = sorted(set(x[0] for x in o["r"] + o["w"] if x[0] in SCRATCH and SCRATCH[x[0]][0] == "psum"))
        if o["kind"] == "rem":
            sends[o["fn"][:2]] = i
    n = len(ops)
    pre = []
    for o in ops:
        p = [(j, ops[j]["lat"]) for j in o["deps"]] + [(j, 0.0) for j in o["ord"]]
        if o["arr"] is not None:
            p.append((sends[o["arr"]], COST["RL"]))
        pre.append(p)
    succ = [[] for _ in ops]
    for i in range(n):
        for j, l in pre[i]:
            succ[j].append((i, l))
    cost = [o["cost"] for o in ops]
    tail = [max(o["lat"] if o["kind"] != "c" else 0.0, o.get("due", 0.0)) for o in ops]

    def place(rank, before, after, first):
        left = [len(p) for p in before]
        ready = list(first)
        pool = {e: [] for e in "VSPGY"}
        for i in range(n):
            if left[i] == 0:
                pool[ops[i]["eng"]].append(i)
        free = {e: 0.0 for e in pool}
        user = {}
        t0 = [0.0] * n
        ahead = CFG["ahead"]

        def when(k):
            r = ready[k]
            for b in ops[k]["banks"]:
                for e2, t in user.get(b, {}).items():
                    if e2 != ops[k]["eng"] and t + LAT > r:
                        r = t + LAT
            return r

        for _ in range(n):
            best = None
            for e, pl in pool.items():
                if pl:
                    w = [when(k) for k in pl]
                    t = max(free[e], min(w))
                    if best is None or t < best[0]:
                        best = (t, e, w)
            t, e, w = best
            r, i = min(((r, k) for r, k in zip(w, pool[e]) if r <= t + ahead), key=lambda x: rank[x[1]])
            pool[e].remove(i)
            t = max(t, r)
            t0[i] = t
            free[e] = t + cost[i]
            for b in ops[i]["banks"]:
                user.setdefault(b, {})[e] = t + cost[i]
            for k, l in after[i]:
                ready[k] = max(ready[k], t + cost[i] + l)
                left[k] -= 1
                if left[k] == 0:
                    pool[ops[k]["eng"]].append(k)
        return t0

    def place1(rank, before, after, first):
        left = [len(p) for p in before]
        ready = list(first)
        pool = [i for i in range(n) if left[i] == 0]
        line = {}
        t0 = [0.0] * n
        while pool:
            i = min(pool, key=lambda k: rank[k])
            pool.remove(i)
            o, t, c = ops[i], ready[i], cost[i]
            moved = True
            while moved:
                moved = False
                for res in [o["eng"]] + o["banks"]:
                    pad = 0.0 if res == o["eng"] else LAT
                    for a, b, e in reversed(line.get(res, ())):
                        if b + 3000.0 < t:
                            break
                        if (pad == 0.0 or e != o["eng"]) and a - pad < t + c and t < b + pad:
                            t = b + pad
                            moved = True
            t0[i] = t
            for res in [o["eng"]] + o["banks"]:
                ln = line.setdefault(res, [])
                k = len(ln)
                while k > 0 and ln[k - 1][0] > t:
                    k -= 1
                ln.insert(k, (t, t + c, o["eng"]))
            for k, l in after[i]:
                ready[k] = max(ready[k], t + c + l)
                left[k] -= 1
                if left[k] == 0:
                    pool.append(k)
        return t0

    def length(t0):
        return max(t0[i] + cost[i] + tail[i] for i in range(n))

    zero = [0.0] * n
    key = []
    guests = {"caU": S, "ag1": 3072, "ab1": 3072, "ag2": 3072, "ab2": 3072, "K0": S, "M": S, "vp": S, "abp": S, "s1": S, "sel": S, "qF": S,
              "qR": S, "NQ": S, "liU": S, "k1U": 12, "qU": 12, "qL": 12, "i2U": 12, "sm": S, "wR": S, "D1": S}
    for o in ops:
        name, lo = o["w"][0][:2] if o["w"] else ("rem", 0)
        name = name.rstrip("012") if name[:2] in ("xr", "wr", "li", "SB") else name
        if name == "K0" and lo % 64:
            name = "Kp"
        if name in ("K1", "D1", "M") and lo >= 256:
            name += str(lo // 16)
        key.append(o["eng"] + name + ("g" if lo >= guests.get(name, 1 << 30) else ""))

    def ranks(bias):
        prio = [0.0] * n
        nxt = {}
        for i in range(n - 1, -1, -1):
            kind = (key[i], ops[i]["step"])
            due = bias.get("due" + key[i])
            due = 0.0 if due is None or kind[1] < 0 else due + bias["period"] * (RO - 2 - kind[1])
            prio[i] = cost[i] + bias.get(key[i], 0.0) + max([tail[i], due, nxt.get(kind, 0.0)] + [l + prio[k] for k, l in succ[i]])
            if key[i][1:] in CFG["line"]:
                nxt[kind] = prio[i] - bias.get(key[i], 0.0)
        return [-p for p in prio]

    def ranks(ph):
        rank, seen = [0.0] * n, {}
        for i in range(n):
            kind = (key[i], ops[i]["step"])
            if kind[1] >= 0:
                c = seen.get(kind, 0.0)
                seen[kind] = c + cost[i] * ph["pace"]
                rank[i] = ph["period"] * kind[1] + 100.0 * ph.get(key[i] + str(kind[1]), ph.get(key[i], 0)) + c
        for i in range(n - 1, -1, -1):
            if ops[i]["step"] < 0:
                rank[i] = min([1e9] + [rank[k] - l for k, l in succ[i]]) - cost[i] - 100.0 * ph["init"]
        return rank

    if CFG.get("hook"):
        marks = [i for i in range(n) if key[i] in ("VtdU", "Shh")]

        def value(b):
            t0 = place(ranks(b), pre, succ, zero)
            return length(t0) + CFG["lam"] * sum(t0[i] for i in marks)
        CFG["hook"](value, key)
    t0 = place(ranks(CFG["bias"]), pre, succ, zero)
    seed = [CFG["seed"]]

    def rnd():
        seed[0] = (seed[0] * 1103515245 + 12345) % 2147483648
        return seed[0] / 2147483648.0

    best = cur = (length(t0), t0)
    for it in range(CFG["ils"]):
        c = cur
        for k in range(6):
            a = 400.0 * rnd() * (k < 4)
            back = place1([-(c[1][i] + cost[i]) + a * rnd() for i in range(n)], succ, pre, tail)
            f = place1([-(back[i] + cost[i]) + a * rnd() for i in range(n)], pre, succ, zero)
            if length(f) < c[0] + 500 or k == 0:
                c = (length(f), f)
        c = swaps(ops, pre, succ, sorted(range(n), key=lambda i: c[1][i]), cost, tail, CFG["ts"], rnd)
        if c[0] < cur[0] + 400:
            cur = c
        if c[0] < best[0]:
            best = c
    t0 = best[1]
    if CFG.get("hook3"):
        t0 = CFG["hook3"](place, place1, t0, pre, succ, zero, tail, cost, length, ops)
    order = sorted(range(n), key=lambda i: t0[i])
    if CFG.get("hook2"):
        order = CFG["hook2"](ops, pre, succ, order, cost, tail)
    end, order, t0 = polish(ops, pre, succ, order, cost, tail, rounds)
    user = {}
    for i in order:
        o = ops[i]
        o["t"] = (t0[i], t0[i] + cost[i])
        for b in o["banks"]:
            us = user.setdefault(b, {})
            o["deps"].update(j for e2, j in us.items() if e2 != o["eng"])
            us[o["eng"]] = i
    return order, end


def plan():
    ops = build_ops()
    order, end = schedule(ops, CFG["rounds"])
    cnt = {e: 0 for e in "VSPG"}
    known = {e: {} for e in "VSPGY"}
    nd = []
    for i in order:
        o = ops[i]
        e = o["eng"]
        need = {}
        for j in o["deps"]:
            s, v = ops[j]["sig"]
            if known[e].get(s, 0) < v and need.get(s, (0, 0))[0] < v:
                need[s] = (v, j)
        if o["arr"] is not None:
            s = "%s%d" % o["arr"]
            if known[e].get(s, 0) < NENG:
                need[s] = (NENG, None)
        waits = []
        for s, (v, j) in sorted(need.items(), key=lambda kv: -1 if kv[1][1] is None else -ops[kv[1][1]]["t"][1]):
            if known[e].get(s, 0) >= v:
                continue
            waits.append((s, v))
            known[e][s] = v
            if j is not None:
                for s2, v2 in ops[j]["clock"].items():
                    if known[e].get(s2, 0) < v2:
                        known[e][s2] = v2
        o["waits"] = waits
        o["clock"] = dict(known[e])
        if o["kind"] == "c":
            cnt[e] += 1
            o["sig"] = ("e" + e, cnt[e])
        elif o["kind"] == "dma":
            o["sig"] = ("d%d" % len(nd), 16 * o["n"])
            nd.append(16 * o["n"])
        else:
            o["sig"] = ("lx", 0)
    return ops, order, cnt, nd, end


PLAN = []


def rank_program(g, core, T, topo):
    rank = T.rank_of(core)
    if rank is None:
        return
    if not PLAN:
        PLAN.append(plan())
    ops, order, cnt, nd, end = PLAN[0]
    queue = {"V": g.vector, "S": g.scalar, "P": g.tensor, "G": g, "Y": g.sync}
    nranks = len(T.cores)
    sent = 0
    for i in order:
        o = ops[i]
        qe = queue[o["eng"]]
        for s, v in o["waits"]:
            qe.wait_ge(T.sem[s], v)
        if o["kind"] == "rem":
            name, t, out, src = o["fn"]
            dst = T.cores[(rank + 1 + t % (nranks - 1)) % nranks]
            rid, pid, _ = topo.addr(dst)
            mask = sum(1 << e for e in topo.engines(core, dst)[:NENG])
            g.remote_dma(ap(T, out), ap(T, src), T.sem["%s%d" % (name, t)], T.sem["lx"], pid, rid, mask)
            sent += NENG
        elif o["kind"] == "dma":
            for ins in o["fn"](g, T):
                ins.then_inc(T.sem[o["sig"][0]], 16)
        else:
            o["fn"](g, T).then_inc(T.sem[o["sig"][0]], 1)
    for e in "VSPG":
        g.wait_ge(T.sem["e" + e], cnt[e])
    for k, v in enumerate(nd):
        g.wait_ge(T.sem["d%d" % k], v)
    for k in range(4):
        g.wait_ge(T.sem["ax%d" % k], NENG)
        g.wait_ge(T.sem["aa%d" % k], NENG)
    g.wait_ge(T.sem["lx"], sent)
